import numpy as np, ml_dtypes
CORES = [2,3,42,43,82,83,122,123]
N = 8
BF = ml_dtypes.bfloat16
S, J, RO = 256, 2, 2
SH, HALF, QLO, QHI = 12, 2048, 1024, 3072
B0, B1, B2, W = 4, 4, 4, 4096
def pack(pos, pf, rf, th, lv):
    turn = lambda a: np.ascontiguousarray(a.transpose(0, 1, 3, 2)).astype(np.float32).astype(BF)
    return {"pos": turn(pos).reshape(N, 24, S), "pf": turn(pf).reshape(N, 128, S), "rf": turn(rf).reshape(N, 128, W),
            "th": np.ascontiguousarray(th.reshape(N, 128, 1)).astype(np.int32), "lv": np.ascontiguousarray(lv.reshape(N, 8, S)).astype(np.int32)}
def parts(rng):
    pos = rng.integers(-31, 32, (N, 8, S, 3)); pf = rng.integers(0, 16, (N, 8, S, 16)); rf = rng.integers(-15, 16, (N, 8, W, 16)); th = rng.integers(0, 301, (N, 8, 16))
    share = rng.choice(np.array([0.8, 0.9, 1.0]), (N, 8, 1))
    return pos, pf, rf, th, (rng.random((N, 8, S)) < share).astype(np.int64)
def setup_inputs(rng):
    pos, pf, rf, th, lv = parts(rng); g = int(rng.integers(0, 8))
    lv[:, g] = rng.random((N, S)) < 0.07
    return pack(pos, pf, rf, th, lv)
def setup_inputs_spread(rng):
    pos, pf, rf, th, lv = parts(rng)
    pos = np.rint(rng.choice(np.array([2, 6, 13, 22, 31, 31, 31, 31]), (N, 8, S, 1)) * (2 * rng.random(pos.shape) - 1)).astype(np.int64)
    pf = np.minimum(np.floor(16 * rng.random(pf.shape) ** rng.choice(np.array([0.25, 1.0, 4.0]), (N, 8, S, 1))), 15).astype(np.int64)
    c = rng.choice(np.array([0, 1, 4, 15]), (N, 8, W, 1)); rf = np.clip(rf, -c, c)
    th = np.clip(np.where(rng.random(th.shape) < 0.5, -1, 1) * np.exp2(12 * rng.random(th.shape)).astype(np.int64), -3600, 3600)
    return pack(pos, pf, rf, th, lv)
def setup_inputs_ends(rng):
    pos = 31 * (2 * rng.integers(0, 2, (N, 8, S, 3)) - 1)
    loose = rng.random((N, 8, S, 1)) < 0.25; loose[:, 7] = False
    pos = np.where(loose, rng.integers(-31, 32, pos.shape), pos)
    u = rng.random((N, 8, S, 1)); pf = np.where(u < 0.45, 15, np.where(u < 0.6, 0, 15 * rng.integers(0, 2, (N, 8, S, 16))))
    u = rng.random((N, 8, W, 1)); c = rng.choice(np.array([0.15, 0.25, 0.35]), (N, 8, 1, 1))
    rf = np.where(u < c, 15, np.where(u > 0.75, -15, 30 * rng.integers(0, 2, (N, 8, W, 16)) - 15))
    lv = (rng.random((N, 8, S)) < 0.85).astype(np.int64); lv[:, 7] = 1; lv[:, :, S - 1] = 1
    th = np.full((N, 8, 16), 3600, np.int64); e = int(rng.integers(0, 7))
    th[:, e] = np.where(rng.random((N, 16)) < 0.5, -3600, 3600); th[:, 7, 15] = -3600; th[:, 7, int(rng.integers(0, 7)) * 2] = -3600
    for a in range(N):
        for g in range(8):
            on = np.flatnonzero(lv[a, g])[45:48]; pos[a, g, on] = 31 * np.array([[1, 1, -1], [1, -1, 1], [-1, 1, 1]])
    pos[:, :, S - 1] = 1; pf[:, :, S - 1] = 15; rf[:, :, W - 1] = 15
    return pack(pos, pf, rf, th, lv)
def setup_inputs_corners(rng):
    pos, pf, rf, th, lv = parts(rng)
    n_ = np.array([0, 1, 2, 3, 4, 5, 46, 47, 48, 49, S - 1, S])[rng.permutation(12)]
    for a in range(N):
        for g in range(8):
            n = int(n_[(8 * a + g) % 12]); w = int(rng.integers(0, 3))
            on = np.arange(n) if w == 0 else (np.arange(S - n, S) if w == 1 else rng.permutation(S)[:n])
            lv[a, g] = 0; lv[a, g, on] = 1
    u = rng.random((N, 8, S, 1)); pf = np.where(u < 0.2, 0, np.where(u > 0.9, 15, pf))
    th = rng.choice(np.array([0, 0, 1, 1, 100, 200, 300, 3600]), (N, 8, 16)); e = rng.permutation(8)[:2]
    th[:, e] = rng.choice(np.array([-3600, -1, 0, 300, 3600]), (N, 2, 16))
    return pack(pos, pf, rf, th, lv)
def setup_inputs_crowd(rng):
    pos, pf, rf, th, lv = parts(rng); lv[:] = 1; gp = rng.permutation(8); m = np.arange(16)
    rf[:, :, 0, :8] = 15; rf[:, :, 0, 8:] = -15
    one = int(rng.integers(0, N)); ms = int(rng.integers(1, 16))
    for i in range(8):
        g = int(gp[i]); m0 = int(rng.integers(1, 16) if i == 0 else rng.integers(0, 16 if i < 4 else 17))
        if i == 4: m0 = (ms + 1 + int(rng.integers(0, 15))) % 16
        for a in range(N):
            if i == 0: n = 0
            elif i == 1: n = a % 4
            elif i < 4: n = 2 + (a >> 1) % 2 if a % 2 == i - 2 else S // 2
            elif i == 4: n = 1 if a == one else 0
            else: n = int(rng.choice(np.array([1, 3, 47, 48, 49, S // 2])))
            o = np.concatenate([np.arange(48), 48 + rng.permutation(S - 48)]); herd, left = o[:S - n], o[S - n:]
            pos[a, g, herd] = rng.integers(-5, 6, (1, 3)) * rng.integers(-6, 7, (S - n, 1))
            b = np.zeros((S - n, 16), np.int64); b[:, :8] = rng.integers(3, 16, (S - n, 8))
            w = int(rng.integers(2 if i == 4 else 1, 16)); b[-1] = 0; b[-1, 0] = w
            pf[a, g, herd] = b
            x = rng.integers(0, 11, (n, 8)); pf[a, g, left] = np.concatenate([x, x + rng.integers(0, 6, (n, 8))], axis=1)
            v = int(rng.integers(1, w)) if i == 4 else 0
            first = 0 if i == 0 and a != one else m0
            th[a, g] = np.where(m < first, 15 * w + 1, rng.integers(15 * v + 1, 15 * w + 1, 16))
            if m0 < 16: th[a, g, m0] = 15 * w
            if i == 4:
                th[a, g, ms] = 15 * v; pf[a, g, left] = 0; pf[a, g, left, 0] = v
                pos[a, g, 48:, 0] = 5 * (2 * rng.integers(0, 2, S - 48) - 1); pos[a, g, 3 * ms:3 * ms + 3] = 16 * np.eye(3, dtype=np.int64)
    return pack(pos, pf, rf, th, lv)
def setup_inputs_ties(rng):
    pos, pf, rf, th, lv = parts(rng); gp = rng.permutation(8)
    base = rng.integers(0, 16, (N, 8, 1, 15)); o = np.argsort(rng.random((N, 8, S, 15)), axis=-1)
    pf[..., :15] = np.take_along_axis(np.broadcast_to(base, (N, 8, S, 15)), o, 3); pf[..., 15] = 1
    b = rng.choice(np.array([15, 14, 13, -15]), (N, 8, 1, 1)); rf[..., :15] = b; rf[..., 15] = rng.integers(-1, 2, (N, 8, W))
    th = (b * np.sum(base, axis=-1, keepdims=True)).reshape(N, 8, 1) + rng.integers(0, 2, (N, 8, 16))
    four = gp[3:6]; pos[:, four] = 4 * rng.integers(-7, 8, (N, 3, S, 3))
    up = ((HALF + 4096 >> SH) & 15) << (B1 + B2); dn = ((HALF - 4096 >> SH) & 15) << (B1 + B2)
    for i in range(3):
        g = int(gp[i])
        for a in range(N):
            kind = rng.integers(0, 2, 16); kind[0] = i % 2; kind[15] = 1 - i % 2
            pos[a, g] = 0; pf[a, g] = 0; lv[a, g] = 1; th[a, g] = rng.integers(1, 361, 16)
            pos[a, g, :48] = (16 * np.eye(3, dtype=np.int64)[None] * kind[:, None, None]).reshape(48, 3)
            x = 48 + rng.permutation(S - 48); h = (S - 48) // 2; one, two = x[:h], x[h:]
            pos[a, g, one, 0] = 16; pos[a, g, two, 0] = -16
            pf[a, g, one, :8] = rng.integers(3, 16, (h, 8)); pf[a, g, two, 8:] = rng.integers(3, 16, (S - 48 - h, 8))
            if i == 2 and a % 2 == 1: pf[a, g, one[0]] = 0
            rf[a, g, 0, :8] = 15; rf[a, g, 0, 8:] = 0; rf[a, g, up] = 0; rf[a, g, dn, :8] = 0; rf[a, g, dn, 8:] = 15
    g = int(gp[6]); s1 = 1 - 2 * ((np.arange(N) + int(rng.integers(0, 2))) % 2); lv[:, g] = 1
    pf[:, g] = 15; pf[:, g, :, 15] = rng.choice(np.array([1, 14, 15]), (N, S)); pf[:, g, S - 1, 15] = 14
    rf[:, g] = 15 * s1[:, None, None]
    rf[:, g, 1:, 15] = np.where(rng.random((N, W - 1)) < 0.4, 15 * s1[:, None], rng.choice(np.array([-14, -1, 0, 1, 14]), (N, W - 1)))
    th[:, g] = np.where(s1[:, None] > 0, rng.choice(np.array([3375, 3376, 3390, 3391, 3585, 3586, 3600]), (N, 16)), rng.choice(np.array([-3599, -3586, -3585, -3584, -3390, -3389, -3375]), (N, 16)))
    th[:, g, 15] = np.where(s1 > 0, 3586, -3585); th[:, g, 14] = np.where(s1 > 0, 3585, -3584)
    flat = rng.random((N, 16)) < 0.4; flat[:, 14:] = True
    pos[:, g, :48] = np.where(np.repeat(flat, 3, axis=1)[..., None], 0, pos[:, g, :48])
    g = int(gp[7]); lv[:, g] = 1; k = int(rng.integers(16, 31)); mm = int(rng.integers(0, 15))
    tri = np.array([[0, 0, 0], [k + 1, 31, -31], [k, 31, 31]]); e = np.arange(-31, 32)
    grid = np.stack(np.meshgrid(e, e, e, indexing="ij"), axis=-1).reshape(-1, 3)
    y = np.matmul(grid, np.cross(tri[1], tri[2])) + HALF
    c1 = y & (2 * HALF - 1); c2 = (y - grid[:, 0]) & (2 * HALF - 1)
    edge = grid[(c1 >= QLO) & (c1 < QHI) & ((c2 < QLO) | (c2 >= QHI))]
    pos[:, g, 45:48] = tri; pos[:, g, 3 * mm:3 * mm + 3] = tri[[0, 2, 1]]
    for a in range(N):
        x = np.append(48 + rng.permutation(S - 49)[:S // 4], S - 1); pos[a, g, x] = edge[rng.integers(0, len(edge), len(x))]
    th[:, g, mm] = -3600; th[:, g, 15] = -3600
    return pack(pos, pf, rf, th, lv)
def check_inputs(d):
    bad = []
    for k, lo, hi in (("pos", -31, 31), ("pf", 0, 15), ("rf", -15, 15), ("th", -3600, 3600), ("lv", 0, 1)):
        v = np.asarray(d[k]).astype(np.float32)
        if not (np.min(v) >= lo and np.max(v) <= hi): bad.append("range of " + k)
        if not np.all(np.floor(v) == v): bad.append("whole numbers in " + k)
    return bad
def judge(ax, P, I, R, T):
    y = np.matmul(ax, P[:, None]) + HALF
    c = y & (2 * HALF - 1); inside = np.all((c >= QLO) & (c < QHI), axis=2); n = y >> SH
    place = ((n[:, :, 0] & (2 ** B0 - 1)) << (B1 + B2)) + ((n[:, :, 1] & (2 ** B1 - 1)) << B2) + (n[:, :, 2] & (2 ** B2 - 1))
    score = np.add.reduce(R[np.arange(8)[:, None, None], place] * I[:, None], axis=-1)
    return inside & (score >= T)
def reference(pos, pf, rf, th, lv):
    P = pos.astype(np.float32).astype(np.int64).reshape(N, 8, 3, S)
    I = np.ascontiguousarray(pf.astype(np.float32).astype(np.int32).reshape(N, 8, 16, S).transpose(0, 1, 3, 2))
    R = np.ascontiguousarray(rf.astype(np.float32).astype(np.int32).reshape(N, 8, 16, W).transpose(0, 1, 3, 2))
    T = th.astype(np.int64).reshape(N, 8, 16, 1); live = lv.reshape(N, 8, S) != 0
    age = live.astype(np.int64); counts = []
    for t in range(RO):
        order = np.argsort(np.where(live, 0, 1), axis=-1, kind="stable")[..., :48]
        there = np.arange(48) < np.add.reduce(live, axis=-1, dtype=np.int64)[..., None]
        seed = (np.take_along_axis(P, order[:, :, None, :], 3) * there[:, :, None, :]).transpose(0, 1, 3, 2)
        p, q, s = seed[:, :, 0::3], seed[:, :, 1::3], seed[:, :, 2::3]
        ax = np.stack([np.cross(q, s), np.cross(s, p), np.cross(p, q)], axis=3)
        cnt = np.zeros((N, 8, 16), np.int64); hits = []
        for a in range(N):
            for i in range(J + 1):
                b = a if i == 0 else (a + t * J + i) % N
                h = judge(ax[a], P[b], I[b], R[b], T[b]); hits.append((a, b, h))
                cnt[a] = cnt[a] + np.add.reduce(h & live[b][:, None, :], axis=-1, dtype=np.int64)
        win = np.argmax(cnt, axis=2)
        die = np.zeros((N, 8, S), bool)
        for a, b, h in hits: die[b] = die[b] | h[np.arange(8), win[a]]
        live = live & ~die; age = age + live; counts.append(cnt)
    return {"yc": np.stack(counts, axis=-1).reshape(N, 128, RO).astype(np.float32), "ya": age.astype(np.float32)}

@@ -1,0 +1,584 @@
+from concourse.bass import DstId, RemoteDMATransfer
+from concourse.mybir import AluOpType as ALU, AxisListType as AX, ActivationFunctionType as AF
+
+N = 8
+S = 256
+N0 = 192
+N1 = 96
+Q0 = N0 // 4
+H1 = N1 // 2
+U0 = 64
+BIG = 32768.0
+WC = 3145536.0
+PWS = 56
+GW = 8 * max(Q0, H1)
+
+SCRATCH = {
+    "lv8": ("sbuf", [8, 256], "int32"),
+    "d8": ("sbuf", [8, 256], "bfloat16"),
+    "ps": ("sbuf", [24, 256], "bfloat16"),
+    "pfs": ("sbuf", [128, 256], "bfloat16"),
+    "pfm": ("sbuf", [128, 256], "bfloat16"),
+    "pfx": ("sbuf", [128, (S - N1) * 16], "bfloat16"),
+    "pfd": ("sbuf", [128, N0 * 8], "bfloat16"),
+    "ths": ("sbuf", [128, 4], "int32"),
+    "th16": ("sbuf", [16, 16], "int32"),
+    "thu": ("sbuf", [16, 32], "float32"),
+    "thh": ("sbuf", [16, 16], "bfloat16"),
+    "tht": ("sbuf", [16, 128], "bfloat16"),
+    "gd": ("sbuf", [16, GW], "bfloat16"),
+    "rfs": ("sbuf", [128, 4112], "bfloat16"),
+    "ones": ("sbuf", [128, 384], "bfloat16"),
+    "ip": ("sbuf", [128, 128], "bfloat16"),
+    "gr": ("sbuf", [128, 128], "bfloat16"),
+    "i3": ("sbuf", [128, 24], "float32"),
+    "t8": ("sbuf", [24, 8], "float32"),
+    "rep": ("sbuf", [8, 128], "bfloat16"),
+    "pa": ("sbuf", [24, 128], "bfloat16"),
+    "pb": ("sbuf", [24, 128], "bfloat16"),
+    "pc": ("sbuf", [24, 128], "bfloat16"),
+    "g192": ("sbuf", [128, 2], "bfloat16"),
+    "cols": ("sbuf", [128, 16], "float32"),
+    "b8": ("sbuf", [128, 8], "float32"),
+    "idm": ("sbuf", [128, 128], "bfloat16"),
+    "wa0": ("sbuf", [128, 128], "bfloat16"),
+    "wa1": ("sbuf", [128, 128], "float16"),
+    "wn": ("sbuf", [128, 128], "bfloat16"),
+    "wb1": ("sbuf", [128, 128], "bfloat16"),
+    "wb2": ("sbuf", [128, 128], "bfloat16"),
+    "blk": ("sbuf", [128, 128], "float32"),
+    "offb": ("sbuf", [128, 128], "bfloat16"),
+    "m16": ("sbuf", [128, 16], "float32"),
+    "zz": ("sbuf", [128, 144], "bfloat16"),
+    "yy": ("sbuf", [128, 752], "bfloat16"),
+    "eo": ("sbuf", [128, 24], "uint16"),
+    "wa": ("sbuf", [128, 272], "bfloat16"),
+    "wb": ("sbuf", [128, 272], "bfloat16"),
+    "posr": ("sbuf", [128, 256], "bfloat16"),
+    "dead": ("sbuf", [128, 512], "bfloat16"),
+    "cum": ("sbuf", [128, 256], "bfloat16"),
+    "junk": ("sbuf", [128, 768], "bfloat16"),
+    "si": ("sbuf", [128, 4], "float32"),
+    "ofi": ("sbuf", [128, 8], "uint16"),
+    "ga": ("sbuf", [128, 64], "bfloat16"),
+    "pw": ("sbuf", [128, 6 * PWS + 8], "float32"),
+    "px": ("sbuf", [128, 3 * 384], "float16"),
+    "cc": ("sbuf", [128, 2304], "bfloat16"),
+    "aa": ("sbuf", [128, 2304], "bfloat16"),
+    "bb": ("sbuf", [128, 2304], "bfloat16"),
+    "ofv": ("sbuf", [128, 3 * S], "uint16"),
+    "ofs": ("sbuf", [128, 2 * N1], "uint16"),
+    "gv": ("sbuf", [128, 3 * (S - N1) * 16], "bfloat16"),
+    "gs0": ("sbuf", [128, N0 * 16], "bfloat16"),
+    "gsr": ("sbuf", [128, N1 * 32], "bfloat16"),
+    "dq": ("sbuf", [128, 3 * GW], "bfloat16"),
+    "hit": ("sbuf", [128, 768], "bfloat16"),
+    "cn": ("sbuf", [128, 8], "float32"),
+    "lc": ("sbuf", [128, 40], "float32"),
+    "key": ("sbuf", [128, 8], "float32"),
+    "kd": ("sbuf", [128, 48], "float32"),
+    "mn": ("sbuf", [128, 4], "float32"),
+    "seld": ("sbuf", [128, 384], "bfloat16"),
+    "base": ("sbuf", [8, 256], "float32"),
+    "yas": ("sbuf", [8, 256], "float32"),
+    "ycs": ("sbuf", [128, 2], "float32"),
+    "da": ("psum", [128, 1024], "float32"),
+    "db": ("psum", [128, 1024], "float32"),
+    "sc0": ("psum", [128, 512], "float32"),
+    "sc1": ("psum", [128, 512], "float32"),
+    "sc2": ("psum", [128, 512], "float32"),
+    "scs": ("psum", [128, 512], "float32"),
+}
+SEMAPHORES = ["cv", "cs", "cp", "cg", "llv", "lps", "lpf", "lth", "lt0", "lt1", "lrf", "oya", "oyc", "sent",
+              "ax01", "ax02", "ax11", "ax12", "ct0", "ct1"]
+
+
+def deal_engines(topo, src, dsts):
+    off = [d for d in dsts if topo.chip(d) != topo.chip(src)]
+    on = [d for d in dsts if topo.chip(d) == topo.chip(src)]
+    pool = [e for e in topo.engines(src, off[0]) if all(e in topo.engines(src, d) for d in off)]
+    share = 1
+    while share * 2 * len(off) <= len(pool):
+        share *= 2
+    out = {}
+    for d in off:
+        out[d], pool = pool[:share], pool[share:]
+    for d in on:
+        if len(pool) < share:
+            used = [e for v in out.values() for e in v]
+            pool = [e for e in topo.engines(src, d) if e not in used]
+        out[d], pool = pool[:share], pool[share:]
+    return out
+
+
+def rank_program(g, core, T, topo):
+    rank = T.rank_of(core)
+    if rank is None:
+        return
+    cores = T.cores
+    E = {"v": g.vector, "s": g.scalar, "p": g.tensor, "g": g, "y": g.sync}
+    SEM = {"v": "cv", "s": "cs", "p": "cp", "g": "cg"}
+    cnt = {"cv": 0, "cs": 0, "cp": 0, "cg": 0}
+    final = {}
+    waited = {q: {} for q in E}
+    W, R, X = {}, {}, {}
+    pend = {q: ([], [], []) for q in E}
+
+    def need(q, deps):
+        best = {}
+        for s_, v_ in deps:
+            best[s_] = max(best.get(s_, 0), v_)
+        for s_, v_ in best.items():
+            if waited[q].get(s_, 0) < v_:
+                E[q].wait_ge(T.sem[s_], v_)
+                waited[q][s_] = v_
+
+    def deps_of(q, r, w, x):
+        own = SEM.get(q)
+        deps = []
+        for k in r:
+            deps.append(W[k])
+        for k in w:
+            if k in W:
+                deps.append(W[k])
+            deps.extend(R.get(k, {}).items())
+        if q == "p":
+            deps = [d for d in deps if d[0] != own]
+        for k in x:
+            deps.extend([d for d in X.get(k, {}).items() if d[0] != own])
+        return deps
+
+    def note(tok, r, w, x):
+        for k in r:
+            R.setdefault(k, {})[tok[0]] = tok[1]
+        for k in w:
+            W[k] = tok
+            R[k] = {}
+        for k in x:
+            X.setdefault(k, {})[tok[0]] = tok[1]
+
+    def op(q, fn, r=(), w=(), x=(), inc=True):
+        need(q, deps_of(q, r, w, x))
+        ins = fn()
+        p_ = pend[q]
+        p_[0].extend(r); p_[1].extend(w); p_[2].extend(x)
+        if inc:
+            s_ = SEM[q]
+            cnt[s_] += 1
+            ins.then_inc(T.sem[s_], 1)
+            note((s_, cnt[s_]), p_[0], p_[1], p_[2])
+            pend[q] = ([], [], [])
+
+    def dma(q, sem, out, in_, r=(), w=()):
+        need(q, deps_of(q, r, w, ()))
+        E[q].dma_start(out, in_).then_inc(T.sem[sem], 16)
+        note((sem, 16), r, w, ())
+        final[sem] = 16
+
+    V, A, P = g.vector, g.scalar, g.tensor
+
+    def ts(out, in0, s1, s2, o0, o1, r, w, x=()):
+        if o1 is None:
+            op("v", lambda: V.tensor_scalar(out, in0, s1, None, o0), r, w, x)
+        else:
+            op("v", lambda: V.tensor_scalar(out, in0, s1, s2, o0, o1), r, w, x)
+
+    def ms(ap, c, w):
+        op("v", lambda: V.memset(ap, c), (), w)
+
+    def mm(out, lhsT, rhs, start, stop, r, w, x, inc=None):
+        op("p", lambda: P.matmul(out, lhsT, rhs, start, stop), r, w, x, stop if inc is None else inc)
+
+    def act(out, in_, func, r, w, x=(), inc=True, **kw):
+        op("s", lambda: A.activation(out, in_, func, **kw), r, w, x, inc)
+
+    def col(i, n=128):
+        return T.cols[0:n, i:i + 1]
+    N16G, TIE, B0, B1, TH2, N80G, THB, YB, CA, CB = range(10)
+
+    sent = [0]
+
+    def send(pieces, r):
+        eng = deal_engines(topo, core, [cores[p_[0]] for p_ in pieces])
+        trs = []
+        for d, src, dst, sem in pieces:
+            rid, pid, _ = topo.addr(cores[d])
+            mask = sum(1 << e for e in eng[cores[d]])
+            trs.append(RemoteDMATransfer(dst_ids=[DstId(rid=rid, pnc=pid)], dma_engine_mask=mask,
+                                         remote_sem=T.sem[sem], src=src, dst=dst))
+            sent[0] += len(eng[cores[d]])
+        need("g", deps_of("g", r, (), ()))
+        g.remote_dma_fused(trs, local_sem=T.sem.sent)
+
+    dma("y", "llv", T.lv8[:], T.lv[:], w=["lv8"])
+    dma("s", "lps", T.ps[:], T.pos[:], w=["ps"])
+    dma("y", "lpf", T.pfs[:], T.pf[:], w=["pfs"])
+    dma("s", "lt0", T.th16[0:8, :], T.th[:], w=["th16a"])
+    dma("y", "lt1", T.th16[8:16, :], T.th[:], w=["th16b"])
+    dma("s", "lth", T.ths[:, 0:1], T.th[:], w=["ths"])
+    dma("y", "lrf", T.rfs[:, 0:4096], T.rf[:], w=["rf"])
+
+    flag = {"allow_small_or_imprecise_dtypes": True}
+
+    def select(out, in_, pattern, cmp_, fill, base, r, w):
+        op("g", lambda: g.affine_select(out, in_, pattern, cmp_, fill, base, 1), r, w)
+
+    ms(T.ones[:], BIG, ["ones"])
+    op("g", lambda: g.iota(T.ip[:], [[1, 128]], 0, -1, **flag), w=["ip"])
+    select(T.rep[:], T.ones[0:8, 0:128], [[-1, 8], [0, 16]], ALU.is_equal, 0.0, 0, ["ones"], ["rep"])
+    select(T.pa[:], T.ones[0:24, 0:128], [[-3, 8], [-1, 4], [0, 4]], ALU.is_equal, 0.0, 0, ["ones"], ["pa"])
+    select(T.pb[:], T.ones[0:24, 0:128], [[-3, 8], [0, 4], [-1, 4]], ALU.is_equal, 0.0, 0, ["ones"], ["pb"])
+    op("g", lambda: g.iota(T.t8[:], [[-3, 8]], 0, 1, **flag), w=["t8"])
+    op("g", lambda: g.iota(T.gr[:], [[1, 8], [0, 16]], 192, 0, **flag), w=["gr"])
+    op("g", lambda: g.iota(T.i3[:], [[16, 3], [64, 8]], 8, 1, **flag), w=["i3"])
+    select(T.gd[:], T.ones[0:16, 0:GW], [[0, GW // 8], [-1, 8]], ALU.is_equal, 0.0, 0, ["ones"], ["gd"])
+
+    ms(T.pc[:], 0.0, ["pc0"])
+    ms(T.wa[:, 256:272], 0.0, ["waz"])
+    ms(T.wb[:, 256:272], 0.0, ["wbz"])
+    ts(T.g192[:, 0:1], T.ip[:, 0:1], -1.0 / 16, 191.53125, ALU.mult, ALU.add, ["ip"], ["g192"])
+    ts(T.idm[:], T.ip[:], 0.0, None, ALU.is_equal, None, ["ip"], ["idm"])
+    ts(col(N16G), T.g192[:, 0:1], -192.0, -16.0, ALU.add, ALU.mult, ["g192"], ["n16g"])
+    ts(col(N80G), T.g192[:, 0:1], -192.0, -80.0, ALU.add, ALU.mult, ["g192"], ["n80g"])
+    ts(col(TIE), T.ip[:, 0:1], col(N16G), -1.0 / 16, ALU.subtract, ALU.mult, ["ip", "n16g"], ["tie"])
+    ts(T.wa1[:], T.idm[:], 511.0 / 512, None, ALU.mult, None, ["idm"], ["wa1"])
+    ts(col(B0), col(TIE), -48.0, -0.5, ALU.mult, ALU.add, ["tie"], ["b0"])
+    ts(col(B1), col(TIE), -48.0, -1.5, ALU.mult, ALU.add, ["tie"], ["b1"])
+    ts(col(TH2), col(TIE), 48.0 * BIG, 2.5 * BIG, ALU.mult, ALU.add, ["tie"], ["th2"])
+    ms(T.zz[:], 0.0, ["zz0"])
+    ms(T.yy[:], 0.0, ["yy0"])
+    ms(T.rfs[:, 4096:4112], -1048576.0, ["rfz"])
+    for i in range(4):
+        ms(T.pw[:, PWS * i:PWS * i + 8], 0.0, ["pwz%d" % i])
+    for name, sc in (("wn", -2.0 ** -13), ("wa0", 31.0 / 32), ("wb1", 1.0 / 16), ("wb2", 1.0 / 256)):
+        act(T[name][:], T.idm[:], AF.Copy, ["idm"], [name], scale=sc)
+    YROW = [0, 16, 32, 64, 96]
+    for i, rb in enumerate(YROW):
+        act(T.yy[:, 128 * i + 112:128 * i + 128], T.idm[:, rb:rb + 16], AF.Copy, ["idm", "yy0"], ["yy%d" % rb], scale=8192.0)
+
+    ts(T.d8[:], T.lv8[:], -1.0, 1.0, ALU.mult, ALU.add, ["lv8"], ["d8"])
+    mm(T.da[:, 512:768], T.pa[:], T.ps[:], True, True, ["pa", "ps"], ["wap"], ["da1"])
+    mm(T.db[:, 0:256], T.pb[:], T.ps[:], True, True, ["pb", "ps"], ["wbp"], ["db0"])
+    mm(T.da[:, 0:256], T.rep[:], T.d8[:], True, True, ["rep", "d8"], ["drep"], ["da0"])
+    act(T.wa[:, 0:256], T.da[:, 512:768], AF.Copy, ["wap"], ["wa"], ["da1"], scale=1.0 / BIG)
+    act(T.wb[:, 0:256], T.db[:, 0:256], AF.Copy, ["wbp"], ["wb"], ["db0"], scale=1.0 / BIG)
+    TERMS = ((0, 1, 2, 1.0), (1, 2, 0, 1.0), (2, 0, 1, 1.0), (1, 0, 2, -1.0), (2, 1, 0, -1.0), (0, 2, 1, -1.0))
+    pck = ["pc%d" % i for i in range(6)]
+
+    def terms(lo, hi):
+        for i in range(lo, hi):
+            a, b, c, sg = TERMS[i]
+            ts(T.pc[:, 4 * a + b::16], T.t8[:], float(c), sg, ALU.is_equal, ALU.mult, ["t8", "pc0"], [pck[i]])
+    ts(T.pfm[:], T.pfs[:], 1.0 / 512, None, ALU.max, None, ["pfs"], ["pfm"])
+    terms(0, 1)
+
+    SCB = [T.sc0, T.sc1, T.sc2]
+    pfxk = ["pfx%d" % m for m in range(16)]
+    pfdk = ["pfd%d" % m for m in range(8)]
+
+    def one_round(t):
+        offs = [0, 2 * t + 1, 2 * t + 2]
+        dead = T.dead[:, 256 * t:256 * t + 256]
+        dk = "dead%d" % t
+        first = t == 0
+
+        if first:
+            op("v", lambda: V.tensor_tensor_scan(T.cum[:], T.ones[:, 0:256], T.da[:, 0:256], 0.0, ALU.add, ALU.subtract),
+               ["ones", "drep"], ["cum"], ["da0"])
+        else:
+            op("v", lambda: V.tensor_tensor_scan(T.cum[:], T.ones[:, 0:256], dead, 0.0, ALU.add, ALU.subtract),
+               ["ones", dk], ["cum"])
+        ts(T.junk[:, 512:768], T.cum[:], col(TH2), None, ALU.is_le, None, ["cum", "th2"], ["le"])
+        for k in range(2):
+            act(T.junk[:, 256 * k:256 * k + 256], T.cum[:], AF.Sign, ["cum", "b%d" % k], ["si%d" % k, "j%d" % k],
+                bias=col(B0 + k), scale=1.0 / BIG, accum_out=T.si[:, k:k + 1])
+        op("v", lambda: V.tensor_reduce(T.si[:, 2:3], T.junk[:, 512:768], AX.X, ALU.add), ["le"], ["si2"])
+        if first:
+            terms(1, 6)
+            mm(T.db[:, 512:768], T.pc[:], T.ps[:], True, True, ["ps"] + pck, ["prp"], ["db1"])
+            act(T.posr[:], T.db[:, 512:768], AF.Copy, ["prp"], ["posr"], ["db1"])
+            act(dead, T.da[:, 0:256], AF.Copy, ["drep"], [dk], ["da0"])
+        op("v", lambda: V.tensor_copy(T.ofi[:, 2:3], T.si[:, 2:3]), ["si2"], ["ofi2"])
+        ts(T.ofi[:, 0:2], T.si[:, 0:2], -0.5, 128.0, ALU.mult, ALU.add, ["si0", "si1"], ["ofi0"])
+        ts(T.ofi[:, 3:5], T.si[:, 0:2], -0.5, 128.0, ALU.mult, ALU.add, ["si0", "si1"], ["ofi3"])
+        op("v", lambda: V.tensor_copy(T.ga[:], T.wa[:, 0:272].indirect(T.ofi[:, 0:4])),
+           ["wa", "waz", "ofi0", "ofi2", "ofi3"], ["ga"])
+        if first:
+            ts(T.eo[:], T.i3[:], col(N80G), 56.0, ALU.add, ALU.min, ["i3", "n80g"], ["eo"])
+        w0 = PWS * 3 * t
+        op("v", lambda: V.tensor_tensor(T.pw[:, w0 + 8:w0 + 56], T.wb[:, 0:272].indirect(T.ofi[:, 2:5]), T.ga[:, 16:64], ALU.mult),
+           ["wb", "wbz", "ofi0", "ofi2", "ofi3", "ga"], ["pw%d0" % t])
+        send([((rank + offs[s]) % N, T.pw[:, w0 + 8:w0 + 56], T.pw[:, w0 + PWS * s + 8:w0 + PWS * s + 56], "ax%d%d" % (t, s))
+              for s in (1, 2)], ["pw%d0" % t])
+        for s in (1, 2):
+            a = (rank - offs[s]) % N
+            n_ = len(deal_engines(topo, cores[a], [cores[(a + offs[1]) % N], cores[(a + offs[2]) % N]])[core])
+            W["pw%d%d" % (t, s)] = ("ax%d%d" % (t, s), n_)
+        if first:
+            select(T.gd[:], T.gd[:], [[0, GW // 8], [-1, 8]], ALU.not_equal, BIG, -8, ["gd"], ["gd"])
+
+        def expand(s):
+            i = 3 * t + s
+            op("v", lambda: V.tensor_copy(T.px[:, 384 * s:384 * s + 384], T.pw[:, PWS * i:PWS * i + 64].indirect(T.eo[:, 0:24])),
+               ["pw%d%d" % (t, s), "pwz%d" % i, "pwz%d" % (i + 1), "eo"], ["px%d" % s])
+
+        units = [(0, 0, U0, "da", 0, "sc1"), (0, U0, S, "db", 512 - 2 * (S - U0), "sc2"),
+                 (1, 0, S, "da", 0, "sc1"), (2, 0, S, "db", 0, "sc2")]
+        width = [u[2] - u[1] for u in units]
+        at = [3 * sum(width[:u]) for u in range(4)]
+
+        def banks(u):
+            return [units[u][3] + "0"] + ([units[u][3] + "1"] if units[u][4] + 3 * width[u] > 512 else [])
+
+        def dot(u):
+            s, lo, hi, buf, c0, _ = units[u]
+            for j in range(3):
+                c = c0 + j * (hi - lo)
+                mm(T[buf][:, c:c + hi - lo], T.px[:, 384 * s + 128 * j:384 * s + 128 * j + 128], T.posr[:, lo:hi],
+                   True, True, ["px%d" % s, "posr"], ["dot%d" % u], banks(u), inc=(j == 2))
+
+        def round_c(u):
+            buf, c0 = units[u][3:5]
+            n_ = 3 * width[u]
+            act(T.cc[:, at[u]:at[u] + n_], T[buf][:, c0:c0 + n_], AF.Identity, ["dot%d" % u], ["c%d" % u], banks(u),
+                bias=786433.0, scale=2.0)
+
+        def round_ab(u):
+            sl = slice(at[u], at[u] + 3 * width[u])
+            ts(T.aa[:, sl], T.cc[:, sl], 784384.0, -1.0, ALU.add, ALU.mult, ["c%d" % u], ["a%d" % u])
+            ts(T.bb[:, sl], T.cc[:, sl], -1.0 / 32, -759872.0, ALU.mult, ALU.add, ["c%d" % u], ["b_%d" % u])
+
+        def place(u):
+            s, lo, hi, _, _, bank = units[u]
+            n_ = width[u]
+            out = T[bank][:, 256:256 + n_]
+            part = lambda buf, j: buf[:, at[u] + n_ * j:at[u] + n_ * j + n_]
+            wk = ["w%d" % u]
+            mm(out, T.idm[:], T.dead[:, 256 * t + lo:256 * t + hi], True, False, ["idm", dk], wk, [bank])
+            for j in range(3):
+                mm(out, T.idm[:], part(T.cc, j), False, False, ["c%d" % u], wk, [bank])
+            for wt, j in (("wa0", 0), ("wa1", 1), ("idm", 2), ("wn", 2)):
+                mm(out, T[wt][:], part(T.aa, j), False, False, [wt, "a%d" % u], wk, [bank])
+            for wt, j in (("idm", 0), ("wb1", 1), ("wb2", 2)):
+                mm(out, T[wt][:], part(T.bb, j), False, j == 2, [wt, "b_%d" % u], wk, [bank])
+
+        def conv(u):
+            s, lo, hi, _, _, bank = units[u]
+            if s > 0:
+                ts(T.ofs[:, s - 1::2], T[bank][:, 256:256 + N1], WC, 4096.0, ALU.add, ALU.min, ["w%d" % u], ["ofs%d" % s], [bank])
+                lo = N1
+            c = 256 + lo - units[u][1]
+            ts(T.ofv[:, S * s + lo:S * s + hi], T[bank][:, c:c + hi - lo], WC, 4096.0, ALU.add, ALU.min,
+               ["w%d" % u], ["ofv%d" % u], [bank])
+
+        win = T.rfs[:, 0:4112]
+
+        def gather(s, lo, hi):
+            b = (S - N1) * 16 * s - 16 * N1
+            op("v", lambda: V.tensor_tensor(T.gv[:, b + 16 * lo:b + 16 * hi], win.indirect(T.ofv[:, S * s + lo:S * s + hi]),
+                                            T.pfx[:, 16 * (lo - N1):16 * (hi - N1)], ALU.mult),
+               ["rf", "rfz", "ofv%d" % (s + 1)] + pfxk, ["gv%d_%d" % (s, lo)])
+
+        def score(s, lo, hi, more=()):
+            b = (S - N1) * 16 * s - 16 * N1
+            for m in range(16):
+                mm(SCB[s][:, lo:hi], T.zz[:, 15 - m:143 - m], T.gv[:, b + 16 * lo + m:b + 16 * hi:16], m == 0, m == 15,
+                   ["zz"] + ["gv%d_%d" % (s, c) for c in [lo] + list(more)], ["sc%d_%d" % (s, lo)], ["sc%d" % s])
+
+        def sgather0(lo, hi):
+            act(T.gs0[:, 16 * lo:16 * hi], win.indirect(T.ofv[:, lo:hi]), AF.Copy,
+                ["rf", "rfz", "ofv0"] + (["ofv1"] if hi > U0 else []), ["gs0_%d" % lo])
+
+        def weigh0(lo, hi):
+            if lo == 0:
+                mm(T.scs[:, 0:8 * Q0], T.tht[:], T.gd[:, 0:8 * Q0], True, False, ["tht", "gd"], ["q0"], ["scs"])
+            for x in range(lo, hi):
+                q, xh = divmod(x, Q0)
+                mm(T.scs[32 * q:32 * q + 16, 8 * xh:8 * xh + 8], T.gs0[:, 16 * x:16 * x + 16], T.pfd[:, 8 * x:8 * x + 8],
+                   False, False, ["gs0_%d" % lo] + pfdk, ["q0"], ["scs"], inc=(x == hi - 1 and hi < N0))
+            if hi == N0:
+                mm(T.scs[:, 0:8 * Q0], T.tht[:], T.gd[:, 0:8 * Q0], False, True, ["tht", "gd"], ["q0"], ["scs"])
+
+        def sign0():
+            act(T.dq[:, 0:8 * Q0], T.scs[:, 0:8 * Q0], AF.Sign, ["q0"], ["dq0"], ["scs"])
+
+        def move0():
+            for q in range(4):
+                c = 128 * YROW.index(32 * q) + 112
+                for k in range(8):
+                    mm(T.sc0[:, Q0 * q:Q0 * q + Q0], T.yy[:, c - 16 * k:c - 16 * k + 128], T.dq[:, k:8 * Q0:8], k == 0, k == 7,
+                       ["dq0", "yy%d" % (32 * q)], ["sc0_q"], ["sc0"], inc=(q == 3 and k == 7))
+
+        def sgather1(lo, hi):
+            act(T.gsr[:, 32 * lo:32 * hi], win.indirect(T.ofs[:, 2 * lo:2 * hi]), AF.Copy,
+                ["rf", "rfz", "ofs1", "ofs2"], ["gsr_%d" % lo])
+
+        def weigh1(lo, hi):
+            h = lo // H1
+            if lo % H1 == 0:
+                mm(T.da[0:32, 512 * h:512 * h + 8 * H1], T.tht[:, 0:32], T.gd[:, 0:8 * H1], True, False,
+                   ["tht", "gd"], ["q1%d" % h], ["da%d" % h])
+            for x in range(lo, hi):
+                c = 512 * h + 8 * (x - H1 * h)
+                mm(T.da[0:32, c:c + 8], T.gsr[:, 32 * x:32 * x + 32], T.pfd[:, 8 * x:8 * x + 8],
+                   False, False, ["gsr_%d" % lo] + pfdk, ["q1%d" % h], ["da%d" % h], inc=(x == hi - 1 and hi % H1 > 0))
+            if hi % H1 == 0:
+                mm(T.da[0:32, 512 * h:512 * h + 8 * H1], T.tht[:, 0:32], T.gd[:, 0:8 * H1], False, True,
+                   ["tht", "gd"], ["q1%d" % h], ["da%d" % h])
+
+        def sign1(h):
+            act(T.dq[0:32, GW * (h + 1):GW * (h + 1) + 8 * H1], T.da[0:32, 512 * h:512 * h + 8 * H1], AF.Sign,
+                ["q1%d" % h], ["dq1%d" % h], ["da%d" % h])
+
+        def move1(h):
+            for s in (1, 2):
+                c = 128 * YROW.index(16 * (s - 1)) + 112
+                for k in range(8):
+                    mm(SCB[s][:, H1 * h:H1 * h + H1], T.yy[0:32, c - 16 * k:c - 16 * k + 128],
+                       T.dq[0:32, GW * (h + 1) + k:GW * (h + 1) + 8 * H1:8], k == 0, k == 7,
+                       ["dq1%d" % h, "yy%d" % (16 * (s - 1))], ["sc%d_q%d" % (s, h)], ["sc%d" % s])
+
+        def hits(s, keys):
+            act(T.hit[:, 256 * s:256 * s + S], SCB[s][:, 0:S], AF.Sign, ["thb"] + ["sc%d_%s" % (s, k) for k in keys],
+                ["hit%d" % s, "cn%d_%d" % (t, s)], ["sc%d" % s], bias=col(THB), scale=-1.0,
+                accum_out=T.cn[:, 4 * t + s:4 * t + s + 1])
+
+        def pfx_v(ms_):
+            for m in ms_:
+                op("v", lambda: V.tensor_copy(T.pfx[:, m::16], T.pfm[:, N1:S]), ["pfm"], [pfxk[m]])
+
+        def pfx_s(ms_):
+            for m in ms_:
+                act(T.pfx[:, m::16], T.pfm[:, N1:S], AF.Copy, ["pfm"], [pfxk[m]])
+
+        def pfd_v(ks):
+            for k in ks:
+                ts(T.pfd[:, k::8], T.pfm[:, 0:N0], T.b8[:, k:k + 1], None, ALU.mult, None, ["pfm", "b8"], [pfdk[k]])
+
+        expand(0)
+        dot(0); dot(1)
+        if first:
+            pfx_s(range(3))
+            for m in range(3, 13):
+                select(T.pfx[:, m::16], T.pfm[:, N1:S], [[0, S - N1]], ALU.is_ge, 0.0, 0, ["pfm"], [pfxk[m]])
+            ts(T.b8[:], T.gr[:, 0::16], T.g192[:, 0:1], None, ALU.is_equal, None, ["gr", "g192"], ["b8"])
+            ts(col(CA, 16), T.ip[0:16, 0:1], -8.0, -0.5 / BIG, ALU.is_le, ALU.mult, ["ip"], ["ca"])
+            ts(T.thh[:], T.th16[:], -0.5, -0.5 / BIG, ALU.add, ALU.mult, ["th16a", "th16b"], ["thh"])
+            ts(col(CB, 16), col(CA, 16), 4 * BIG, 1.0, ALU.mult, ALU.add, ["ca"], ["cb"])
+            ts(T.thu[:, 0:16], T.th16[:], -0.5, col(CA, 16), ALU.add, ALU.mult, ["th16a", "th16b", "ca"], ["thu0"])
+        round_c(0); round_c(1)
+        round_ab(0)
+        place(0)
+        if first:
+            ts(T.thu[:, 16:32], T.thh[:], col(CB, 16), None, ALU.mult, None, ["thh", "cb"], ["thu1"])
+            pfd_v(range(2))
+            op("v", lambda: V.tensor_tensor(T.tht[:, 0:16], T.thu[:, 0:16], T.thu[:, 16:32], ALU.add), ["thu0", "thu1"], ["tht"])
+        else:
+            mm(T.sc0[0:8, 256:512], T.wn[:, 0::16], T.dead[:, 0:256], True, False, ["wn", "dead0"], ["bp"], ["sc0"])
+            mm(T.sc0[0:8, 256:512], T.wn[:, 0::16], T.dead[:, 256:512], False, True, ["wn", "dead1"], ["bp"], ["sc0"])
+        conv(0)
+        sgather0(0, U0)
+        round_ab(1); place(1)
+        if first:
+            pfd_v(range(2, 8))
+            for n_ in (16, 32, 64):
+                act(T.tht[:, n_:2 * n_], T.tht[:, 0:n_], AF.Copy, ["tht"], ["tht"])
+        expand(1); dot(2); round_c(2)
+        conv(1)
+        expand(2); dot(3)
+        if first:
+            pfx_v(range(13, 16))
+            ts(T.zz[:, 15:143:16], T.gr[:, 0::16], T.g192[:, 0:1], None, ALU.is_equal, None, ["gr", "g192", "zz0"], ["zz"])
+            ts(col(THB), T.ths[:, 0:1], -0.5, None, ALU.add, None, ["ths"], ["thb"])
+        round_ab(2); place(2)
+        sgather0(U0, 128)
+        round_c(3)
+        gather(0, N0, S)
+        conv(2)
+        weigh0(0, U0)
+        weigh0(U0, 128)
+        round_ab(3); place(3)
+        sgather0(128, N0)
+        if not first:
+            act(T.base[:], T.sc0[0:8, 256:512], AF.Identity, ["bp"], ["base"], ["sc0"], bias=2.0, scale=0.25)
+        c0, c1, c2 = N1 + 32, N1 + 80, S - 64
+        h1, h2 = H1 // 2, H1 + H1 * 2 // 3
+        gather(1, N1, c0)
+        conv(3)
+        weigh0(128, N0)
+        score(0, N0, S)
+        sign0()
+        sgather1(0, h1)
+        gather(1, c0, c1)
+        move0()
+        sgather1(h1, H1)
+        weigh1(0, h1)
+        gather(1, c1, S)
+        score(1, N1, c1, [c0])
+        weigh1(h1, H1)
+        sgather1(H1, h2)
+        sign1(0)
+        gather(2, N1, c2)
+        score(1, c1, S)
+        weigh1(H1, h2)
+        sgather1(h2, N1)
+        move1(0)
+        weigh1(h2, N1)
+        hits(0, ["q", N0])
+        sign1(1)
+        gather(2, c2, S)
+        score(2, N1, c2)
+        move1(1)
+        hits(1, ["q0", "q1", N1, c1])
+        score(2, c2, S)
+        hits(2, ["q0", "q1", N1, c2])
+        if first:
+            ts(T.blk[:], T.gr[:], T.g192[:, 0:1], None, ALU.is_equal, None, ["gr", "g192"], ["blk"])
+            ts(T.offb[:], T.gr[:], T.g192[:, 0:1], 4096.0, ALU.not_equal, ALU.mult, ["gr", "g192"], ["offb"])
+            ts(T.m16[:], T.ip[:, 0:16], col(N16G), None, ALU.is_equal, None, ["ip", "n16g"], ["m16"])
+            ts(col(YB), col(TIE), 0.5, 384.0, ALU.mult, ALU.add, ["tie"], ["yb"])
+            for i in range(4, 7):
+                ms(T.pw[:, PWS * i:PWS * i + 8], 0.0, ["pwz%d" % i])
+
+        deltas = sorted(set((offs[b] - offs[a]) % N for a in range(3) for b in range(3) if a != b))
+        cnk = ["cn%d_%d" % (t, i) for i in range(3)]
+        send([((rank - d) % N, T.cn[:, 4 * t:4 * t + 3], T.lc[:, 20 * t + 4 * i:20 * t + 4 * i + 3], "ct%d" % t)
+              for i, d in enumerate(deltas)], cnk)
+        tot = 0
+        for d in deltas:
+            b = (rank + d) % N
+            tot += len(deal_engines(topo, cores[b], [cores[(b - e) % N] for e in deltas])[core])
+        W["lc%d" % t] = ("ct%d" % t, tot)
+        ts(T.key[:, 0:3], T.cn[:, 4 * t:4 * t + 3], col(TIE), None, ALU.add, None, cnk + ["tie"], ["k0"])
+        M = 128 if first else 8
+        mm(T.db[0:M, 0:256], T.wn[:] if first else T.wn[:, 0::16], dead, True, False, ["wn", dk], ["die"], ["db0"])
+        for s in range(3):
+            c = [20 * t + 4 * deltas.index((offs[q] - offs[s]) % N) + q for q in range(3) if q != s]
+            ts(T.key[:, 4 + s:5 + s], T.key[:, s:s + 1], T.lc[:, c[0]:c[0] + 1], T.lc[:, c[1]:c[1] + 1], ALU.add, ALU.add,
+               ["lc%d" % t, "k0"], ["k1%d" % s])
+        for s in range(3):
+            ts(T.kd[:, 16 * s:16 * s + 16], T.m16[:], T.key[:, 4 + s:5 + s], None, ALU.mult, None, ["m16", "k1%d" % s], ["kd%d" % s])
+        mm(T.da[:, 0:48], T.blk[:], T.kd[:], True, True, ["blk", "kd0", "kd1", "kd2"], ["kp"], ["da0"])
+        ts(T.ycs[:, t:t + 1], T.key[:, 4:5], -0.5, col(YB), ALU.mult, ALU.add, ["k10", "yb"], ["yc%d" % t])
+        if not first:
+            dma("s", "oyc", T.yc[:], T.ycs[:], r=["yc0", "yc1"])
+        for s in range(3):
+            op("v", lambda: V.tensor_reduce(T.mn[:, s:s + 1], T.da[:, 16 * s:16 * s + 16], AX.X, ALU.min),
+               ["kp"], ["mn%d" % s], ["da0"])
+        for s in range(3):
+            ts(T.seld[:, 128 * s:128 * s + M], T.offb[:] if first else T.offb[:, 0::16], T.key[:, 4 + s:5 + s], T.mn[:, s:s + 1],
+               ALU.add, ALU.is_le, ["offb", "k1%d" % s, "mn%d" % s], ["seld%d" % s])
+            mm(T.db[0:M, 0:256], T.seld[:, 128 * s:128 * s + M], T.hit[:, 256 * s:256 * s + 256], False, s == 2,
+               ["seld%d" % s, "hit%d" % s], ["die"], ["db0"])
+        if first:
+            ts(T.dead[:, 256:512], T.db[:, 0:256], 2.5, BIG, ALU.is_lt, ALU.mult, ["die"], ["dead1"], ["db0"])
+        else:
+            op("v", lambda: V.tensor_tensor(T.yas[:], T.db[0:8, 0:256], T.base[:], ALU.max), ["die", "base"], ["yas"], ["db0"])
+            dma("y", "oya", T.ya[:], T.yas[:], r=["yas"])
+
+    one_round(0)
+    one_round(1)
+
+    final.update(cnt)
+    final["sent"] = sent[0]
+    need("g", list(final.items()))

@@ -3,94 +3,90 @@ from concourse.mybir import AluOpType as ALU, AxisListType as AX, ActivationFunc
 
 N = 8
 S = 256
-N0 = 192
-N1 = 96
-Q0 = N0 // 4
-H1 = N1 // 2
-U0 = 64
-BIG = 32768.0
-WC = 3145536.0
-PWS = 56
-GW = 8 * max(Q0, H1)
+X = 128
+H = 64
 
 SCRATCH = {
     "lv8": ("sbuf", [8, 256], "int32"),
     "d8": ("sbuf", [8, 256], "bfloat16"),
+    "cum8": ("sbuf", [8, 256], "bfloat16"),
     "ps": ("sbuf", [24, 256], "bfloat16"),
-    "pfs": ("sbuf", [128, 256], "bfloat16"),
-    "pfm": ("sbuf", [128, 256], "bfloat16"),
-    "pfx": ("sbuf", [128, (S - N1) * 16], "bfloat16"),
-    "pfd": ("sbuf", [128, N0 * 8], "bfloat16"),
-    "ths": ("sbuf", [128, 4], "int32"),
+    "pfs": ("sbuf", [128, 320], "bfloat16"),
+    "pfx": ("sbuf", [128, 128 * 16], "bfloat16"),
+    "pfd": ("sbuf", [128, 128 * 8], "bfloat16"),
     "th16": ("sbuf", [16, 16], "int32"),
     "thu": ("sbuf", [16, 32], "float32"),
     "thh": ("sbuf", [16, 16], "bfloat16"),
-    "tht": ("sbuf", [16, 128], "bfloat16"),
-    "gd": ("sbuf", [16, GW], "bfloat16"),
-    "rfs": ("sbuf", [128, 4112], "bfloat16"),
-    "ones": ("sbuf", [128, 384], "bfloat16"),
-    "ip": ("sbuf", [128, 128], "bfloat16"),
+    "thq": ("sbuf", [32, 128], "bfloat16"),
+    "thx": ("sbuf", [16, 256], "bfloat16"),
+    "thm": ("sbuf", [16, 256], "bfloat16"),
+    "gd": ("sbuf", [32, 256], "bfloat16"),
+    "rf0": ("sbuf", [128, 4112], "bfloat16"),
+    "rf1": ("sbuf", [128, 4112], "bfloat16"),
+    "one": ("sbuf", [128, 256], "bfloat16"),
+    "o193": ("sbuf", [128, 256], "bfloat16"),
+    "dc": ("sbuf", [1, 4 * 128], "bfloat16"),
+    "pp": ("sbuf", [128, 3], "float32"),
+    "jr": ("sbuf", [128, 32], "bfloat16"),
     "gr": ("sbuf", [128, 128], "bfloat16"),
-    "i3": ("sbuf", [128, 24], "float32"),
-    "t8": ("sbuf", [24, 8], "float32"),
+    "t16": ("sbuf", [24, 32], "float32"),
     "rep": ("sbuf", [8, 128], "bfloat16"),
     "pa": ("sbuf", [24, 128], "bfloat16"),
     "pb": ("sbuf", [24, 128], "bfloat16"),
-    "pc": ("sbuf", [24, 128], "bfloat16"),
-    "g192": ("sbuf", [128, 2], "bfloat16"),
-    "cols": ("sbuf", [128, 16], "float32"),
-    "b8": ("sbuf", [128, 8], "float32"),
+    "pc": ("sbuf", [24, 256], "bfloat16"),
+    "fl": ("sbuf", [128, 4], "bfloat16"),
+    "cols": ("sbuf", [128, 24], "float32"),
+    "b8": ("sbuf", [128, 16], "float32"),
     "idm": ("sbuf", [128, 128], "bfloat16"),
-    "wa0": ("sbuf", [128, 128], "bfloat16"),
-    "wa1": ("sbuf", [128, 128], "float16"),
     "wn": ("sbuf", [128, 128], "bfloat16"),
-    "wb1": ("sbuf", [128, 128], "bfloat16"),
-    "wb2": ("sbuf", [128, 128], "bfloat16"),
+    "mask": ("sbuf", [128, 384], "bfloat16"),
+    "sel": ("sbuf", [128, 192], "bfloat16"),
     "blk": ("sbuf", [128, 128], "float32"),
+    "id2": ("sbuf", [128, 128], "float32"),
     "offb": ("sbuf", [128, 128], "bfloat16"),
     "m16": ("sbuf", [128, 16], "float32"),
     "zz": ("sbuf", [128, 144], "bfloat16"),
-    "yy": ("sbuf", [128, 752], "bfloat16"),
-    "eo": ("sbuf", [128, 24], "uint16"),
+    "yy": ("sbuf", [128, 496], "bfloat16"),
     "wa": ("sbuf", [128, 272], "bfloat16"),
     "wb": ("sbuf", [128, 272], "bfloat16"),
-    "posr": ("sbuf", [128, 256], "bfloat16"),
+    "posr": ("sbuf", [128, X], "bfloat16"),
+    "rv": ("sbuf", [128, 8 * X], "bfloat16"),
     "dead": ("sbuf", [128, 512], "bfloat16"),
     "cum": ("sbuf", [128, 256], "bfloat16"),
     "junk": ("sbuf", [128, 768], "bfloat16"),
     "si": ("sbuf", [128, 4], "float32"),
-    "ofi": ("sbuf", [128, 8], "uint16"),
-    "ga": ("sbuf", [128, 64], "bfloat16"),
-    "pw": ("sbuf", [128, 6 * PWS + 8], "float32"),
+    "ofi": ("sbuf", [128, 4], "uint16"),
+    "ga": ("sbuf", [128, 96], "bfloat16"),
+    "pw": ("sbuf", [128, 9 * 48], "float16"),
     "px": ("sbuf", [128, 3 * 384], "float16"),
-    "cc": ("sbuf", [128, 2304], "bfloat16"),
-    "aa": ("sbuf", [128, 2304], "bfloat16"),
-    "bb": ("sbuf", [128, 2304], "bfloat16"),
-    "ofv": ("sbuf", [128, 3 * S], "uint16"),
-    "ofs": ("sbuf", [128, 2 * N1], "uint16"),
-    "gv": ("sbuf", [128, 3 * (S - N1) * 16], "bfloat16"),
-    "gs0": ("sbuf", [128, N0 * 16], "bfloat16"),
-    "gsr": ("sbuf", [128, N1 * 32], "bfloat16"),
-    "dq": ("sbuf", [128, 3 * GW], "bfloat16"),
-    "hit": ("sbuf", [128, 768], "bfloat16"),
-    "cn": ("sbuf", [128, 8], "float32"),
-    "lc": ("sbuf", [128, 40], "float32"),
-    "key": ("sbuf", [128, 8], "float32"),
+    "ofv": ("sbuf", [128, 2 * 3 * X], "uint16"),
+    "ofs": ("sbuf", [128, 2 * 2 * H], "uint16"),
+    "gv": ("sbuf", [128, 2 * 3 * H * 16], "bfloat16"),
+    "gs0": ("sbuf", [128, 2 * H * 16], "bfloat16"),
+    "gs1": ("sbuf", [128, 2 * H * 32], "bfloat16"),
+    "dq": ("sbuf", [128, 4 * 512], "bfloat16"),
+    "dt": ("sbuf", [128, 2 * 128], "bfloat16"),
+    "hit": ("sbuf", [128, 2 * 3 * X], "bfloat16"),
+    "cn": ("sbuf", [128, 16], "float32"),
+    "lc": ("sbuf", [128, 4 * 24], "float32"),
+    "key": ("sbuf", [128, 16], "float32"),
     "kd": ("sbuf", [128, 48], "float32"),
     "mn": ("sbuf", [128, 4], "float32"),
     "seld": ("sbuf", [128, 384], "bfloat16"),
-    "base": ("sbuf", [8, 256], "float32"),
-    "yas": ("sbuf", [8, 256], "float32"),
-    "ycs": ("sbuf", [128, 2], "float32"),
-    "da": ("psum", [128, 1024], "float32"),
-    "db": ("psum", [128, 1024], "float32"),
+    "base": ("sbuf", [4, 512], "float32"),
+    "yas": ("sbuf", [4, 512], "float32"),
+    "ycs": ("sbuf", [64, 8], "float32"),
+    "w0": ("psum", [128, 512], "float32"),
+    "w1": ("psum", [128, 512], "float32"),
+    "q0": ("psum", [128, 512], "float32"),
+    "q1": ("psum", [128, 512], "float32"),
+    "tb": ("psum", [128, 512], "float32"),
     "sc0": ("psum", [128, 512], "float32"),
     "sc1": ("psum", [128, 512], "float32"),
-    "sc2": ("psum", [128, 512], "float32"),
-    "scs": ("psum", [128, 512], "float32"),
+    "ch": ("psum", [128, 512], "float32"),
 }
-SEMAPHORES = ["cv", "cs", "cp", "cg", "llv", "lps", "lpf", "lth", "lt0", "lt1", "lrf", "oya", "oyc", "sent",
-              "ax01", "ax02", "ax11", "ax12", "ct0", "ct1"]
+SEMAPHORES = ["cv", "cs", "cp", "cg", "llv", "lps", "lpf", "lth", "lrf0", "lrf1", "oya0", "oya1", "oyc0", "oyc1", "sent",
+              "pw1", "pw2", "pw4", "pw5", "pw7", "pw8", "ct00", "ct01", "ct10", "ct11"]
 
 
 def deal_engines(topo, src, dsts):
@@ -121,7 +117,7 @@ def rank_program(g, core, T, topo):
     cnt = {"cv": 0, "cs": 0, "cp": 0, "cg": 0}
     final = {}
     waited = {q: {} for q in E}
-    W, R, X = {}, {}, {}
+    W, R, XB = {}, {}, {}
     pend = {q: ([], [], []) for q in E}
 
     def need(q, deps):
@@ -145,7 +141,7 @@ def rank_program(g, core, T, topo):
         if q == "p":
             deps = [d for d in deps if d[0] != own]
         for k in x:
-            deps.extend([d for d in X.get(k, {}).items() if d[0] != own])
+            deps.extend([d for d in XB.get(k, {}).items() if d[0] != own])
         return deps
 
     def note(tok, r, w, x):
@@ -155,7 +151,7 @@ def rank_program(g, core, T, topo):
             W[k] = tok
             R[k] = {}
         for k in x:
-            X.setdefault(k, {})[tok[0]] = tok[1]
+            XB.setdefault(k, {})[tok[0]] = tok[1]
 
     def op(q, fn, r=(), w=(), x=(), inc=True):
         need(q, deps_of(q, r, w, x))
@@ -169,11 +165,12 @@ def rank_program(g, core, T, topo):
             note((s_, cnt[s_]), p_[0], p_[1], p_[2])
             pend[q] = ([], [], [])
 
-    def dma(q, sem, out, in_, r=(), w=()):
+    def dmas(q, sem, pairs, r=(), w=()):
         need(q, deps_of(q, r, w, ()))
-        E[q].dma_start(out, in_).then_inc(T.sem[sem], 16)
-        note((sem, 16), r, w, ())
-        final[sem] = 16
+        for out, in_ in pairs:
+            E[q].dma_start(out, in_).then_inc(T.sem[sem], 16)
+        note((sem, 16 * len(pairs)), r, w, ())
+        final[sem] = 16 * len(pairs)
 
     V, A, P = g.vector, g.scalar, g.tensor
 
@@ -183,8 +180,14 @@ def rank_program(g, core, T, topo):
         else:
             op("v", lambda: V.tensor_scalar(out, in0, s1, s2, o0, o1), r, w, x)
 
+    def tt(out, in0, in1, o, r, w, x=()):
+        op("v", lambda: V.tensor_tensor(out, in0, in1, o), r, w, x)
+
     def ms(ap, c, w):
         op("v", lambda: V.memset(ap, c), (), w)
+
+    def cp(out, in_, r, w):
+        op("v", lambda: V.tensor_copy(out, in_), r, w)
 
     def mm(out, lhsT, rhs, start, stop, r, w, x, inc=None):
         op("p", lambda: P.matmul(out, lhsT, rhs, start, stop), r, w, x, stop if inc is None else inc)
@@ -192,9 +195,15 @@ def rank_program(g, core, T, topo):
     def act(out, in_, func, r, w, x=(), inc=True, **kw):
         op("s", lambda: A.activation(out, in_, func, **kw), r, w, x, inc)
 
-    def col(i, n=128):
-        return T.cols[0:n, i:i + 1]
-    N16G, TIE, B0, B1, TH2, N80G, THB, YB, CA, CB = range(10)
+    def lin(q, out, in_, scale, bias, r, w, x=()):
+        if q == "v":
+            ts(out, in_, scale, bias, ALU.mult, ALU.add, r, w, x)
+        else:
+            act(out, in_, AF.Identity, r, w, x, scale=scale, bias=bias)
+
+    def col(i, lo=0, hi=128):
+        return T.cols[lo:hi, i:i + 1]
+    R16, R8, R32, TIH, B0, B1, TH2, YB, CA, CB, WS, WO, HF, C1, C2, CI, CM, QU, EP = range(19)
 
     sent = [0]
 
@@ -210,375 +219,471 @@ def rank_program(g, core, T, topo):
         need("g", deps_of("g", r, (), ()))
         g.remote_dma_fused(trs, local_sem=T.sem.sent)
 
-    dma("y", "llv", T.lv8[:], T.lv[:], w=["lv8"])
-    dma("s", "lps", T.ps[:], T.pos[:], w=["ps"])
-    dma("y", "lpf", T.pfs[:], T.pf[:], w=["pfs"])
-    dma("s", "lt0", T.th16[0:8, :], T.th[:], w=["th16a"])
-    dma("y", "lt1", T.th16[8:16, :], T.th[:], w=["th16b"])
-    dma("s", "lth", T.ths[:, 0:1], T.th[:], w=["ths"])
-    dma("y", "lrf", T.rfs[:, 0:4096], T.rf[:], w=["rf"])
+    def arrivals(steps):
+        return {d: len(deal_engines(topo, cores[(rank - d) % N], [cores[(rank - d + e) % N] for e in steps])[core]) for d in steps}
+
+    RF = [T.rf0, T.rf1]
+    dmas("y", "llv", [(T.lv8[:], T.lv[:])], w=["lv8"])
+    dmas("s", "lps", [(T.ps[:], T.pos[:])], w=["ps"])
+    dmas("y", "lpf", [(T.pfs[64 * h:64 * h + 64, c:c + n], T.pf[64 * q:64 * q + 64, X * h:X * h + n])
+                      for q, c, n in ((0, 0, X), (1, X, X), (0, 2 * X, H)) for h in range(2)], w=["pfs"])
+    dmas("y", "lth", [(T.th16[8 * k:8 * k + 8, :], T.th[:]) for k in range(2)], w=["th16"])
+    for q in range(2):
+        dmas("y", "lrf%d" % q, [(RF[q][64 * h:64 * h + 64, 0:4096], T.rf[64 * q:64 * q + 64, :]) for h in range(2)], w=["rf%d" % q])
 
     flag = {"allow_small_or_imprecise_dtypes": True}
 
     def select(out, in_, pattern, cmp_, fill, base, r, w):
         op("g", lambda: g.affine_select(out, in_, pattern, cmp_, fill, base, 1), r, w)
 
-    ms(T.ones[:], BIG, ["ones"])
-    op("g", lambda: g.iota(T.ip[:], [[1, 128]], 0, -1, **flag), w=["ip"])
-    select(T.rep[:], T.ones[0:8, 0:128], [[-1, 8], [0, 16]], ALU.is_equal, 0.0, 0, ["ones"], ["rep"])
-    select(T.pa[:], T.ones[0:24, 0:128], [[-3, 8], [-1, 4], [0, 4]], ALU.is_equal, 0.0, 0, ["ones"], ["pa"])
-    select(T.pb[:], T.ones[0:24, 0:128], [[-3, 8], [0, 4], [-1, 4]], ALU.is_equal, 0.0, 0, ["ones"], ["pb"])
-    op("g", lambda: g.iota(T.t8[:], [[-3, 8]], 0, 1, **flag), w=["t8"])
-    op("g", lambda: g.iota(T.gr[:], [[1, 8], [0, 16]], 192, 0, **flag), w=["gr"])
-    op("g", lambda: g.iota(T.i3[:], [[16, 3], [64, 8]], 8, 1, **flag), w=["i3"])
-    select(T.gd[:], T.ones[0:16, 0:GW], [[0, GW // 8], [-1, 8]], ALU.is_equal, 0.0, 0, ["ones"], ["gd"])
+    def iota(out, pattern, base, cm, w):
+        op("g", lambda: g.iota(out, pattern, base, cm, **flag), w=w)
 
-    ms(T.pc[:], 0.0, ["pc0"])
-    ms(T.wa[:, 256:272], 0.0, ["waz"])
-    ms(T.wb[:, 256:272], 0.0, ["wbz"])
-    ts(T.g192[:, 0:1], T.ip[:, 0:1], -1.0 / 16, 191.53125, ALU.mult, ALU.add, ["ip"], ["g192"])
-    ts(T.idm[:], T.ip[:], 0.0, None, ALU.is_equal, None, ["ip"], ["idm"])
-    ts(col(N16G), T.g192[:, 0:1], -192.0, -16.0, ALU.add, ALU.mult, ["g192"], ["n16g"])
-    ts(col(N80G), T.g192[:, 0:1], -192.0, -80.0, ALU.add, ALU.mult, ["g192"], ["n80g"])
-    ts(col(TIE), T.ip[:, 0:1], col(N16G), -1.0 / 16, ALU.subtract, ALU.mult, ["ip", "n16g"], ["tie"])
-    ts(T.wa1[:], T.idm[:], 511.0 / 512, None, ALU.mult, None, ["idm"], ["wa1"])
-    ts(col(B0), col(TIE), -48.0, -0.5, ALU.mult, ALU.add, ["tie"], ["b0"])
-    ts(col(B1), col(TIE), -48.0, -1.5, ALU.mult, ALU.add, ["tie"], ["b1"])
-    ts(col(TH2), col(TIE), 48.0 * BIG, 2.5 * BIG, ALU.mult, ALU.add, ["tie"], ["th2"])
-    ms(T.zz[:], 0.0, ["zz0"])
-    ms(T.yy[:], 0.0, ["yy0"])
-    ms(T.rfs[:, 4096:4112], -1048576.0, ["rfz"])
-    for i in range(4):
-        ms(T.pw[:, PWS * i:PWS * i + 8], 0.0, ["pwz%d" % i])
-    for name, sc in (("wn", -2.0 ** -13), ("wa0", 31.0 / 32), ("wb1", 1.0 / 16), ("wb2", 1.0 / 256)):
-        act(T[name][:], T.idm[:], AF.Copy, ["idm"], [name], scale=sc)
-    YROW = [0, 16, 32, 64, 96]
-    for i, rb in enumerate(YROW):
-        act(T.yy[:, 128 * i + 112:128 * i + 128], T.idm[:, rb:rb + 16], AF.Copy, ["idm", "yy0"], ["yy%d" % rb], scale=8192.0)
+    def floor_p(i, d):
+        ts(T.fl[:, i:i + 1], T.pp[:, 0:1], 1.0 / d, 191.5 + 0.5 / d, ALU.mult, ALU.add, ["pp"], ["fl%d" % d])
 
-    ts(T.d8[:], T.lv8[:], -1.0, 1.0, ALU.mult, ALU.add, ["lv8"], ["d8"])
-    mm(T.da[:, 512:768], T.pa[:], T.ps[:], True, True, ["pa", "ps"], ["wap"], ["da1"])
-    mm(T.db[:, 0:256], T.pb[:], T.ps[:], True, True, ["pb", "ps"], ["wbp"], ["db0"])
-    mm(T.da[:, 0:256], T.rep[:], T.d8[:], True, True, ["rep", "d8"], ["drep"], ["da0"])
-    act(T.wa[:, 0:256], T.da[:, 512:768], AF.Copy, ["wap"], ["wa"], ["da1"], scale=1.0 / BIG)
-    act(T.wb[:, 0:256], T.db[:, 0:256], AF.Copy, ["wbp"], ["wb"], ["db0"], scale=1.0 / BIG)
-    TERMS = ((0, 1, 2, 1.0), (1, 2, 0, 1.0), (2, 0, 1, 1.0), (1, 0, 2, -1.0), (2, 1, 0, -1.0), (0, 2, 1, -1.0))
+    ms(T.one[:], 1.0, ["one"])
+    iota(T.pp[:], [[1536, 3]], 0, 1, ["pp"])
+    EQ, NE = ALU.is_equal, ALU.not_equal
     pck = ["pc%d" % i for i in range(6)]
-
-    def terms(lo, hi):
-        for i in range(lo, hi):
-            a, b, c, sg = TERMS[i]
-            ts(T.pc[:, 4 * a + b::16], T.t8[:], float(c), sg, ALU.is_equal, ALU.mult, ["t8", "pc0"], [pck[i]])
-    ts(T.pfm[:], T.pfs[:], 1.0 / 512, None, ALU.max, None, ["pfs"], ["pfm"])
-    terms(0, 1)
-
-    SCB = [T.sc0, T.sc1, T.sc2]
     pfxk = ["pfx%d" % m for m in range(16)]
     pfdk = ["pfd%d" % m for m in range(8)]
+    VAR = [(C1, ALU.add, 1.0), (C1, ALU.subtract, -1.0), (C2, ALU.add, -2.0 ** -4), (None, None, 2.0 ** -4),
+           (C2, ALU.add, -2.0 ** -8), (None, None, 2.0 ** -8), (C2, ALU.add, -2.0 ** -12), (None, None, 2.0 ** -12)]
+    STEPS = [(0, 0), (1, 0), (2, 0), (0, 1), (1, 1), (2, 1), (0, 2), (None, 0), (0, 3), (1, 4), (None, 1), (1, 5), (2, 6),
+             (None, 2), (2, 7)]
 
-    def one_round(t):
-        offs = [0, 2 * t + 1, 2 * t + 2]
-        dead = T.dead[:, 256 * t:256 * t + 256]
-        dk = "dead%d" % t
-        first = t == 0
-
-        if first:
-            op("v", lambda: V.tensor_tensor_scan(T.cum[:], T.ones[:, 0:256], T.da[:, 0:256], 0.0, ALU.add, ALU.subtract),
-               ["ones", "drep"], ["cum"], ["da0"])
+    def rows(d):
+        i = (16, 8, 64, 32).index(d)
+        floor_p(i, d)
+        if d == 64:
+            ts(col(CI), T.fl[:, 2:3], -4.0, T.fl[:, 0:1], ALU.mult, ALU.add, ["fl64", "fl16"], ["ci"])
+            ts(col(CM), col(R16), 7.5, 4.0, ALU.is_gt, ALU.mult, ["r16"], ["cm"])
+            ts(col(CM), col(CM), col(CI), None, ALU.add, None, ["cm", "ci"], ["cm"])
+        elif d == 32:
+            ts(col(R32), T.fl[:, 3:4], -192.0, -32.0, ALU.add, ALU.mult, ["fl32"], ["r32"])
+            ts(col(R32), col(R32), T.pp[:, 0:1], None, ALU.add, None, ["r32", "pp"], ["r32"])
         else:
-            op("v", lambda: V.tensor_tensor_scan(T.cum[:], T.ones[:, 0:256], dead, 0.0, ALU.add, ALU.subtract),
-               ["ones", dk], ["cum"])
-        ts(T.junk[:, 512:768], T.cum[:], col(TH2), None, ALU.is_le, None, ["cum", "th2"], ["le"])
-        for k in range(2):
-            act(T.junk[:, 256 * k:256 * k + 256], T.cum[:], AF.Sign, ["cum", "b%d" % k], ["si%d" % k, "j%d" % k],
-                bias=col(B0 + k), scale=1.0 / BIG, accum_out=T.si[:, k:k + 1])
-        op("v", lambda: V.tensor_reduce(T.si[:, 2:3], T.junk[:, 512:768], AX.X, ALU.add), ["le"], ["si2"])
-        if first:
-            terms(1, 6)
-            mm(T.db[:, 512:768], T.pc[:], T.ps[:], True, True, ["ps"] + pck, ["prp"], ["db1"])
-            act(T.posr[:], T.db[:, 512:768], AF.Copy, ["prp"], ["posr"], ["db1"])
-            act(dead, T.da[:, 0:256], AF.Copy, ["drep"], [dk], ["da0"])
-        op("v", lambda: V.tensor_copy(T.ofi[:, 2:3], T.si[:, 2:3]), ["si2"], ["ofi2"])
-        ts(T.ofi[:, 0:2], T.si[:, 0:2], -0.5, 128.0, ALU.mult, ALU.add, ["si0", "si1"], ["ofi0"])
-        ts(T.ofi[:, 3:5], T.si[:, 0:2], -0.5, 128.0, ALU.mult, ALU.add, ["si0", "si1"], ["ofi3"])
-        op("v", lambda: V.tensor_copy(T.ga[:], T.wa[:, 0:272].indirect(T.ofi[:, 0:4])),
-           ["wa", "waz", "ofi0", "ofi2", "ofi3"], ["ga"])
-        if first:
-            ts(T.eo[:], T.i3[:], col(N80G), 56.0, ALU.add, ALU.min, ["i3", "n80g"], ["eo"])
-        w0 = PWS * 3 * t
-        op("v", lambda: V.tensor_tensor(T.pw[:, w0 + 8:w0 + 56], T.wb[:, 0:272].indirect(T.ofi[:, 2:5]), T.ga[:, 16:64], ALU.mult),
-           ["wb", "wbz", "ofi0", "ofi2", "ofi3", "ga"], ["pw%d0" % t])
-        send([((rank + offs[s]) % N, T.pw[:, w0 + 8:w0 + 56], T.pw[:, w0 + PWS * s + 8:w0 + PWS * s + 56], "ax%d%d" % (t, s))
-              for s in (1, 2)], ["pw%d0" % t])
-        for s in (1, 2):
-            a = (rank - offs[s]) % N
-            n_ = len(deal_engines(topo, cores[a], [cores[(a + offs[1]) % N], cores[(a + offs[2]) % N]])[core])
-            W["pw%d%d" % (t, s)] = ("ax%d%d" % (t, s), n_)
-        if first:
-            select(T.gd[:], T.gd[:], [[0, GW // 8], [-1, 8]], ALU.not_equal, BIG, -8, ["gd"], ["gd"])
+            ts(col(R16 + i), T.fl[:, i:i + 1], -float(d), T.pp[:, 2 - i:3 - i], ALU.mult, ALU.add, ["fl%d" % d, "pp"], ["r%d" % d])
 
-        def expand(s):
-            i = 3 * t + s
-            op("v", lambda: V.tensor_copy(T.px[:, 384 * s:384 * s + 384], T.pw[:, PWS * i:PWS * i + 64].indirect(T.eo[:, 0:24])),
-               ["pw%d%d" % (t, s), "pwz%d" % i, "pwz%d" % (i + 1), "eo"], ["px%d" % s])
-
-        units = [(0, 0, U0, "da", 0, "sc1"), (0, U0, S, "db", 512 - 2 * (S - U0), "sc2"),
-                 (1, 0, S, "da", 0, "sc1"), (2, 0, S, "db", 0, "sc2")]
-        width = [u[2] - u[1] for u in units]
-        at = [3 * sum(width[:u]) for u in range(4)]
-
-        def banks(u):
-            return [units[u][3] + "0"] + ([units[u][3] + "1"] if units[u][4] + 3 * width[u] > 512 else [])
-
-        def dot(u):
-            s, lo, hi, buf, c0, _ = units[u]
+    def pick(k):
+        if k == "t":
+            iota(T.t16[:, 0:16], [[0, 2], [-3, 8]], 0, 1, ["t16c"])
+            iota(T.t16[:, 16:32], [[-3, 8], [0, 2]], 0, 1, ["t16a"])
+        elif k in "ab":
+            select(T["p" + k][:], T.one[0:24, 0:128], [[-3, 8], [0, 4], [-1, 4]], EQ, 0.0, 0, ["one"], ["p" + k])
+        elif k in "AB":
+            n = "p" + k.lower()
             for j in range(3):
-                c = c0 + j * (hi - lo)
-                mm(T[buf][:, c:c + hi - lo], T.px[:, 384 * s + 128 * j:384 * s + 128 * j + 128], T.posr[:, lo:hi],
-                   True, True, ["px%d" % s, "posr"], ["dot%d" % u], banks(u), inc=(j == 2))
+                ts(T[n][:, (4 if k == "A" else 0) + j::8], T.t16[:, 16:32], float((j + 1) % 3), None, EQ, None, ["t16a", n], [n + str(j)])
+            bank = "q%d" % "AB".index(k)
+            mm(T[bank][:, 0:256], T[n][:], T.ps[:], True, True, [n + "0", n + "1", n + "2", "ps"], [bank], [bank])
+        elif k == "z":
+            ms(T.pc[:], 0.0, ["pc0"])
+        elif k == "c":
+            for i in range(6):
+                s_, j = divmod(i, 3)
+                ts(T.pc[:, 4 * s_ + j::16], T.t16[:, 0:16], float((j + 2) % 3), 1.0 - 2 * s_, EQ, ALU.mult, ["t16c", "pc0"], [pck[i]])
+            mm(T.tb[:, 0:X], T.pc[:, 0:128], T.ps[:, 0:X], True, False, ["ps"] + pck, ["tb"], ["tb"])
+            mm(T.tb[:, 0:X], T.pc[:, 120:248], T.ps[:, X:S], False, True, ["ps"] + pck, ["tb"], ["tb"])
+        else:
+            act(T.posr[:], T.tb[:, 0:X], AF.Identity, ["tb", "hf"], ["posr"], ["tb"], bias=col(HF))
 
-        def round_c(u):
-            buf, c0 = units[u][3:5]
-            n_ = 3 * width[u]
-            act(T.cc[:, at[u]:at[u] + n_], T[buf][:, c0:c0 + n_], AF.Identity, ["dot%d" % u], ["c%d" % u], banks(u),
-                bias=786433.0, scale=2.0)
+    def columns(k):
+        if k == 0:
+            lin("s", col(B0), col(R16), -1.0, -0.5, ["r16"], ["b0"])
+            lin("s", col(B1), col(R16), -1.0, -16.5, ["r16"], ["b1"])
+            lin("s", col(TH2), col(R16), 1.0, 32.5, ["r16"], ["th2"])
+        elif k == 1:
+            ts(col(HF), col(R8), 7.0, 0.5, EQ, ALU.mult, ["r8"], ["hf"])
+            ts(col(C1), col(R8), 3.0, 1024.0, EQ, ALU.mult, ["r8"], ["c1"])
+            ts(col(C2), col(R8), 3.0, -30720.0, EQ, ALU.mult, ["r8"], ["c2"])
+        elif k == 2:
+            lin("s", col(WO), col(C1), 1.0 / 2048, col(HF), ["c1", "hf"], ["wo"])
+            lin("s", col(WS), col(WO), -2.0, 1.0, ["wo"], ["ws"])
+            lin("s", col(WO), col(WO), 2.0, 0.0, ["wo"], ["wo"])
+        elif k == 3:
+            for i, v in enumerate((-45.0 * 2 ** 30, -45.0 * 2 ** 26, -1.5 * 2 ** 27)):
+                ms(T.dc[:, 128 * i:128 * i + 128], v, ["dc%d" % i])
+        elif k == 4:
+            lin("s", col(EP), T.one[:, 0:1], 1.0 / 512, 0.0, ["one"], ["ep"])
+            lin("s", T.rf0[:, 4096:4112], T.one[:, 0:16], -2.0 ** 20, 0.0, ["one"], ["rfz0"])
+        elif k == 5:
+            lin("s", col(QU), T.one[:, 0:1], 1.0 / 64, 0.0, ["one"], ["qu"])
+            lin("s", T.rf1[:, 4096:4112], T.one[:, 0:16], -2.0 ** 20, 0.0, ["one"], ["rfz1"])
+        else:
+            lin("s", col(YB), col(R16), 1.0 / 32, 384.0, ["r16"], ["yb"])
+            lin("s", col(TIH), col(R16), 1.0 / 32, 0.0, ["r16"], ["tih"])
+            lin("s", T.wn[:], T.idm[:], -4.0, 0.0, ["idm"], ["wn"])
+            lin("s", T.dc[:, 384:392], T.one[0:1, 0:8], 768.0, 0.0, ["one"], ["dc3"])
 
-        def round_ab(u):
-            sl = slice(at[u], at[u] + 3 * width[u])
-            ts(T.aa[:, sl], T.cc[:, sl], 784384.0, -1.0, ALU.add, ALU.mult, ["c%d" % u], ["a%d" % u])
-            ts(T.bb[:, sl], T.cc[:, sl], -1.0 / 32, -759872.0, ALU.mult, ALU.add, ["c%d" % u], ["b_%d" % u])
+    def windows(k):
+        w_, key, bank = (T.wa, "wa", "q0") if k == 0 else (T.wb, "wb", "q1")
+        act(w_[:, 0:256], T[bank][:, 0:256], AF.Identity, [bank, "ws", "wo"], [key], [bank], scale=col(WS), bias=col(WO))
+        lin("s", w_[:, 256:272], T.one[:, 0:16], col(WO), 0.0, ["one", "wo"], [key + "z"])
 
-        def place(u):
-            s, lo, hi, _, _, bank = units[u]
-            n_ = width[u]
-            out = T[bank][:, 256:256 + n_]
-            part = lambda buf, j: buf[:, at[u] + n_ * j:at[u] + n_ * j + n_]
-            wk = ["w%d" % u]
-            mm(out, T.idm[:], T.dead[:, 256 * t + lo:256 * t + hi], True, False, ["idm", dk], wk, [bank])
+    def flags(k):
+        if k == 0:
+            ts(T.d8[:], T.lv8[:], -1.0, 193.0, ALU.mult, ALU.add, ["lv8"], ["d8"])
+            mm(T.ch[:, 0:256], T.rep[:], T.d8[:], True, True, ["rep", "d8"], ["ch"], ["ch"])
+        else:
+            act(T.dead[:, 0:256], T.ch[:, 0:256], AF.Copy, ["ch"], ["dead0"], ["ch"])
+
+    def masks(k):
+        if k < 3:
+            ts(T.mask[:, k::3], T.gr[:], 768.0, col(CM), ALU.subtract, EQ, ["gr", "cm"], ["mask%d" % k])
+        else:
+            lin("s", T.sel[:, 64:128], T.one[:, 0:64], 0.0, 0.0, ["one"], ["selz"])
+            for h in range(2):
+                lin("s", T.sel[:, 128 * h:128 * h + 64], T.mask[:, 192 * h:192 * h + 192:3], 2.0 ** 25, 0.0, ["mask0", "selz"], ["sel%d" % h])
+
+    def variants(q, lo, hi):
+        for k in range(lo, hi):
+            c_, o_, sc_ = VAR[k]
+            out = T.rv[:, X * k:X * k + X]
+            if c_ is None:
+                lin(q, out, T.posr[:], sc_, 0.0, ["posr"], ["rv%d" % k])
+            else:
+                ts(out, T.posr[:], col(c_), sc_, o_, ALU.mult, ["posr", "c1", "c2"], ["rv%d" % k])
+
+    def pfx(q, lo, hi):
+        for m in range(lo, hi):
+            lin(q, T.pfx[:, m::16], T.pfs[:, H:H + X], 1.0, col(EP), ["pfs", "ep"], [pfxk[m]])
+
+    def pfd(q, lo, hi):
+        for k in range(lo, hi):
+            lin(q, T.pfd[:, k::8], T.pfs[:, H + X:H + 2 * X], T.b8[:, k:k + 1], T.b8[:, 8 + k:9 + k], ["pfs", "b8", "b8e"], [pfdk[k]])
+
+    def tables(k):
+        if k == "rep":
+            select(T.rep[:], T.one[0:8, 0:128], [[-1, 8], [0, 16]], EQ, 0.0, 0, ["one"], ["rep"])
+        elif k == "gr":
+            iota(T.gr[:], [[1, 8], [0, 16]], 192, 0, ["gr"])
+        elif k == "idm":
+            select(T.idm[:], T.one[:, 0:128], [[-1, 128]], EQ, 0.0, 0, ["one"], ["idm"])
+        elif k == "thq":
+            select(T.thq[:], T.one[0:32, 0:128], [[-1, 8], [0, 16]], NE, 0.0, -16, ["one"], ["thq"])
+            select(T.thq[:], T.thq[:], [[-1, 4], [0, 32]], NE, 0.0, -24, ["thq"], ["thq"])
+        elif k == "gd":
+            select(T.gd[:], T.one[0:32, :], [[-4, 2], [0, 32], [-1, 4]], EQ, 0.0, 0, ["one"], ["gd"])
+            select(T.gd[:], T.gd[:], [[-4, 2], [0, 32], [-1, 4]], NE, 1.0, -8, ["gd"], ["gd"])
+        elif k[0:2] == "gd":
+            q, s = int(k[2]), int(k[3])
+            a = T.gd[:, 128 * q + 64 * s:128 * q + 64 * s + 64]
+            select(a, a, [[0, 2], [-1, 4], [0, 8]] if s else [[-1, 8], [0, 8]], NE, -32768.0, -16 - 8 * s, ["gd"], [k])
+        elif k[0:3] == "thm":
+            q = int(k[3])
+            a = T.thm[:, 128 * q:128 * q + 128]
+            select(a, T.one[0:16, 0:128], [[0, 2], [-1, 4], [0, 16]], EQ, 0.0, -4 * q, ["one"], [k])
+            select(a, a, [[0, 2], [-1, 4], [0, 16]], NE, 1.0, -8 - 4 * q, [k], [k])
+        elif k == "zz":
+            iota(T.zz[:], [[0, 144]], 0, 0, ["zz0"])
+            iota(T.jr[:], [[1, 32]], 0, 0, ["jr"])
+        elif k == "yy":
+            iota(T.yy[:], [[0, 496]], 0, 0, ["yyz"])
+        elif k == "o193":
+            iota(T.o193[:], [[0, 256]], 193, 0, ["o193"])
+        else:
+            select(T.id2[:], T.idm[:], [[-1, 128]], NE, 1.0, -64, ["idm"], ["id2"])
+            select(T.id2[:], T.id2[:], [[-1, 128]], NE, 1.0, 64, ["id2"], ["id2"])
+
+    def thresholds(k):
+        if k == 0:
+            ts(col(CA, 0, 16), T.pp[0:16, 0:1], 8.0, -1.0, ALU.is_ge, ALU.mult, ["pp"], ["ca"])
+            ts(T.thh[:], T.th16[:], -0.5, -1.0, ALU.add, ALU.mult, ["th16"], ["thh"])
+            ts(col(CB, 0, 16), col(CA, 0, 16), 2.0, 1.0, ALU.mult, ALU.add, ["ca"], ["cb"])
+            ts(T.thu[:, 0:16], T.th16[:], -0.5, col(CA, 0, 16), ALU.add, ALU.mult, ["th16", "ca"], ["thu0"])
+        elif k == 1:
+            lin("s", T.thu[:, 16:32], T.thh[:], col(CB, 0, 16), 0.0, ["thh", "cb"], ["thu1"])
+        elif k == 2:
+            tt(T.thq[0:16, 0:16], T.thu[:, 0:16], T.thu[:, 16:32], ALU.add, ["thu0", "thu1", "thq"], ["thq"])
+        elif k < 6:
+            n_ = 16 << (k - 3)
+            lin("s", T.thq[0:16, n_:2 * n_], T.thq[0:16, 0:n_], 1.0, 0.0, ["thq"], ["thq"])
+        else:
+            c = 128 * (k - 6)
+            tt(T.thx[:, c:c + 128], T.thq[0:16, :], T.thm[:, c:c + 128], ALU.mult, ["thq", "thm%d" % (k - 6)], ["thx%d" % (k - 6)])
+
+    def movers(k):
+        if k == 0:
+            ts(T.b8[:, 0:8], T.gr[:, 0::16], T.fl[:, 0:1], None, EQ, None, ["gr", "fl16"], ["b8"])
+            ts(T.b8[:, 8:16], T.gr[:, 0::16], T.fl[:, 0:1], 1.0 / 512, EQ, ALU.mult, ["gr", "fl16"], ["b8e"])
+        elif k == 1:
+            lin("s", T.zz[:, 15:143:16], T.b8[:, 0:8], 1.0, 0.0, ["b8", "zz0"], ["zz"])
+        elif k == 2:
+            ts(T.yy[:, 112:128], T.jr[:, 0:16], col(R16), None, EQ, None, ["jr", "r16", "yyz"], ["yy0"])
+        elif k == 3:
+            ts(T.yy[:, 240:256], T.jr[:, 0:16], col(R32), None, EQ, None, ["jr", "r32", "yyz"], ["yy1"])
+            ts(T.yy[:, 368:384], T.jr[:, 16:32], col(R32), None, EQ, None, ["jr", "r32", "yyz"], ["yy2"])
+        else:
+            ts(T.offb[:], T.gr[:], T.fl[:, 0:1], 4096.0, NE, ALU.mult, ["gr", "fl16"], ["offb"])
+            lin("s", T.m16[:], T.yy[:, 112:128], 1.0, 0.0, ["yy0"], ["m16"])
+            for h in range(2):
+                ts(T.blk[:, 64 * h:64 * h + 64], T.gr[:, 0:64], 768.0, col(CI), ALU.subtract, EQ, ["gr", "ci"], ["blk%d" % h])
+
+    def offsets(t):
+        return [0, 2 * t + 1, 2 * t + 2]
+
+    def lattices(t, q):
+        lo, hi = (0, 128) if q is None else (64 * q, 64 * q + 64)
+        i = 0 if t == 0 else 3 + 3 * q
+        offs = offsets(t)
+        cum = [T.w0[:, 0:256], T.w1[:, 0:256]] if t == 0 else [T.cum[lo:hi, :]] * 2
+        ck, cx = (["w0", "w1"], [["w0"], ["w1"]]) if t == 0 else (["cum", "cum"], [[], []])
+
+        def scan():
+            if t == 0:
+                op("v", lambda: V.tensor_tensor_scan(T.cum8[:], T.one[0:8, :], T.lv8[:], 0.0, ALU.mult, ALU.add), ["one", "lv8"], ["cum8"])
+                for k in range(2):
+                    mm(cum[k], T.rep[:], T.cum8[:], True, True, ["rep", "cum8"], [ck[k]], cx[k])
+            else:
+                op("v", lambda: V.tensor_tensor_scan(cum[0], T.o193[lo:hi, :], T.dead[lo:hi, 256:512], 0.0, ALU.add, ALU.subtract),
+                   ["o193", "dead1%d" % q], ["cum"])
+
+        def count(k):
+            if k < 2:
+                act(T.junk[lo:hi, 256 * k:256 * k + 256], cum[0], AF.Sign, [ck[0], "b%d" % k], ["si%d" % k, "j%d" % k], cx[0],
+                    bias=col(B0 + k, lo, hi), accum_out=T.si[lo:hi, k:k + 1])
+            elif k == 2:
+                ts(T.junk[lo:hi, 512:768], cum[1], col(TH2, lo, hi), None, ALU.is_le, None, [ck[1], "th2"], ["le"], cx[1])
+            else:
+                op("v", lambda: V.tensor_reduce(T.si[lo:hi, 2:3], T.junk[lo:hi, 512:768], AX.X, ALU.add), ["le"], ["si2"])
+
+        def lists(k):
+            if k == 0:
+                cp(T.ofi[lo:hi, 2:3], T.si[lo:hi, 2:3], ["si2"], ["ofi2"])
+            else:
+                ts(T.ofi[lo:hi, 0:2], T.si[lo:hi, 0:2], -0.5, 128.0, ALU.mult, ALU.add, ["si0", "si1"], ["ofi0"])
+
+        def seeds():
+            for k, n in enumerate(("wa", "wb")):
+                cp(T.ga[:, 48 * k:48 * k + 48], T[n][:, 0:272].indirect(T.ofi[:, 0:3]), [n, n + "z", "ofi0", "ofi2"], ["g" + n])
+
+        def terms():
+            keys = ["pw%d" % i + "abc"[j] for j in range(3)]
             for j in range(3):
-                mm(out, T.idm[:], part(T.cc, j), False, False, ["c%d" % u], wk, [bank])
-            for wt, j in (("wa0", 0), ("wa1", 1), ("idm", 2), ("wn", 2)):
-                mm(out, T[wt][:], part(T.aa, j), False, False, [wt, "a%d" % u], wk, [bank])
-            for wt, j in (("idm", 0), ("wb1", 1), ("wb2", 2)):
-                mm(out, T[wt][:], part(T.bb, j), False, j == 2, [wt, "b_%d" % u], wk, [bank])
-
-        def conv(u):
-            s, lo, hi, _, _, bank = units[u]
-            if s > 0:
-                ts(T.ofs[:, s - 1::2], T[bank][:, 256:256 + N1], WC, 4096.0, ALU.add, ALU.min, ["w%d" % u], ["ofs%d" % s], [bank])
-                lo = N1
-            c = 256 + lo - units[u][1]
-            ts(T.ofv[:, S * s + lo:S * s + hi], T[bank][:, c:c + hi - lo], WC, 4096.0, ALU.add, ALU.min,
-               ["w%d" % u], ["ofv%d" % u], [bank])
-
-        win = T.rfs[:, 0:4112]
-
-        def gather(s, lo, hi):
-            b = (S - N1) * 16 * s - 16 * N1
-            op("v", lambda: V.tensor_tensor(T.gv[:, b + 16 * lo:b + 16 * hi], win.indirect(T.ofv[:, S * s + lo:S * s + hi]),
-                                            T.pfx[:, 16 * (lo - N1):16 * (hi - N1)], ALU.mult),
-               ["rf", "rfz", "ofv%d" % (s + 1)] + pfxk, ["gv%d_%d" % (s, lo)])
-
-        def score(s, lo, hi, more=()):
-            b = (S - N1) * 16 * s - 16 * N1
-            for m in range(16):
-                mm(SCB[s][:, lo:hi], T.zz[:, 15 - m:143 - m], T.gv[:, b + 16 * lo + m:b + 16 * hi:16], m == 0, m == 15,
-                   ["zz"] + ["gv%d_%d" % (s, c) for c in [lo] + list(more)], ["sc%d_%d" % (s, lo)], ["sc%d" % s])
-
-        def sgather0(lo, hi):
-            act(T.gs0[:, 16 * lo:16 * hi], win.indirect(T.ofv[:, lo:hi]), AF.Copy,
-                ["rf", "rfz", "ofv0"] + (["ofv1"] if hi > U0 else []), ["gs0_%d" % lo])
-
-        def weigh0(lo, hi):
-            if lo == 0:
-                mm(T.scs[:, 0:8 * Q0], T.tht[:], T.gd[:, 0:8 * Q0], True, False, ["tht", "gd"], ["q0"], ["scs"])
-            for x in range(lo, hi):
-                q, xh = divmod(x, Q0)
-                mm(T.scs[32 * q:32 * q + 16, 8 * xh:8 * xh + 8], T.gs0[:, 16 * x:16 * x + 16], T.pfd[:, 8 * x:8 * x + 8],
-                   False, False, ["gs0_%d" % lo] + pfdk, ["q0"], ["scs"], inc=(x == hi - 1 and hi < N0))
-            if hi == N0:
-                mm(T.scs[:, 0:8 * Q0], T.tht[:], T.gd[:, 0:8 * Q0], False, True, ["tht", "gd"], ["q0"], ["scs"])
-
-        def sign0():
-            act(T.dq[:, 0:8 * Q0], T.scs[:, 0:8 * Q0], AF.Sign, ["q0"], ["dq0"], ["scs"])
-
-        def move0():
-            for q in range(4):
-                c = 128 * YROW.index(32 * q) + 112
-                for k in range(8):
-                    mm(T.sc0[:, Q0 * q:Q0 * q + Q0], T.yy[:, c - 16 * k:c - 16 * k + 128], T.dq[:, k:8 * Q0:8], k == 0, k == 7,
-                       ["dq0", "yy%d" % (32 * q)], ["sc0_q"], ["sc0"], inc=(q == 3 and k == 7))
-
-        def sgather1(lo, hi):
-            act(T.gsr[:, 32 * lo:32 * hi], win.indirect(T.ofs[:, 2 * lo:2 * hi]), AF.Copy,
-                ["rf", "rfz", "ofs1", "ofs2"], ["gsr_%d" % lo])
-
-        def weigh1(lo, hi):
-            h = lo // H1
-            if lo % H1 == 0:
-                mm(T.da[0:32, 512 * h:512 * h + 8 * H1], T.tht[:, 0:32], T.gd[:, 0:8 * H1], True, False,
-                   ["tht", "gd"], ["q1%d" % h], ["da%d" % h])
-            for x in range(lo, hi):
-                c = 512 * h + 8 * (x - H1 * h)
-                mm(T.da[0:32, c:c + 8], T.gsr[:, 32 * x:32 * x + 32], T.pfd[:, 8 * x:8 * x + 8],
-                   False, False, ["gsr_%d" % lo] + pfdk, ["q1%d" % h], ["da%d" % h], inc=(x == hi - 1 and hi % H1 > 0))
-            if hi % H1 == 0:
-                mm(T.da[0:32, 512 * h:512 * h + 8 * H1], T.tht[:, 0:32], T.gd[:, 0:8 * H1], False, True,
-                   ["tht", "gd"], ["q1%d" % h], ["da%d" % h])
-
-        def sign1(h):
-            act(T.dq[0:32, GW * (h + 1):GW * (h + 1) + 8 * H1], T.da[0:32, 512 * h:512 * h + 8 * H1], AF.Sign,
-                ["q1%d" % h], ["dq1%d" % h], ["da%d" % h])
-
-        def move1(h):
+                tt(T.pw[:, 48 * i + j:48 * i + 48:3], T.ga[:, (j + 1) % 3:48:3], T.ga[:, 48 + (j + 2) % 3:96:3], ALU.mult,
+                   ["gwa", "gwb"], [keys[j]] + (["pw%d" % i] if j == 2 else []))
+            send([((rank + offs[s]) % N, T.pw[:, 48 * i:48 * i + 48], T.pw[:, 48 * (i + s):48 * (i + s) + 48], "pw%d" % (i + s))
+                  for s in (1, 2)], keys)
             for s in (1, 2):
-                c = 128 * YROW.index(16 * (s - 1)) + 112
-                for k in range(8):
-                    mm(SCB[s][:, H1 * h:H1 * h + H1], T.yy[0:32, c - 16 * k:c - 16 * k + 128],
-                       T.dq[0:32, GW * (h + 1) + k:GW * (h + 1) + 8 * H1:8], k == 0, k == 7,
-                       ["dq1%d" % h, "yy%d" % (16 * (s - 1))], ["sc%d_q%d" % (s, h)], ["sc%d" % s])
+                W["pw%d" % (i + s)] = ("pw%d" % (i + s), arrivals(offs[1:])[offs[s]])
 
-        def hits(s, keys):
-            act(T.hit[:, 256 * s:256 * s + S], SCB[s][:, 0:S], AF.Sign, ["thb"] + ["sc%d_%s" % (s, k) for k in keys],
-                ["hit%d" % s, "cn%d_%d" % (t, s)], ["sc%d" % s], bias=col(THB), scale=-1.0,
-                accum_out=T.cn[:, 4 * t + s:4 * t + s + 1])
+        def repeat(s, bank):
+            c = 48 * (i + s)
+            for k in range(8):
+                mm(T[bank][lo:hi, 48 * k:48 * k + 48], T.idm[lo:hi, lo:hi], T.pw[lo:hi, c:c + 48], True, True,
+                   ["idm", "pw%d" % (i + s)], [bank], [bank], inc=(k == 7))
 
-        def pfx_v(ms_):
-            for m in ms_:
-                op("v", lambda: V.tensor_copy(T.pfx[:, m::16], T.pfm[:, N1:S]), ["pfm"], [pfxk[m]])
+        def expand(s, bank):
+            tt(T.px[lo:hi, 384 * s:384 * s + 384], T[bank][lo:hi, 0:384], T.mask[lo:hi, :], ALU.mult, [bank, "mask0", "mask1", "mask2"],
+               ["px%d%d" % (s, k) for k in range(2) if q in (None, k)], [bank])
 
-        def pfx_s(ms_):
-            for m in ms_:
-                act(T.pfx[:, m::16], T.pfm[:, N1:S], AF.Copy, ["pfm"], [pfxk[m]])
+        return {"scan": scan, "count": count, "lists": lists, "seeds": seeds, "terms": terms, "repeat": repeat, "expand": expand}
 
-        def pfd_v(ks):
-            for k in ks:
-                ts(T.pfd[:, k::8], T.pfm[:, 0:N0], T.b8[:, k:k + 1], None, ALU.mult, None, ["pfm", "b8"], [pfdk[k]])
+    def stream(t, q):
+        offs = offsets(t)
+        first = t == 0
+        lo64, hi64 = 64 * q, 64 * q + 64
+        dk = "dead0" if first else "dead1%d" % q
+        s0, v0 = (0, H) if q == 0 else (H, 0)
+        sc, scb = (T.sc0, T.sc1)[q], "sc%d" % q
+        win = RF[q][:, 0:4112]
+        rfk = ["rf%d" % q, "rfz%d" % q]
+        spans, units, slot = {}, {}, {}
 
-        expand(0)
-        dot(0); dot(1)
-        if first:
-            pfx_s(range(3))
-            for m in range(3, 13):
-                select(T.pfx[:, m::16], T.pfm[:, N1:S], [[0, S - N1]], ALU.is_ge, 0.0, 0, ["pfm"], [pfxk[m]])
-            ts(T.b8[:], T.gr[:, 0::16], T.g192[:, 0:1], None, ALU.is_equal, None, ["gr", "g192"], ["b8"])
-            ts(col(CA, 16), T.ip[0:16, 0:1], -8.0, -0.5 / BIG, ALU.is_le, ALU.mult, ["ip"], ["ca"])
-            ts(T.thh[:], T.th16[:], -0.5, -0.5 / BIG, ALU.add, ALU.mult, ["th16a", "th16b"], ["thh"])
-            ts(col(CB, 16), col(CA, 16), 4 * BIG, 1.0, ALU.mult, ALU.add, ["ca"], ["cb"])
-            ts(T.thu[:, 0:16], T.th16[:], -0.5, col(CA, 16), ALU.add, ALU.mult, ["th16a", "th16b", "ca"], ["thu0"])
-        round_c(0); round_c(1)
-        round_ab(0)
-        place(0)
-        if first:
-            ts(T.thu[:, 16:32], T.thh[:], col(CB, 16), None, ALU.mult, None, ["thh", "cb"], ["thu1"])
-            pfd_v(range(2))
-            op("v", lambda: V.tensor_tensor(T.tht[:, 0:16], T.thu[:, 0:16], T.thu[:, 16:32], ALU.add), ["thu0", "thu1"], ["tht"])
-        else:
-            mm(T.sc0[0:8, 256:512], T.wn[:, 0::16], T.dead[:, 0:256], True, False, ["wn", "dead0"], ["bp"], ["sc0"])
-            mm(T.sc0[0:8, 256:512], T.wn[:, 0::16], T.dead[:, 256:512], False, True, ["wn", "dead1"], ["bp"], ["sc0"])
-        conv(0)
-        sgather0(0, U0)
-        round_ab(1); place(1)
-        if first:
-            pfd_v(range(2, 8))
-            for n_ in (16, 32, 64):
-                act(T.tht[:, n_:2 * n_], T.tht[:, 0:n_], AF.Copy, ["tht"], ["tht"])
-        expand(1); dot(2); round_c(2)
-        conv(1)
-        expand(2); dot(3)
-        if first:
-            pfx_v(range(13, 16))
-            ts(T.zz[:, 15:143:16], T.gr[:, 0::16], T.g192[:, 0:1], None, ALU.is_equal, None, ["gr", "g192", "zz0"], ["zz"])
-            ts(col(THB), T.ths[:, 0:1], -0.5, None, ALU.add, None, ["ths"], ["thb"])
-        round_ab(2); place(2)
-        sgather0(U0, 128)
-        round_c(3)
-        gather(0, N0, S)
-        conv(2)
-        weigh0(0, U0)
-        weigh0(U0, 128)
-        round_ab(3); place(3)
-        sgather0(128, N0)
-        if not first:
-            act(T.base[:], T.sc0[0:8, 256:512], AF.Identity, ["bp"], ["base"], ["sc0"], bias=2.0, scale=0.25)
-        c0, c1, c2 = N1 + 32, N1 + 80, S - 64
-        h1, h2 = H1 // 2, H1 + H1 * 2 // 3
-        gather(1, N1, c0)
-        conv(3)
-        weigh0(128, N0)
-        score(0, N0, S)
-        sign0()
-        sgather1(0, h1)
-        gather(1, c0, c1)
-        move0()
-        sgather1(h1, H1)
-        weigh1(0, h1)
-        gather(1, c1, S)
-        score(1, N1, c1, [c0])
-        weigh1(h1, H1)
-        sgather1(H1, h2)
-        sign1(0)
-        gather(2, N1, c2)
-        score(1, c1, S)
-        weigh1(H1, h2)
-        sgather1(h2, N1)
-        move1(0)
-        weigh1(h2, N1)
-        hits(0, ["q", N0])
-        sign1(1)
-        gather(2, c2, S)
-        score(2, N1, c2)
-        move1(1)
-        hits(1, ["q0", "q1", N1, c1])
-        score(2, c2, S)
-        hits(2, ["q0", "q1", N1, c2])
-        if first:
-            ts(T.blk[:], T.gr[:], T.g192[:, 0:1], None, ALU.is_equal, None, ["gr", "g192"], ["blk"])
-            ts(T.offb[:], T.gr[:], T.g192[:, 0:1], 4096.0, ALU.not_equal, ALU.mult, ["gr", "g192"], ["offb"])
-            ts(T.m16[:], T.ip[:, 0:16], col(N16G), None, ALU.is_equal, None, ["ip", "n16g"], ["m16"])
-            ts(col(YB), col(TIE), 0.5, 384.0, ALU.mult, ALU.add, ["tie"], ["yb"])
-            for i in range(4, 7):
-                ms(T.pw[:, PWS * i:PWS * i + 8], 0.0, ["pwz%d" % i])
+        def made(name, lo, hi):
+            spans.setdefault(name, []).append((lo, hi))
+            return ["%s%d_%d" % (name, q, lo)]
 
-        deltas = sorted(set((offs[b] - offs[a]) % N for a in range(3) for b in range(3) if a != b))
-        cnk = ["cn%d_%d" % (t, i) for i in range(3)]
-        send([((rank - d) % N, T.cn[:, 4 * t:4 * t + 3], T.lc[:, 20 * t + 4 * i:20 * t + 4 * i + 3], "ct%d" % t)
-              for i, d in enumerate(deltas)], cnk)
-        tot = 0
-        for d in deltas:
-            b = (rank + d) % N
-            tot += len(deal_engines(topo, cores[b], [cores[(b - e) % N] for e in deltas])[core])
-        W["lc%d" % t] = ("ct%d" % t, tot)
-        ts(T.key[:, 0:3], T.cn[:, 4 * t:4 * t + 3], col(TIE), None, ALU.add, None, cnk + ["tie"], ["k0"])
-        M = 128 if first else 8
-        mm(T.db[0:M, 0:256], T.wn[:] if first else T.wn[:, 0::16], dead, True, False, ["wn", dk], ["die"], ["db0"])
-        for s in range(3):
-            c = [20 * t + 4 * deltas.index((offs[q] - offs[s]) % N) + q for q in range(3) if q != s]
-            ts(T.key[:, 4 + s:5 + s], T.key[:, s:s + 1], T.lc[:, c[0]:c[0] + 1], T.lc[:, c[1]:c[1] + 1], ALU.add, ALU.add,
-               ["lc%d" % t, "k0"], ["k1%d" % s])
-        for s in range(3):
-            ts(T.kd[:, 16 * s:16 * s + 16], T.m16[:], T.key[:, 4 + s:5 + s], None, ALU.mult, None, ["m16", "k1%d" % s], ["kd%d" % s])
-        mm(T.da[:, 0:48], T.blk[:], T.kd[:], True, True, ["blk", "kd0", "kd1", "kd2"], ["kp"], ["da0"])
-        ts(T.ycs[:, t:t + 1], T.key[:, 4:5], -0.5, col(YB), ALU.mult, ALU.add, ["k10", "yb"], ["yc%d" % t])
-        if not first:
-            dma("s", "oyc", T.yc[:], T.ycs[:], r=["yc0", "yc1"])
-        for s in range(3):
-            op("v", lambda: V.tensor_reduce(T.mn[:, s:s + 1], T.da[:, 16 * s:16 * s + 16], AX.X, ALU.min),
-               ["kp"], ["mn%d" % s], ["da0"])
-        for s in range(3):
-            ts(T.seld[:, 128 * s:128 * s + M], T.offb[:] if first else T.offb[:, 0::16], T.key[:, 4 + s:5 + s], T.mn[:, s:s + 1],
-               ALU.add, ALU.is_le, ["offb", "k1%d" % s, "mn%d" % s], ["seld%d" % s])
-            mm(T.db[0:M, 0:256], T.seld[:, 128 * s:128 * s + M], T.hit[:, 256 * s:256 * s + 256], False, s == 2,
-               ["seld%d" % s, "hit%d" % s], ["die"], ["db0"])
-        if first:
-            ts(T.dead[:, 256:512], T.db[:, 0:256], 2.5, BIG, ALU.is_lt, ALU.mult, ["die"], ["dead1"], ["db0"])
-        else:
-            op("v", lambda: V.tensor_tensor(T.yas[:], T.db[0:8, 0:256], T.base[:], ALU.max), ["die", "base"], ["yas"], ["db0"])
-            dma("y", "oya", T.ya[:], T.yas[:], r=["yas"])
+        def from_(name, lo, hi):
+            return ["%s%d_%d" % (name, q, a) for a, b in spans[name] if a < hi and lo < b]
 
-    one_round(0)
-    one_round(1)
+        def place(s, who, bank):
+            units[(s, who)] = bank
+            lo = s0 if who == "s" else v0
+            out = T[bank][:, 0:H]
+            for h in range(2):
+                c = 256 * t + X * h + lo
+                mm(out, T.sel[lo64:hi64, 64 * h:64 * h + 128], T.dead[lo64:hi64, c:c + H], h == 0, False, ["sel0", "sel1", dk], [bank], [bank])
+            for i, (j, k) in enumerate(STEPS):
+                if j is None:
+                    mm(out, T.dc[:, 128 * k:128 * k + 128], T.one[0:1, 0:H], False, False, ["dc%d" % k, "one"], [bank], [bank])
+                else:
+                    mm(out, T.px[lo64:hi64, 384 * s + j:384 * s + 384:3], T.rv[lo64:hi64, X * k + lo:X * k + lo + H],
+                       False, i == len(STEPS) - 1, ["px%d%d" % (s, q), "rv%d" % k], [bank], [bank])
+
+        def conv(s, who):
+            bank = units[(s, who)]
+            if who == "s" and s > 0:
+                b = 2 * H * q
+                out = T.ofs[:, b + s - 1:b + 2 * H:2]
+            else:
+                b = 3 * X * q + X * s + (s0 if who == "s" else v0)
+                out = T.ofv[:, b:b + H]
+            ts(out, T[bank][:, 0:H], 0.2, 4096.0, ALU.add, ALU.min, [bank], ["of%s%d%d" % (who, q, s)], [bank])
+
+        def vgather(s, lo=0, hi=H):
+            b = 16 * H * (3 * q + s)
+            c = 3 * X * q + X * s + v0
+            tt(T.gv[:, b + 16 * lo:b + 16 * hi], win.indirect(T.ofv[:, c + lo:c + hi]),
+               T.pfx[:, 16 * (H * q + lo):16 * (H * q + hi)], ALU.mult, rfk + ["ofv%d%d" % (q, s)] + pfxk, made("gv%d" % s, lo, hi))
+
+        def score(s):
+            b = 16 * H * (3 * q + s)
+            out = sc[:, X * s + v0:X * s + v0 + H]
+            key = made("sc%d" % s, v0, v0 + H)
+            mm(out, T.thx[:, 128 * q:128 * q + 128], T.one[0:16, 0:H], True, False, ["thx%d" % q, "one"], key, [scb])
+            for m in range(16):
+                mm(out, T.zz[:, 15 - m:143 - m], T.gv[:, b + m:b + 16 * H:16], False, m == 15, ["zz"] + from_("gv%d" % s, 0, H), key, [scb])
+
+        def tsum():
+            b = 16 * H * 3 * q
+            mm(T.tb[:, 0:128], T.one[0:16, 0:128], T.thx[:, 128 * q:128 * q + 128], True, False, ["thx%d" % q, "one"], ["tb"], ["tb"])
+            for m in range(16):
+                mm(T.tb[:, m:128:16], T.gv[:, b + m:b + 32 * H:16], T.zz[:, 15:143:16], False, m == 15,
+                   ["zz"] + from_("gv0", 0, H) + from_("gv1", 0, H), ["tb"], ["tb"])
+
+        def trelu():
+            act(T.dt[:, 128 * q:128 * q + 128], T.tb[:, 0:128], AF.Relu, ["tb"], ["dt%d" % q], ["tb"])
+
+        def tmove():
+            for s in range(2):
+                mm(sc[:, X * s + v0:X * s + v0 + H], T.dt[:, 128 * q:128 * q + 128], T.idm[:, H * s:H * s + H], True, True,
+                   ["dt%d" % q, "idm"], made("sc%d" % s, v0, v0 + H), [scb], inc=(s == 1))
+
+        def sgather(s, lo=0, hi=H):
+            if s == 0:
+                b, c = 16 * H * q, 3 * X * q + s0
+                act(T.gs0[:, b + 16 * lo:b + 16 * hi], win.indirect(T.ofv[:, c + lo:c + hi]), AF.Copy,
+                    rfk + ["ofs%d0" % q], made("gs0", lo, hi))
+            else:
+                b, c = 32 * H * q, 2 * H * q
+                act(T.gs1[:, b + 32 * lo:b + 32 * hi], win.indirect(T.ofs[:, c + 2 * lo:c + 2 * hi]), AF.Copy,
+                    rfk + ["ofs%d1" % q, "ofs%d2" % q], made("gs1", lo, hi))
+
+        def weigh(s, lo=0, hi=H):
+            bank = "q%d" % s
+            key = [bank]
+            r = from_("gs%d" % s, lo, hi) + pfdk
+            d = 8 * H * (1 - q)
+            gd = T.gd[:, 128 * q + 64 * s:128 * q + 64 * s + 64]
+            for x in range(lo, hi, 8):
+                mm(T[bank][:, 8 * x:8 * x + 64], T.thq[:], gd, True, False, ["thq", "gd%d%d" % (q, s)], key, [bank])
+                if s == 0:
+                    b = 16 * (H * q + x)
+                    mm(T[bank][:, 8 * x:8 * x + 64], T.gs0[:, b:b + 128], T.pfd[:, d + 8 * x:d + 8 * x + 64], False, True,
+                       r, key, [bank], inc=(x + 8 == hi))
+                else:
+                    for y in (x, x + 4):
+                        b = 32 * (H * q + y)
+                        mm(T[bank][:, 8 * y:8 * y + 32], T.gs1[:, b:b + 128], T.pfd[:, d + 8 * y:d + 8 * y + 32], False, y > x,
+                           r, key, [bank], inc=(y + 4 == hi))
+
+        def relu(s):
+            b = 512 * (2 * q + s)
+            act(T.dq[:, b:b + 512], T["q%d" % s][:, 0:512], AF.Relu, ["q%d" % s], ["dq%d%d" % (q, s)], ["q%d" % s])
+
+        def move(s):
+            b = 512 * (2 * q + min(s, 1))
+            key = made("sc%d" % s, s0, s0 + H)
+            for k in range(8):
+                c = 128 * s + 112 - 16 * k
+                mm(sc[:, X * s + s0:X * s + s0 + H], T.yy[:, c:c + 128], T.dq[:, b + k:b + 512:8], k == 0, k == 7,
+                   ["dq%d%d" % (q, min(s, 1)), "yy%d" % s], key, [scb])
+
+        cn0 = 8 * t + 4 * q
+        cnk = ["cn%d%d%d" % (t, q, s) for s in range(3)]
+
+        def hits(s):
+            b = X * (3 * q + s)
+            act(T.hit[:, b:b + X], sc[:, X * s:X * s + X], AF.Sign, from_("sc%d" % s, 0, X) + ["qu"],
+                ["hit%d%d" % (q, s), cnk[s]], [scb], bias=col(QU), scale=-1.0, accum_out=T.cn[:, cn0 + s:cn0 + s + 1])
+
+        def counts():
+            sem = "ct%d%d" % (t, q)
+            steps = sorted(set((offs[a] - offs[b]) % N for b in range(3) for a in range(3) if a != b))
+            c0 = 24 * (2 * t + q)
+            send([((rank + d) % N, T.cn[:, cn0:cn0 + 3], T.lc[:, c0 + 4 * i:c0 + 4 * i + 3], sem) for i, d in enumerate(steps)], cnk)
+            W[sem] = (sem, sum(arrivals(steps).values()))
+            for b in range(3):
+                for a in range(3):
+                    if a != b:
+                        slot[(a, b)] = c0 + 4 * steps.index((offs[a] - offs[b]) % N) + b
+
+        M, p0 = (64, lo64) if first else (4, 0)
+        die = sc[p0:p0 + M, 0:256]
+        k0 = 8 * q
+
+        def before():
+            lin("s", T.key[:, k0:k0 + 3], T.cn[:, cn0:cn0 + 3], 1.0, col(TIH), cnk + ["tih"], ["k0%d" % q])
+            wn = T.wn[lo64:hi64, lo64:hi64] if first else T.wn[lo64:hi64, lo64:hi64:16]
+            mm(die, wn, T.dead[lo64:hi64, 256 * t:256 * t + 256], True, False, ["wn", dk] + cnk, ["die%d" % q], [scb])
+            if not first:
+                mm(die, T.dc[:, 384:388], T.one[0:1, :], False, False, ["dc3", "one"], ["die%d" % q], [scb])
+
+        def keys():
+            for s in range(3):
+                c0, c1 = [slot[(s, b)] for b in range(3) if b != s]
+                ts(T.key[:, k0 + 4 + s:k0 + 5 + s], T.key[:, k0 + s:k0 + s + 1], T.lc[:, c0:c0 + 1], T.lc[:, c1:c1 + 1], ALU.add, ALU.add,
+                   ["ct%d%d" % (t, q), "k0%d" % q], ["k1%d%d" % (q, s)])
+            mm(T.ch[:, 64:67], T.id2[:], T.key[:, k0 + 4:k0 + 7], True, True, ["id2"] + ["k1%d%d" % (q, s) for s in range(3)], ["kt"], ["ch"])
+
+        def spread():
+            for s in range(3):
+                ts(T.kd[:, 16 * s:16 * s + 16], T.m16[:], T.key[:, k0 + 4 + s:k0 + 5 + s], None, ALU.mult, None,
+                   ["m16", "k1%d%d" % (q, s)], ["kd%d" % s])
+            mm(T.ch[:, 0:48], T.blk[:], T.kd[:], True, True, ["blk0", "blk1", "kd0", "kd1", "kd2"], ["kp"], ["ch"])
+
+        def winners():
+            for s in range(3):
+                op("v", lambda: V.tensor_reduce(T.mn[:, s:s + 1], T.ch[:, 16 * s:16 * s + 16], AX.X, ALU.min), ["kp"], ["mn%d" % s], ["ch"])
+            for s in range(3):
+                ts(T.seld[:, 128 * s:128 * s + 2 * M], T.offb[:] if first else T.offb[:, 0::16], T.ch[:, 64 + s:65 + s], T.mn[:, s:s + 1],
+                   ALU.add, ALU.is_le, ["offb", "kt", "mn%d" % s], ["seld%d" % s], ["ch"])
+                for h in range(2):
+                    b = X * (3 * q + s)
+                    mm(sc[p0:p0 + M, X * h:X * h + X], T.seld[:, 128 * s + M * h:128 * s + M * h + M], T.hit[:, b:b + X],
+                       False, (s, h) == (2, 1), ["seld%d" % s, "hit%d%d" % (q, s)], ["die%d" % q], [scb])
+
+        def report():
+            lin("s", T.ycs[:, 4 * q + t:4 * q + t + 1], T.ch[0:64, 64:65], -0.5, col(YB, 0, 64), ["kt", "yb"], ["yc%d%d" % (q, t)], ["ch"])
+            if not first:
+                dmas("s", "oyc%d" % q, [(T.yc[lo64:hi64, :], T.ycs[:, 4 * q:4 * q + 2])], r=["yc%d0" % q, "yc%d1" % q])
+
+        def deaths():
+            if first:
+                ts(T.dead[lo64:hi64, 256:512], die, 2.5 - 768, 192.0, ALU.is_lt, ALU.add, ["die%d" % q], ["dead1%d" % q], [scb])
+            else:
+                tt(T.yas[:, 256 * q:256 * q + 256], die, T.base[:, 256 * q:256 * q + 256], ALU.max, ["die%d" % q, "base%d" % q],
+                   ["yas%d" % q], [scb])
+                dmas("y", "oya%d" % q, [(T.ya[4 * q:4 * q + 4, :], T.yas[:, 256 * q:256 * q + 256])], r=["yas%d" % q])
+
+        def base():
+            for k in range(2):
+                mm(T.ch[0:4, 256:512], T.wn[lo64:hi64, lo64:hi64:16], T.dead[lo64:hi64, 256 * k:256 * k + 256], k == 0, k == 1,
+                   ["wn", "dead0", dk], ["bp"], ["ch"])
+            act(T.base[:, 256 * q:256 * q + 256], T.ch[0:4, 256:512], AF.Identity, ["bp"], ["base%d" % q], ["ch"], bias=386.0, scale=0.25)
+
+        return {"place": place, "conv": conv, "vg": vgather, "score": score, "tsum": tsum, "trelu": trelu, "tmove": tmove,
+                "sg": sgather, "weigh": weigh, "relu": relu, "move": move, "hits": hits, "counts": counts, "before": before,
+                "keys": keys, "spread": spread, "winners": winners, "report": report, "deaths": deaths, "base": base}
+
+    steps = {"K": {"rows": rows, "pick": pick, "columns": columns, "windows": windows, "flags": flags, "masks": masks, "rv": variants,
+                   "pfx": pfx, "pfd": pfd, "tables": tables, "thresholds": thresholds, "movers": movers},
+             "A": stream(0, 0), "B": stream(0, 1), "C": stream(1, 0), "D": stream(1, 1)}
+    steps["A"].update(lattices(0, None))
+    steps["C"].update(lattices(1, 0))
+    steps["D"].update(lattices(1, 1))
+    for word in ORDER.split():
+        name, *args = word[1:].split(".")
+        steps[word[0]][name](*[int(a) if a.isdigit() else a for a in args])
 
     final.update(cnt)
     final["sent"] = sent[0]
     need("g", list(final.items()))
+
+
+ORDER = """
+Kcolumns.4 Kpick.z Kpick.t Kpick.a Krows.8 Krows.16 Kpick.c Kcolumns.1 Ktables.rep Kpick.A Kcolumns.2 Kcolumns.0 Ascan Krows.64 Kpick.b Acount.2 Kpick.B Ktables.gr Acount.1 Acount.0 Kwindows.0 Kwindows.1 Acount.3 Ktables.idm Alists.1 Kmasks.0 Alists.0 Kflags.0 Aseeds Kmasks.2 Kpick.p Krv.v.6.7 Ktables.thq Aterms Kmasks.1 Kmasks.3 Kcolumns.3 Krv.v.0.3 Ktables.zz Krv.s.5.6 Krv.s.7.8 Ktables.yy Kcolumns.5 Kflags.1 Ktables.gd Arepeat.0.w0 Krv.v.4.5 Krv.s.3.4 Ktables.id2 Ktables.gd11 Kpfx.s.0.4 Aexpand.0.w0 Aplace.0.s.w1 Kthresholds.0 Kmovers.0 Krows.32 Aconv.0.s Kpfx.v.4.10 Aplace.0.v.w0 Bplace.0.s.w1 Kthresholds.1 Ktables.gd10 Aconv.0.v Bplace.0.v.w0 Kpfx.v.10.16 Kthresholds.2 Ktables.gd01 Ktables.gd00 Avg.0.0.32 Bconv.0.s Bconv.0.v Kmovers.3 Kpfd.v.4.8 Ktables.o193 Arepeat.1.w1 Arepeat.2.w0 Aexpand.1.w1 Aexpand.2.w0 Aplace.1.s.w1 Avg.0.32.64 Aconv.1.s Aplace.2.s.w0 Aconv.2.s Bvg.0.32.64 Aplace.1.v.w1 Kcolumns.6 Aconv.1.v Aplace.2.v.w0 Kmovers.2 Asg.0.0.64 Kthresholds.3 Kpfd.s.0.4 Kthresholds.4 Bsg.0.0.64 Kmovers.1 Kthresholds.5 Asg.1.0.32 Ktables.thm0 Asg.1.32.48 Aconv.2.v Aweigh.0.0.64 Avg.1.0.32 Ktables.thm1 Bplace.2.s.w0 Bplace.1.s.w1 Aweigh.1.0.32 Avg.1.32.64 Kthresholds.6 Bconv.1.s Bconv.2.s Avg.2.0.32 Bvg.0.0.32 Aweigh.1.32.48 Asg.1.48.64 Arelu.0 Aweigh.1.48.64 Bplace.2.v.w0 Atsum Amove.0 Bplace.1.v.w1 Avg.2.32.64 Bsg.1.32.48 Bsg.1.48.64 Kthresholds.7 Atrelu Arelu.1 Atmove Ascore.2 Amove.1 Amove.2 Bconv.1.v Bsg.1.16.32 Bconv.2.v Ahits.2 Ahits.0 Ahits.1 Bweigh.0.0.64 Bvg.1.0.32 Bvg.1.32.64 Bvg.2.0.32 Bsg.1.0.16 Btsum Abefore Btrelu Brelu.0 Acounts Bweigh.1.0.32 Bweigh.1.32.64 Bvg.2.32.64 Bmove.0 Kmovers.4 Bscore.2 Brelu.1 Akeys Aspread Btmove Bmove.1 Bhits.0 Awinners Adeaths Cscan Bhits.1 Bmove.2 Ccount.2 Ccount.3 Clists.0 Bhits.2 Bcounts Ccount.0 Ccount.1 Clists.1 Cseeds Cterms Bbefore Crepeat.0.w1 Cexpand.0.w1 Areport Cbase Cplace.0.s.w0 Cplace.0.v.w1 Bkeys Bspread Cconv.0.s Cconv.0.v Crepeat.2.w1 Bwinners Cexpand.2.w1 Csg.0.0.32 Breport Crepeat.1.w0 Bdeaths Cexpand.1.w0 Csg.0.32.64 Cplace.2.s.w1 Dscan Dcount.2 Cplace.1.s.w0 Dcount.0 Cconv.2.s Dcount.1 Dcount.3 Cconv.1.s Dlists.0 Dlists.1 Csg.1.32.48 Csg.1.16.32 Dseeds Dterms Cplace.1.v.w0 Cconv.1.v Csg.1.0.16 Csg.1.48.64 Cvg.1.0.32 Cplace.2.v.w1 Drepeat.0.w0 Dexpand.0.w0 Cconv.2.v Cvg.1.32.64 Cweigh.0.0.64 Dplace.0.v.w0 Crelu.0 Dconv.0.v Cvg.0.0.32 Dplace.0.s.w1 Dconv.0.s Dvg.0.0.32 Cweigh.1.0.32 Cweigh.1.32.64 Drepeat.2.w0 Dexpand.2.w0 Drepeat.1.w1 Dexpand.1.w1 Crelu.1 Cmove.1 Cvg.0.32.64 Cmove.0 Dplace.2.s.w0 Dplace.1.s.w1 Dsg.0.0.32 Dconv.2.s Dconv.1.s Dplace.2.v.w0 Dplace.1.v.w1 Ctsum Dsg.0.32.64 Cvg.2.0.32 Cvg.2.32.64 Dconv.1.v Dvg.0.32.64 Dconv.2.v Dvg.1.32.64 Dsg.1.32.48 Dsg.1.0.32 Cmove.2 Cscore.2 Ctrelu Dweigh.0.0.64 Dweigh.1.0.32 Dsg.1.48.64 Dweigh.1.32.48 Dweigh.1.48.64 Dvg.1.0.32 Chits.2 Drelu.0 Ctmove Drelu.1 Chits.1 Chits.0 Dtsum Dmove.0 Dtrelu Dmove.1 Dmove.2 Dtmove Dhits.1 Dhits.0 Dbase Ccounts Dvg.2.0.32 Dvg.2.32.64 Dscore.2 Dhits.2 Dcounts Dbefore Cbefore Ckeys Creport Cspread Cwinners Dkeys Dspread Dwinners Cdeaths Ddeaths Dreport
+"""

@@ -4,16 +4,18 @@ from concourse.mybir import AluOpType as ALU, AxisListType as AX, ActivationFunc
 N = 8
 S = 256
 X = 128
-H = 64
+SHARE = ((64, 64), (64, 72), (64, 72), (64, 64))
+HM = max(max(s) for s in SHARE)
+H = X - min(min(s) for s in SHARE)
 
 SCRATCH = {
     "lv8": ("sbuf", [8, 256], "int32"),
     "d8": ("sbuf", [8, 256], "bfloat16"),
     "cum8": ("sbuf", [8, 256], "bfloat16"),
-    "ps": ("sbuf", [24, 256], "bfloat16"),
-    "pfs": ("sbuf", [128, 320], "bfloat16"),
-    "pfx": ("sbuf", [128, 128 * 16], "bfloat16"),
-    "pfd": ("sbuf", [128, 128 * 8], "bfloat16"),
+    "ps": ("sbuf", [33, 272], "bfloat16"),
+    "pfs": ("sbuf", [128, 256 + HM], "bfloat16"),
+    "pfx": ("sbuf", [128, 2 * H * 16], "bfloat16"),
+    "pfd": ("sbuf", [128, 2 * HM * 8], "bfloat16"),
     "th16": ("sbuf", [16, 16], "int32"),
     "thu": ("sbuf", [16, 32], "float32"),
     "thh": ("sbuf", [16, 16], "bfloat16"),
@@ -27,15 +29,15 @@ SCRATCH = {
     "o193": ("sbuf", [128, 256], "bfloat16"),
     "dc": ("sbuf", [1, 4 * 128], "bfloat16"),
     "pp": ("sbuf", [128, 3], "float32"),
-    "jr": ("sbuf", [128, 32], "bfloat16"),
+    "jr": ("sbuf", [128, 16], "bfloat16"),
     "gr": ("sbuf", [128, 128], "bfloat16"),
-    "t16": ("sbuf", [24, 32], "float32"),
+    "t16": ("sbuf", [33, 32], "float32"),
     "rep": ("sbuf", [8, 128], "bfloat16"),
-    "pa": ("sbuf", [24, 128], "bfloat16"),
-    "pb": ("sbuf", [24, 128], "bfloat16"),
-    "pc": ("sbuf", [24, 256], "bfloat16"),
+    "pa": ("sbuf", [33, 128], "bfloat16"),
+    "pb": ("sbuf", [33, 128], "bfloat16"),
+    "pc": ("sbuf", [33, 256], "bfloat16"),
     "fl": ("sbuf", [128, 4], "bfloat16"),
-    "cols": ("sbuf", [128, 24], "float32"),
+    "cols": ("sbuf", [128, 16], "float32"),
     "b8": ("sbuf", [128, 16], "float32"),
     "idm": ("sbuf", [128, 128], "bfloat16"),
     "wn": ("sbuf", [128, 128], "bfloat16"),
@@ -44,7 +46,6 @@ SCRATCH = {
     "blk": ("sbuf", [128, 128], "float32"),
     "id2": ("sbuf", [128, 128], "float32"),
     "offb": ("sbuf", [128, 128], "bfloat16"),
-    "m16": ("sbuf", [128, 16], "float32"),
     "zz": ("sbuf", [128, 144], "bfloat16"),
     "yy": ("sbuf", [128, 496], "bfloat16"),
     "wa": ("sbuf", [128, 272], "bfloat16"),
@@ -53,57 +54,55 @@ SCRATCH = {
     "rv": ("sbuf", [128, 8 * X], "bfloat16"),
     "dead": ("sbuf", [128, 512], "bfloat16"),
     "cum": ("sbuf", [128, 256], "bfloat16"),
-    "junk": ("sbuf", [128, 768], "bfloat16"),
+    "junk": ("sbuf", [128, 770], "bfloat16"),
     "si": ("sbuf", [128, 4], "float32"),
     "ofi": ("sbuf", [128, 4], "uint16"),
     "ga": ("sbuf", [128, 96], "bfloat16"),
     "pw": ("sbuf", [128, 9 * 48], "float16"),
     "px": ("sbuf", [128, 3 * 384], "float16"),
     "ofv": ("sbuf", [128, 2 * 3 * X], "uint16"),
-    "ofs": ("sbuf", [128, 2 * 2 * H], "uint16"),
+    "ofs": ("sbuf", [128, 2 * 2 * HM], "uint16"),
     "gv": ("sbuf", [128, 2 * 3 * H * 16], "bfloat16"),
-    "gs0": ("sbuf", [128, 2 * H * 16], "bfloat16"),
-    "gs1": ("sbuf", [128, 2 * H * 32], "bfloat16"),
-    "dq": ("sbuf", [128, 4 * 512], "bfloat16"),
+    "gs0": ("sbuf", [128, 2 * HM * 16], "bfloat16"),
+    "gs1": ("sbuf", [128, 2 * HM * 32], "bfloat16"),
+    "dq": ("sbuf", [128, 4 * HM * 8], "bfloat16"),
     "dt": ("sbuf", [128, 2 * 128], "bfloat16"),
     "hit": ("sbuf", [128, 2 * 3 * X], "bfloat16"),
     "cn": ("sbuf", [128, 16], "float32"),
-    "lc": ("sbuf", [128, 4 * 24], "float32"),
+    "lc": ("sbuf", [128, 4 * 96], "float32"),
     "key": ("sbuf", [128, 16], "float32"),
     "kd": ("sbuf", [128, 48], "float32"),
     "mn": ("sbuf", [128, 4], "float32"),
     "seld": ("sbuf", [128, 384], "bfloat16"),
-    "base": ("sbuf", [4, 512], "float32"),
-    "yas": ("sbuf", [4, 512], "float32"),
+    "selw": ("sbuf", [128, 12], "bfloat16"),
+    "base": ("sbuf", [8, 256], "float32"),
+    "yas": ("sbuf", [8, 256], "float32"),
     "ycs": ("sbuf", [64, 8], "float32"),
     "w0": ("psum", [128, 512], "float32"),
     "w1": ("psum", [128, 512], "float32"),
-    "q0": ("psum", [128, 512], "float32"),
-    "q1": ("psum", [128, 512], "float32"),
+    "qq": ("psum", [128, 1024], "float32"),
     "tb": ("psum", [128, 512], "float32"),
     "sc0": ("psum", [128, 512], "float32"),
     "sc1": ("psum", [128, 512], "float32"),
     "ch": ("psum", [128, 512], "float32"),
 }
-SEMAPHORES = ["cv", "cs", "cp", "cg", "llv", "lps", "lpf", "lth", "lrf0", "lrf1", "oya0", "oya1", "oyc0", "oyc1", "sent",
+SEMAPHORES = ["cv", "cs", "cp", "cg", "llv", "lps", "lpf", "lth", "lrf0", "lrf1", "oya00", "oya01", "oya10", "oya11", "oyc0", "oyc1", "sent",
               "pw1", "pw2", "pw4", "pw5", "pw7", "pw8", "ct00", "ct01", "ct10", "ct11"]
 
 
 def deal_engines(topo, src, dsts):
-    off = [d for d in dsts if topo.chip(d) != topo.chip(src)]
-    on = [d for d in dsts if topo.chip(d) == topo.chip(src)]
-    pool = [e for e in topo.engines(src, off[0]) if all(e in topo.engines(src, d) for d in off)]
+    off = [i for i, d in enumerate(dsts) if topo.chip(d) != topo.chip(src)]
+    on = [i for i in range(len(dsts)) if i not in off]
+    far = [e for e in topo.engines(src, dsts[off[0]]) if all(e in topo.engines(src, dsts[i]) for i in off)]
+    near = [e for e in topo.engines(src, dsts[on[0]]) if e not in far] if on else []
     share = 1
-    while share * 2 * len(off) <= len(pool):
+    while share * 2 * len(off) <= len(far):
         share *= 2
-    out = {}
-    for d in off:
-        out[d], pool = pool[:share], pool[share:]
-    for d in on:
-        if len(pool) < share:
-            used = [e for v in out.values() for e in v]
-            pool = [e for e in topo.engines(src, d) if e not in used]
-        out[d], pool = pool[:share], pool[share:]
+    out = [None] * len(dsts)
+    for k, i in enumerate(off):
+        out[i] = far[k * share:(k + 1) * share]
+    for k, i in enumerate(on):
+        out[i] = near[k * share:(k + 1) * share]
     return out
 
 
@@ -203,30 +202,37 @@ def rank_program(g, core, T, topo):
 
     def col(i, lo=0, hi=128):
         return T.cols[lo:hi, i:i + 1]
-    R16, R8, R32, TIH, B0, B1, TH2, YB, CA, CB, WS, WO, HF, C1, C2, CI, CM, QU, EP = range(19)
+    R16, R8, R32, TIH, B0, B1, TH2, YB, CA, CB, C1, C2, CI, CM = range(14)
 
     sent = [0]
 
     def send(pieces, r):
         eng = deal_engines(topo, core, [cores[p_[0]] for p_ in pieces])
         trs = []
-        for d, src, dst, sem in pieces:
+        for (d, src, dst, sem), mine in zip(pieces, eng):
             rid, pid, _ = topo.addr(cores[d])
-            mask = sum(1 << e for e in eng[cores[d]])
-            trs.append(RemoteDMATransfer(dst_ids=[DstId(rid=rid, pnc=pid)], dma_engine_mask=mask,
+            trs.append(RemoteDMATransfer(dst_ids=[DstId(rid=rid, pnc=pid)], dma_engine_mask=sum(1 << e for e in mine),
                                          remote_sem=T.sem[sem], src=src, dst=dst))
-            sent[0] += len(eng[cores[d]])
+            sent[0] += len(mine)
         need("g", deps_of("g", r, (), ()))
         g.remote_dma_fused(trs, local_sem=T.sem.sent)
 
-    def arrivals(steps):
-        return {d: len(deal_engines(topo, cores[(rank - d) % N], [cores[(rank - d + e) % N] for e in steps])[core]) for d in steps}
+    def lands(b, dsts):
+        return sum(len(e) for d, e in zip(dsts, deal_engines(topo, cores[b], [cores[d] for d in dsts])) if d == rank)
+
+    def judges(t, b, o):
+        return [((b - o + a) % N, a) for a in (0, 2 * t + 1, 2 * t + 2) if a != o]
+
+    def offsets(t, b):
+        near = lambda o: any(topo.chip(cores[d]) == topo.chip(cores[b]) for d, _ in judges(t, b, o))
+        return [0] + sorted((2 * t + 1, 2 * t + 2), key=near)
 
     RF = [T.rf0, T.rf1]
     dmas("y", "llv", [(T.lv8[:], T.lv[:])], w=["lv8"])
-    dmas("s", "lps", [(T.ps[:], T.pos[:])], w=["ps"])
+    ms(T.ps[0:32, :], 0.0, ["ps"])
+    dmas("s", "lps", [(T.ps[0:24, 0:S], T.pos[:])], w=["ps"])
     dmas("y", "lpf", [(T.pfs[64 * h:64 * h + 64, c:c + n], T.pf[64 * q:64 * q + 64, X * h:X * h + n])
-                      for q, c, n in ((0, 0, X), (1, X, X), (0, 2 * X, H)) for h in range(2)], w=["pfs"])
+                      for q, c, n in ((0, 0, X), (1, X, X), (0, 2 * X, HM)) for h in range(2)], w=["pfs"])
     dmas("y", "lth", [(T.th16[8 * k:8 * k + 8, :], T.th[:]) for k in range(2)], w=["th16"])
     for q in range(2):
         dmas("y", "lrf%d" % q, [(RF[q][64 * h:64 * h + 64, 0:4096], T.rf[64 * q:64 * q + 64, :]) for h in range(2)], w=["rf%d" % q])
@@ -254,15 +260,12 @@ def rank_program(g, core, T, topo):
              (None, 2), (2, 7)]
 
     def rows(d):
-        i = (16, 8, 64, 32).index(d)
+        i = (16, 8, 64).index(d)
         floor_p(i, d)
         if d == 64:
             ts(col(CI), T.fl[:, 2:3], -4.0, T.fl[:, 0:1], ALU.mult, ALU.add, ["fl64", "fl16"], ["ci"])
             ts(col(CM), col(R16), 7.5, 4.0, ALU.is_gt, ALU.mult, ["r16"], ["cm"])
             ts(col(CM), col(CM), col(CI), None, ALU.add, None, ["cm", "ci"], ["cm"])
-        elif d == 32:
-            ts(col(R32), T.fl[:, 3:4], -192.0, -32.0, ALU.add, ALU.mult, ["fl32"], ["r32"])
-            ts(col(R32), col(R32), T.pp[:, 0:1], None, ALU.add, None, ["r32", "pp"], ["r32"])
         else:
             ts(col(R16 + i), T.fl[:, i:i + 1], -float(d), T.pp[:, 2 - i:3 - i], ALU.mult, ALU.add, ["fl%d" % d, "pp"], ["r%d" % d])
 
@@ -271,23 +274,26 @@ def rank_program(g, core, T, topo):
             iota(T.t16[:, 0:16], [[0, 2], [-3, 8]], 0, 1, ["t16c"])
             iota(T.t16[:, 16:32], [[-3, 8], [0, 2]], 0, 1, ["t16a"])
         elif k in "ab":
-            select(T["p" + k][:], T.one[0:24, 0:128], [[-3, 8], [0, 4], [-1, 4]], EQ, 0.0, 0, ["one"], ["p" + k])
+            select(T["p" + k][:], T.one[0:33, 0:128], [[-3, 8], [0, 4], [-1, 4]], EQ, 0.0, 0, ["one"], ["p" + k])
+            select(T["p" + k][:, 3::4], T.one[0:33, 0:32], [[0, 32]], EQ, 0.0, -32, ["one", "p" + k], ["p" + k + "3"])
         elif k in "AB":
             n = "p" + k.lower()
             for j in range(3):
                 ts(T[n][:, (4 if k == "A" else 0) + j::8], T.t16[:, 16:32], float((j + 1) % 3), None, EQ, None, ["t16a", n], [n + str(j)])
-            bank = "q%d" % "AB".index(k)
-            mm(T[bank][:, 0:256], T[n][:], T.ps[:], True, True, [n + "0", n + "1", n + "2", "ps"], [bank], [bank])
+            i = "AB".index(k)
+            bank = "q%d" % i
+            mm(T.qq[:, 512 * i:512 * i + 272], T[n][:], T.ps[:], True, True, [n + str(j) for j in range(4)] + ["ps", "ps1"], [bank], [bank])
         elif k == "z":
             ms(T.pc[:], 0.0, ["pc0"])
+            ms(T.pc[32:33, 7::16], 0.5, ["pc0"])
         elif k == "c":
             for i in range(6):
                 s_, j = divmod(i, 3)
                 ts(T.pc[:, 4 * s_ + j::16], T.t16[:, 0:16], float((j + 2) % 3), 1.0 - 2 * s_, EQ, ALU.mult, ["t16c", "pc0"], [pck[i]])
-            mm(T.tb[:, 0:X], T.pc[:, 0:128], T.ps[:, 0:X], True, False, ["ps"] + pck, ["tb"], ["tb"])
+            mm(T.tb[:, 0:X], T.pc[:, 0:128], T.ps[:, 0:X], True, False, ["ps", "ps1"] + pck, ["tb"], ["tb"])
             mm(T.tb[:, 0:X], T.pc[:, 120:248], T.ps[:, X:S], False, True, ["ps"] + pck, ["tb"], ["tb"])
         else:
-            act(T.posr[:], T.tb[:, 0:X], AF.Identity, ["tb", "hf"], ["posr"], ["tb"], bias=col(HF))
+            act(T.posr[:], T.tb[:, 0:X], AF.Copy, ["tb"], ["posr"], ["tb"])
 
     def columns(k):
         if k == 0:
@@ -295,32 +301,28 @@ def rank_program(g, core, T, topo):
             lin("s", col(B1), col(R16), -1.0, -16.5, ["r16"], ["b1"])
             lin("s", col(TH2), col(R16), 1.0, 32.5, ["r16"], ["th2"])
         elif k == 1:
-            ts(col(HF), col(R8), 7.0, 0.5, EQ, ALU.mult, ["r8"], ["hf"])
             ts(col(C1), col(R8), 3.0, 1024.0, EQ, ALU.mult, ["r8"], ["c1"])
             ts(col(C2), col(R8), 3.0, -30720.0, EQ, ALU.mult, ["r8"], ["c2"])
         elif k == 2:
-            lin("s", col(WO), col(C1), 1.0 / 2048, col(HF), ["c1", "hf"], ["wo"])
-            lin("s", col(WS), col(WO), -2.0, 1.0, ["wo"], ["ws"])
-            lin("s", col(WO), col(WO), 2.0, 0.0, ["wo"], ["wo"])
+            ms(T.ps[32:33, :], 1.0, ["ps1"])
         elif k == 3:
             for i, v in enumerate((-45.0 * 2 ** 30, -45.0 * 2 ** 26, -1.5 * 2 ** 27)):
                 ms(T.dc[:, 128 * i:128 * i + 128], v, ["dc%d" % i])
-        elif k == 4:
-            lin("s", col(EP), T.one[:, 0:1], 1.0 / 512, 0.0, ["one"], ["ep"])
-            lin("s", T.rf0[:, 4096:4112], T.one[:, 0:16], -2.0 ** 20, 0.0, ["one"], ["rfz0"])
-        elif k == 5:
-            lin("s", col(QU), T.one[:, 0:1], 1.0 / 64, 0.0, ["one"], ["qu"])
-            lin("s", T.rf1[:, 4096:4112], T.one[:, 0:16], -2.0 ** 20, 0.0, ["one"], ["rfz1"])
         else:
             lin("s", col(YB), col(R16), 1.0 / 32, 384.0, ["r16"], ["yb"])
             lin("s", col(TIH), col(R16), 1.0 / 32, 0.0, ["r16"], ["tih"])
             lin("s", T.wn[:], T.idm[:], -4.0, 0.0, ["idm"], ["wn"])
             lin("s", T.dc[:, 384:392], T.one[0:1, 0:8], 768.0, 0.0, ["one"], ["dc3"])
+            lin("s", T.selw[:], T.sel[:, 0::16], -2.0 ** -26, 0.0, ["sel0", "sel1"], ["selw"])
+
+    def fills(k):
+        out, value, key = ((T.yy[:, 0:248], 0.0, "yya"), (T.yy[:, 248:496], 0.0, "yyb"), (T.zz[:], 0.0, "zz0"),
+                           (T.rf0[:, 4096:4112], -2.0 ** 20, "rfz0"), (T.rf1[:, 4096:4112], -2.0 ** 20, "rfz1"), (T.o193[:], 193.0, "o193"))[k]
+        lin("s", out, T.one[:, 0:out.shape[1]], value, 0.0, ["one"], [key])
 
     def windows(k):
         w_, key, bank = (T.wa, "wa", "q0") if k == 0 else (T.wb, "wb", "q1")
-        act(w_[:, 0:256], T[bank][:, 0:256], AF.Identity, [bank, "ws", "wo"], [key], [bank], scale=col(WS), bias=col(WO))
-        lin("s", w_[:, 256:272], T.one[:, 0:16], col(WO), 0.0, ["one", "wo"], [key + "z"])
+        act(w_[:], T.qq[:, 512 * k:512 * k + 272], AF.Copy, [bank], [key], [bank])
 
     def flags(k):
         if k == 0:
@@ -348,11 +350,11 @@ def rank_program(g, core, T, topo):
 
     def pfx(q, lo, hi):
         for m in range(lo, hi):
-            lin(q, T.pfx[:, m::16], T.pfs[:, H:H + X], 1.0, col(EP), ["pfs", "ep"], [pfxk[m]])
+            lin(q, T.pfx[:, m::16], T.pfs[:, X - H:X + H], 1.0, 1.0 / 512, ["pfs"], [pfxk[m]])
 
     def pfd(q, lo, hi):
         for k in range(lo, hi):
-            lin(q, T.pfd[:, k::8], T.pfs[:, H + X:H + 2 * X], T.b8[:, k:k + 1], T.b8[:, 8 + k:9 + k], ["pfs", "b8", "b8e"], [pfdk[k]])
+            lin(q, T.pfd[:, k::8], T.pfs[:, S - HM:S + HM], T.b8[:, k:k + 1], T.b8[:, 8 + k:9 + k], ["pfs", "b8", "b8e"], [pfdk[k]])
 
     def tables(k):
         if k == "rep":
@@ -364,25 +366,23 @@ def rank_program(g, core, T, topo):
         elif k == "thq":
             select(T.thq[:], T.one[0:32, 0:128], [[-1, 8], [0, 16]], NE, 0.0, -16, ["one"], ["thq"])
             select(T.thq[:], T.thq[:], [[-1, 4], [0, 32]], NE, 0.0, -24, ["thq"], ["thq"])
-        elif k == "gd":
-            select(T.gd[:], T.one[0:32, :], [[-4, 2], [0, 32], [-1, 4]], EQ, 0.0, 0, ["one"], ["gd"])
-            select(T.gd[:], T.gd[:], [[-4, 2], [0, 32], [-1, 4]], NE, 1.0, -8, ["gd"], ["gd"])
         elif k[0:2] == "gd":
-            q, s = int(k[2]), int(k[3])
-            a = T.gd[:, 128 * q + 64 * s:128 * q + 64 * s + 64]
-            select(a, a, [[0, 2], [-1, 4], [0, 8]] if s else [[-1, 8], [0, 8]], NE, -32768.0, -16 - 8 * s, ["gd"], [k])
+            q = int(k[2])
+            a = T.gd[:, 128 * q:128 * q + 128]
+            select(a, T.one[0:32, 0:128], [[0, 32], [-1, 4]], EQ, 0.0, -4 * q, ["one"], [k])
+            select(a, a, [[0, 32], [-1, 4]], NE, 1.0, -8 - 4 * q, [k], [k])
+            for s in range(2):
+                a = T.gd[:, 128 * q + 64 * s:128 * q + 64 * s + 64]
+                select(a, a, [[0, 2], [-1, 4], [0, 8]] if s else [[-1, 8], [0, 8]], NE, -32768.0, -16 - 8 * s, [k], [k + str(s)])
         elif k[0:3] == "thm":
             q = int(k[3])
             a = T.thm[:, 128 * q:128 * q + 128]
             select(a, T.one[0:16, 0:128], [[0, 2], [-1, 4], [0, 16]], EQ, 0.0, -4 * q, ["one"], [k])
             select(a, a, [[0, 2], [-1, 4], [0, 16]], NE, 1.0, -8 - 4 * q, [k], [k])
-        elif k == "zz":
-            iota(T.zz[:], [[0, 144]], 0, 0, ["zz0"])
-            iota(T.jr[:], [[1, 32]], 0, 0, ["jr"])
-        elif k == "yy":
-            iota(T.yy[:], [[0, 496]], 0, 0, ["yyz"])
-        elif k == "o193":
-            iota(T.o193[:], [[0, 256]], 193, 0, ["o193"])
+        elif k == "jr":
+            iota(T.jr[:], [[1, 16]], 0, 0, ["jr"])
+        elif k == "end":
+            iota(T.junk[:, 768:770], [[0, 2]], 256, 0, ["end"])
         else:
             select(T.id2[:], T.idm[:], [[-1, 128]], NE, 1.0, -64, ["idm"], ["id2"])
             select(T.id2[:], T.id2[:], [[-1, 128]], NE, 1.0, 64, ["id2"], ["id2"])
@@ -411,23 +411,23 @@ def rank_program(g, core, T, topo):
         elif k == 1:
             lin("s", T.zz[:, 15:143:16], T.b8[:, 0:8], 1.0, 0.0, ["b8", "zz0"], ["zz"])
         elif k == 2:
-            ts(T.yy[:, 112:128], T.jr[:, 0:16], col(R16), None, EQ, None, ["jr", "r16", "yyz"], ["yy0"])
-        elif k == 3:
-            ts(T.yy[:, 240:256], T.jr[:, 0:16], col(R32), None, EQ, None, ["jr", "r32", "yyz"], ["yy1"])
-            ts(T.yy[:, 368:384], T.jr[:, 16:32], col(R32), None, EQ, None, ["jr", "r32", "yyz"], ["yy2"])
+            ts(T.yy[:, 112:128], T.jr[:], col(R16), None, EQ, None, ["jr", "r16", "yya"], ["yy0"])
+        elif k == 4:
+            floor_p(3, 32)
+            ts(col(R32), T.fl[:, 3:4], -2.0, T.fl[:, 0:1], ALU.mult, ALU.add, ["fl32", "fl16"], ["r32"])
+        elif k == 5:
+            for s in (1, 2):
+                ts(T.yy[:, 112 + 128 * s:128 + 128 * s], T.yy[:, 112:128], col(R32), s - 193.0, ALU.mult, EQ,
+                   ["yy0", "r32", "yya", "yyb"], ["yy%d" % s])
         else:
             ts(T.offb[:], T.gr[:], T.fl[:, 0:1], 4096.0, NE, ALU.mult, ["gr", "fl16"], ["offb"])
-            lin("s", T.m16[:], T.yy[:, 112:128], 1.0, 0.0, ["yy0"], ["m16"])
             for h in range(2):
                 ts(T.blk[:, 64 * h:64 * h + 64], T.gr[:, 0:64], 768.0, col(CI), ALU.subtract, EQ, ["gr", "ci"], ["blk%d" % h])
-
-    def offsets(t):
-        return [0, 2 * t + 1, 2 * t + 2]
 
     def lattices(t, q):
         lo, hi = (0, 128) if q is None else (64 * q, 64 * q + 64)
         i = 0 if t == 0 else 3 + 3 * q
-        offs = offsets(t)
+        far = (2 * t + 1, 2 * t + 2)
         cum = [T.w0[:, 0:256], T.w1[:, 0:256]] if t == 0 else [T.cum[lo:hi, :]] * 2
         ck, cx = (["w0", "w1"], [["w0"], ["w1"]]) if t == 0 else (["cum", "cum"], [[], []])
 
@@ -445,29 +445,31 @@ def rank_program(g, core, T, topo):
                 act(T.junk[lo:hi, 256 * k:256 * k + 256], cum[0], AF.Sign, [ck[0], "b%d" % k], ["si%d" % k, "j%d" % k], cx[0],
                     bias=col(B0 + k, lo, hi), accum_out=T.si[lo:hi, k:k + 1])
             elif k == 2:
-                ts(T.junk[lo:hi, 512:768], cum[1], col(TH2, lo, hi), None, ALU.is_le, None, [ck[1], "th2"], ["le"], cx[1])
+                ts(T.junk[lo:hi, 512:768], cum[1], col(TH2, lo, hi), -2.0, ALU.is_le, ALU.mult, [ck[1], "th2"], ["le"], cx[1])
             else:
-                op("v", lambda: V.tensor_reduce(T.si[lo:hi, 2:3], T.junk[lo:hi, 512:768], AX.X, ALU.add), ["le"], ["si2"])
+                op("v", lambda: V.tensor_reduce(T.si[lo:hi, 2:3], T.junk[lo:hi, 512:769], AX.X, ALU.add), ["le", "end"], ["si2"])
 
-        def lists(k):
+        def lists():
+            ts(T.ofi[lo:hi, 0:3], T.si[lo:hi, 0:3], -0.5, 128.0, ALU.mult, ALU.add, ["si0", "si1", "si2"], ["ofi"])
+
+        def seeds(k):
+            n = ("wa", "wb")[k]
+            a = (T.ga[:, 48 * k:48 * k + 48], T[n][:, 0:272].indirect(T.ofi[:, 0:3]))
             if k == 0:
-                cp(T.ofi[lo:hi, 2:3], T.si[lo:hi, 2:3], ["si2"], ["ofi2"])
+                cp(*a, [n, "ofi"], ["g" + n])
             else:
-                ts(T.ofi[lo:hi, 0:2], T.si[lo:hi, 0:2], -0.5, 128.0, ALU.mult, ALU.add, ["si0", "si1"], ["ofi0"])
-
-        def seeds():
-            for k, n in enumerate(("wa", "wb")):
-                cp(T.ga[:, 48 * k:48 * k + 48], T[n][:, 0:272].indirect(T.ofi[:, 0:3]), [n, n + "z", "ofi0", "ofi2"], ["g" + n])
+                act(*a, AF.Copy, [n, "ofi"], ["g" + n])
 
         def terms():
             keys = ["pw%d" % i + "abc"[j] for j in range(3)]
             for j in range(3):
                 tt(T.pw[:, 48 * i + j:48 * i + 48:3], T.ga[:, (j + 1) % 3:48:3], T.ga[:, 48 + (j + 2) % 3:96:3], ALU.mult,
                    ["gwa", "gwb"], [keys[j]] + (["pw%d" % i] if j == 2 else []))
-            send([((rank + offs[s]) % N, T.pw[:, 48 * i:48 * i + 48], T.pw[:, 48 * (i + s):48 * (i + s) + 48], "pw%d" % (i + s))
-                  for s in (1, 2)], keys)
+            there = [((rank + o) % N, i + offsets(t, (rank + o) % N).index(o)) for o in far]
+            send([(d, T.pw[:, 48 * i:48 * i + 48], T.pw[:, 48 * k:48 * k + 48], "pw%d" % k) for d, k in there], keys)
             for s in (1, 2):
-                W["pw%d" % (i + s)] = ("pw%d" % (i + s), arrivals(offs[1:])[offs[s]])
+                b = (rank - offsets(t, rank)[s]) % N
+                W["pw%d" % (i + s)] = ("pw%d" % (i + s), lands(b, [(b + o) % N for o in far]))
 
         def repeat(s, bank):
             c = 48 * (i + s)
@@ -482,15 +484,19 @@ def rank_program(g, core, T, topo):
         return {"scan": scan, "count": count, "lists": lists, "seeds": seeds, "terms": terms, "repeat": repeat, "expand": expand}
 
     def stream(t, q):
-        offs = offsets(t)
+        offs = offsets(t, rank)
         first = t == 0
         lo64, hi64 = 64 * q, 64 * q + 64
         dk = "dead0" if first else "dead1%d" % q
-        s0, v0 = (0, H) if q == 0 else (H, 0)
+        HS = SHARE[2 * t + q] + SHARE[2 * t + q][1:]
+        HV = [X - n for n in HS]
+        s0 = [0 if q == 0 else X - n for n in HS]
+        v0 = [n if q == 0 else 0 for n in HS]
+        gv0 = [16 * (3 * H * q + sum(HV[:s])) for s in range(3)]
         sc, scb = (T.sc0, T.sc1)[q], "sc%d" % q
         win = RF[q][:, 0:4112]
         rfk = ["rf%d" % q, "rfz%d" % q]
-        spans, units, slot = {}, {}, {}
+        spans, units = {}, {}
 
         def made(name, lo, hi):
             spans.setdefault(name, []).append((lo, hi))
@@ -501,95 +507,103 @@ def rank_program(g, core, T, topo):
 
         def place(s, who, bank):
             units[(s, who)] = bank
-            lo = s0 if who == "s" else v0
-            out = T[bank][:, 0:H]
+            lo, n = (s0[s], HS[s]) if who == "s" else (v0[s], HV[s])
+            out = T[bank][:, 0:n]
             for h in range(2):
                 c = 256 * t + X * h + lo
-                mm(out, T.sel[lo64:hi64, 64 * h:64 * h + 128], T.dead[lo64:hi64, c:c + H], h == 0, False, ["sel0", "sel1", dk], [bank], [bank])
+                mm(out, T.sel[lo64:hi64, 64 * h:64 * h + 128], T.dead[lo64:hi64, c:c + n], h == 0, False, ["sel0", "sel1", dk], [bank], [bank])
             for i, (j, k) in enumerate(STEPS):
                 if j is None:
-                    mm(out, T.dc[:, 128 * k:128 * k + 128], T.one[0:1, 0:H], False, False, ["dc%d" % k, "one"], [bank], [bank])
+                    mm(out, T.dc[:, 128 * k:128 * k + 128], T.one[0:1, 0:n], False, False, ["dc%d" % k, "one"], [bank], [bank])
                 else:
-                    mm(out, T.px[lo64:hi64, 384 * s + j:384 * s + 384:3], T.rv[lo64:hi64, X * k + lo:X * k + lo + H],
+                    mm(out, T.px[lo64:hi64, 384 * s + j:384 * s + 384:3], T.rv[lo64:hi64, X * k + lo:X * k + lo + n],
                        False, i == len(STEPS) - 1, ["px%d%d" % (s, q), "rv%d" % k], [bank], [bank])
 
         def conv(s, who):
             bank = units[(s, who)]
+            lo, n = (s0[s], HS[s]) if who == "s" else (v0[s], HV[s])
             if who == "s" and s > 0:
-                b = 2 * H * q
-                out = T.ofs[:, b + s - 1:b + 2 * H:2]
+                out = T.ofs[:, 2 * HM * q + s - 1:2 * HM * q + 2 * n:2]
             else:
-                b = 3 * X * q + X * s + (s0 if who == "s" else v0)
-                out = T.ofv[:, b:b + H]
-            ts(out, T[bank][:, 0:H], 0.2, 4096.0, ALU.add, ALU.min, [bank], ["of%s%d%d" % (who, q, s)], [bank])
+                b = 3 * X * q + X * s + lo
+                out = T.ofv[:, b:b + n]
+            ts(out, T[bank][:, 0:n], 0.2, 4096.0, ALU.add, ALU.min, [bank], ["of%s%d%d" % (who, q, s)], [bank])
 
-        def vgather(s, lo=0, hi=H):
-            b = 16 * H * (3 * q + s)
-            c = 3 * X * q + X * s + v0
-            tt(T.gv[:, b + 16 * lo:b + 16 * hi], win.indirect(T.ofv[:, c + lo:c + hi]),
-               T.pfx[:, 16 * (H * q + lo):16 * (H * q + hi)], ALU.mult, rfk + ["ofv%d%d" % (q, s)] + pfxk, made("gv%d" % s, lo, hi))
+        def vgather(s, lo, hi):
+            c = 3 * X * q + X * s + v0[s]
+            f = 16 * (X * q + v0[s] - X + H)
+            tt(T.gv[:, gv0[s] + 16 * lo:gv0[s] + 16 * hi], win.indirect(T.ofv[:, c + lo:c + hi]), T.pfx[:, f + 16 * lo:f + 16 * hi],
+               ALU.mult, rfk + ["ofv%d%d" % (q, s)] + pfxk, made("gv%d" % s, lo, hi))
 
         def score(s):
-            b = 16 * H * (3 * q + s)
-            out = sc[:, X * s + v0:X * s + v0 + H]
-            key = made("sc%d" % s, v0, v0 + H)
-            mm(out, T.thx[:, 128 * q:128 * q + 128], T.one[0:16, 0:H], True, False, ["thx%d" % q, "one"], key, [scb])
+            out = sc[:, X * s + v0[s]:X * s + v0[s] + HV[s]]
+            key = made("sc%d" % s, v0[s], v0[s] + HV[s])
+            mm(out, T.thx[:, 128 * q:128 * q + 128], T.one[0:16, 0:HV[s]], True, False, ["thx%d" % q, "one"], key, [scb])
             for m in range(16):
-                mm(out, T.zz[:, 15 - m:143 - m], T.gv[:, b + m:b + 16 * H:16], False, m == 15, ["zz"] + from_("gv%d" % s, 0, H), key, [scb])
+                mm(out, T.zz[:, 15 - m:143 - m], T.gv[:, gv0[s] + m:gv0[s] + 16 * HV[s]:16], False, m == 15,
+                   ["zz"] + from_("gv%d" % s, 0, X), key, [scb])
+
+        nt = HV[0] + HV[1]
 
         def tsum():
-            b = 16 * H * 3 * q
-            mm(T.tb[:, 0:128], T.one[0:16, 0:128], T.thx[:, 128 * q:128 * q + 128], True, False, ["thx%d" % q, "one"], ["tb"], ["tb"])
+            mm(T.tb[0:nt, 0:128], T.one[0:16, 0:nt], T.thx[:, 128 * q:128 * q + 128], True, False, ["thx%d" % q, "one"], ["tb"], ["tb"])
             for m in range(16):
-                mm(T.tb[:, m:128:16], T.gv[:, b + m:b + 32 * H:16], T.zz[:, 15:143:16], False, m == 15,
-                   ["zz"] + from_("gv0", 0, H) + from_("gv1", 0, H), ["tb"], ["tb"])
+                mm(T.tb[0:nt, m:128:16], T.gv[:, gv0[0] + m:gv0[2]:16], T.zz[:, 15:143:16], False, m == 15,
+                   ["zz"] + from_("gv0", 0, X) + from_("gv1", 0, X), ["tb"], ["tb"])
 
         def trelu():
-            act(T.dt[:, 128 * q:128 * q + 128], T.tb[:, 0:128], AF.Relu, ["tb"], ["dt%d" % q], ["tb"])
+            act(T.dt[0:nt, 128 * q:128 * q + 128], T.tb[0:nt, 0:128], AF.Relu, ["tb"], ["dt%d" % q], ["tb"])
 
         def tmove():
             for s in range(2):
-                mm(sc[:, X * s + v0:X * s + v0 + H], T.dt[:, 128 * q:128 * q + 128], T.idm[:, H * s:H * s + H], True, True,
-                   ["dt%d" % q, "idm"], made("sc%d" % s, v0, v0 + H), [scb], inc=(s == 1))
+                mm(sc[:, X * s + v0[s]:X * s + v0[s] + HV[s]], T.dt[0:nt, 128 * q:128 * q + 128], T.idm[0:nt, HV[0] * s:HV[0] * s + HV[s]],
+                   True, True, ["dt%d" % q, "idm"], made("sc%d" % s, v0[s], v0[s] + HV[s]), [scb], inc=(s == 1))
 
-        def sgather(s, lo=0, hi=H):
+        def sgather(s, lo, hi):
             if s == 0:
-                b, c = 16 * H * q, 3 * X * q + s0
+                b, c = 16 * HM * q, 3 * X * q + s0[0]
                 act(T.gs0[:, b + 16 * lo:b + 16 * hi], win.indirect(T.ofv[:, c + lo:c + hi]), AF.Copy,
                     rfk + ["ofs%d0" % q], made("gs0", lo, hi))
             else:
-                b, c = 32 * H * q, 2 * H * q
+                b, c = 32 * HM * q, 2 * HM * q
                 act(T.gs1[:, b + 32 * lo:b + 32 * hi], win.indirect(T.ofs[:, c + 2 * lo:c + 2 * hi]), AF.Copy,
                     rfk + ["ofs%d1" % q, "ofs%d2" % q], made("gs1", lo, hi))
 
-        def weigh(s, lo=0, hi=H):
-            bank = "q%d" % s
-            key = [bank]
+        q0 = [0, 1024 - 8 * HS[1]]
+
+        def qbanks(s, lo, hi):
+            return ["q%d" % k for k in range((q0[s] + 8 * lo) // 512, (q0[s] + 8 * hi - 1) // 512 + 1)]
+
+        def weigh(s, lo, hi):
+            banks = qbanks(s, lo, hi)
             r = from_("gs%d" % s, lo, hi) + pfdk
-            d = 8 * H * (1 - q)
+            d = 8 * (HM if q == 0 else HM - HS[s])
             gd = T.gd[:, 128 * q + 64 * s:128 * q + 64 * s + 64]
             for x in range(lo, hi, 8):
-                mm(T[bank][:, 8 * x:8 * x + 64], T.thq[:], gd, True, False, ["thq", "gd%d%d" % (q, s)], key, [bank])
+                c = q0[s] + 8 * x
+                mm(T.qq[:, c:c + 64], T.thq[:], gd, True, False, ["thq", "gd%d%d" % (q, s)], banks, banks)
                 if s == 0:
-                    b = 16 * (H * q + x)
-                    mm(T[bank][:, 8 * x:8 * x + 64], T.gs0[:, b:b + 128], T.pfd[:, d + 8 * x:d + 8 * x + 64], False, True,
-                       r, key, [bank], inc=(x + 8 == hi))
+                    b = 16 * (HM * q + x)
+                    mm(T.qq[:, c:c + 64], T.gs0[:, b:b + 128], T.pfd[:, d + 8 * x:d + 8 * x + 64], False, True,
+                       r, banks, banks, inc=(x + 8 == hi))
                 else:
-                    for y in (x, x + 4):
-                        b = 32 * (H * q + y)
-                        mm(T[bank][:, 8 * y:8 * y + 32], T.gs1[:, b:b + 128], T.pfd[:, d + 8 * y:d + 8 * y + 32], False, y > x,
-                           r, key, [bank], inc=(y + 4 == hi))
+                    for y in (0, 4):
+                        b = 32 * (HM * q + x + y)
+                        mm(T.qq[:, c + 8 * y:c + 8 * y + 32], T.gs1[:, b:b + 128], T.pfd[:, d + 8 * (x + y):d + 8 * (x + y) + 32],
+                           False, y > 0, r, banks, banks, inc=(x + y + 4 == hi))
+
+        dq0 = [16 * HM * q, 16 * HM * q + 8 * HM]
 
         def relu(s):
-            b = 512 * (2 * q + s)
-            act(T.dq[:, b:b + 512], T["q%d" % s][:, 0:512], AF.Relu, ["q%d" % s], ["dq%d%d" % (q, s)], ["q%d" % s])
+            banks = qbanks(s, 0, HS[s])
+            act(T.dq[:, dq0[s]:dq0[s] + 8 * HS[s]], T.qq[:, q0[s]:q0[s] + 8 * HS[s]], AF.Relu, banks, ["dq%d%d" % (q, s)], banks)
 
         def move(s):
-            b = 512 * (2 * q + min(s, 1))
-            key = made("sc%d" % s, s0, s0 + H)
+            b = dq0[min(s, 1)]
+            key = made("sc%d" % s, s0[s], s0[s] + HS[s])
             for k in range(8):
                 c = 128 * s + 112 - 16 * k
-                mm(sc[:, X * s + s0:X * s + s0 + H], T.yy[:, c:c + 128], T.dq[:, b + k:b + 512:8], k == 0, k == 7,
+                mm(sc[:, X * s + s0[s]:X * s + s0[s] + HS[s]], T.yy[:, c:c + 128], T.dq[:, b + k:b + 8 * HS[s]:8], k == 0, k == 7,
                    ["dq%d%d" % (q, min(s, 1)), "yy%d" % s], key, [scb])
 
         cn0 = 8 * t + 4 * q
@@ -597,54 +611,65 @@ def rank_program(g, core, T, topo):
 
         def hits(s):
             b = X * (3 * q + s)
-            act(T.hit[:, b:b + X], sc[:, X * s:X * s + X], AF.Sign, from_("sc%d" % s, 0, X) + ["qu"],
-                ["hit%d%d" % (q, s), cnk[s]], [scb], bias=col(QU), scale=-1.0, accum_out=T.cn[:, cn0 + s:cn0 + s + 1])
+            act(T.hit[:, b:b + X], sc[:, X * s:X * s + X], AF.Sign, from_("sc%d" % s, 0, X),
+                ["hit%d%d" % (q, s), cnk[s]], [scb], bias=1.0 / 64, scale=-1.0, accum_out=T.cn[:, cn0 + s:cn0 + s + 1])
 
-        def counts():
-            sem = "ct%d%d" % (t, q)
-            steps = sorted(set((offs[a] - offs[b]) % N for b in range(3) for a in range(3) if a != b))
-            c0 = 24 * (2 * t + q)
-            send([((rank + d) % N, T.cn[:, cn0:cn0 + 3], T.lc[:, c0 + 4 * i:c0 + 4 * i + 3], sem) for i, d in enumerate(steps)], cnk)
-            W[sem] = (sem, sum(arrivals(steps).values()))
-            for b in range(3):
-                for a in range(3):
-                    if a != b:
-                        slot[(a, b)] = c0 + 4 * steps.index((offs[a] - offs[b]) % N) + b
+        def counts(lo, hi):
+            to = lambda b: sorted(set(d for s in range(lo, hi) for d, _ in judges(t, b, offsets(t, b)[s])))
+            call.update({s: lo for s in range(lo, hi)})
+            send([(d, T.cn[:, cn0 + lo:cn0 + hi], T.lc[:, slot(rank, d, lo):slot(rank, d, lo) + hi - lo], ct) for d in to(rank)], cnk[lo:hi])
+            got[0] += sum(lands(b, to(b)) for b in range(N) if b != rank)
+            W[ct] = (ct, got[0])
 
-        M, p0 = (64, lo64) if first else (4, 0)
-        die = sc[p0:p0 + M, 0:256]
+        ct, got, call = "ct%d%d" % (t, q), [0], {}
+
+        def slot(b, d, s):
+            return 96 * (2 * t + q) + 32 * call[s] + 4 * ((d - b) % N) + s - call[s]
+
+        die = sc[lo64:hi64, 0:256] if first else sc[0:8, 0:X]
         k0 = 8 * q
+
+        def halves(out, ks, start, stop, key, bank):
+            for k in ks:
+                for h in range(2):
+                    c = 256 * k + X * h
+                    mm(out, T.selw[lo64:hi64, 4 * h:4 * h + 8], T.dead[lo64:hi64, c:c + X], start and (k, h) == (ks[0], 0),
+                       stop and (k, h) == (ks[-1], 1), ["selw", "dead0", dk] + cnk * (not stop), key, bank)
 
         def before():
             lin("s", T.key[:, k0:k0 + 3], T.cn[:, cn0:cn0 + 3], 1.0, col(TIH), cnk + ["tih"], ["k0%d" % q])
-            wn = T.wn[lo64:hi64, lo64:hi64] if first else T.wn[lo64:hi64, lo64:hi64:16]
-            mm(die, wn, T.dead[lo64:hi64, 256 * t:256 * t + 256], True, False, ["wn", dk] + cnk, ["die%d" % q], [scb])
-            if not first:
-                mm(die, T.dc[:, 384:388], T.one[0:1, :], False, False, ["dc3", "one"], ["die%d" % q], [scb])
+            if first:
+                mm(die, T.wn[lo64:hi64, lo64:hi64], T.dead[lo64:hi64, 0:256], True, False, ["wn", dk] + cnk, ["die%d" % q], [scb])
+            else:
+                halves(die, [1], True, False, ["die%d" % q], [scb])
+                mm(die, T.dc[:, 384:392], T.one[0:1, 0:X], False, False, ["dc3", "one"], ["die%d" % q], [scb])
 
         def keys():
             for s in range(3):
-                c0, c1 = [slot[(s, b)] for b in range(3) if b != s]
+                c0, c1 = [slot(b, rank, offsets(t, b).index(o)) for b, o in judges(t, rank, offs[s])]
                 ts(T.key[:, k0 + 4 + s:k0 + 5 + s], T.key[:, k0 + s:k0 + s + 1], T.lc[:, c0:c0 + 1], T.lc[:, c1:c1 + 1], ALU.add, ALU.add,
-                   ["ct%d%d" % (t, q), "k0%d" % q], ["k1%d%d" % (q, s)])
+                   [ct, "k0%d" % q], ["k1%d%d" % (q, s)])
             mm(T.ch[:, 64:67], T.id2[:], T.key[:, k0 + 4:k0 + 7], True, True, ["id2"] + ["k1%d%d" % (q, s) for s in range(3)], ["kt"], ["ch"])
 
         def spread():
             for s in range(3):
-                ts(T.kd[:, 16 * s:16 * s + 16], T.m16[:], T.key[:, k0 + 4 + s:k0 + 5 + s], None, ALU.mult, None,
-                   ["m16", "k1%d%d" % (q, s)], ["kd%d" % s])
+                lin("v", T.kd[:, 16 * s:16 * s + 16], T.yy[:, 112:128], T.key[:, k0 + 4 + s:k0 + 5 + s], 0.0, ["yy0", "k1%d%d" % (q, s)], ["kd%d" % s])
             mm(T.ch[:, 0:48], T.blk[:], T.kd[:], True, True, ["blk0", "blk1", "kd0", "kd1", "kd2"], ["kp"], ["ch"])
 
         def winners():
             for s in range(3):
                 op("v", lambda: V.tensor_reduce(T.mn[:, s:s + 1], T.ch[:, 16 * s:16 * s + 16], AX.X, ALU.min), ["kp"], ["mn%d" % s], ["ch"])
             for s in range(3):
-                ts(T.seld[:, 128 * s:128 * s + 2 * M], T.offb[:] if first else T.offb[:, 0::16], T.ch[:, 64 + s:65 + s], T.mn[:, s:s + 1],
+                c, b = 128 * s, X * (3 * q + s)
+                ts(T.seld[:, c:c + (128 if first else 8)], T.offb[:] if first else T.offb[:, 0::16], T.ch[:, 64 + s:65 + s], T.mn[:, s:s + 1],
                    ALU.add, ALU.is_le, ["offb", "kt", "mn%d" % s], ["seld%d" % s], ["ch"])
-                for h in range(2):
-                    b = X * (3 * q + s)
-                    mm(sc[p0:p0 + M, X * h:X * h + X], T.seld[:, 128 * s + M * h:128 * s + M * h + M], T.hit[:, b:b + X],
-                       False, (s, h) == (2, 1), ["seld%d" % s, "hit%d%d" % (q, s)], ["die%d" % q], [scb])
+                r = ["seld%d" % s, "hit%d%d" % (q, s)]
+                if first:
+                    for h in range(2):
+                        mm(sc[lo64:hi64, X * h:X * h + X], T.seld[:, c + 64 * h:c + 64 * h + 64], T.hit[:, b:b + X],
+                           False, (s, h) == (2, 1), r, ["die%d" % q], [scb])
+                else:
+                    mm(die, T.seld[:, c:c + 8], T.hit[:, b:b + X], False, s == 2, r, ["die%d" % q], [scb])
 
         def report():
             lin("s", T.ycs[:, 4 * q + t:4 * q + t + 1], T.ch[0:64, 64:65], -0.5, col(YB, 0, 64), ["kt", "yb"], ["yc%d%d" % (q, t)], ["ch"])
@@ -655,22 +680,21 @@ def rank_program(g, core, T, topo):
             if first:
                 ts(T.dead[lo64:hi64, 256:512], die, 2.5 - 768, 192.0, ALU.is_lt, ALU.add, ["die%d" % q], ["dead1%d" % q], [scb])
             else:
-                tt(T.yas[:, 256 * q:256 * q + 256], die, T.base[:, 256 * q:256 * q + 256], ALU.max, ["die%d" % q, "base%d" % q],
-                   ["yas%d" % q], [scb])
-                dmas("y", "oya%d" % q, [(T.ya[4 * q:4 * q + 4, :], T.yas[:, 256 * q:256 * q + 256])], r=["yas%d" % q])
+                tt(T.yas[:, X * q:X * q + X], die, T.base[:, X * q:X * q + X], ALU.max, ["die%d" % q, "base%d" % q], ["yas%d" % q], [scb])
+                for h in range(2):
+                    dmas("ys"[h], "oya%d%d" % (q, h), [(T.ya[4 * q:4 * q + 4, X * h:X * h + X], T.yas[4 * h:4 * h + 4, X * q:X * q + X])],
+                         r=["yas%d" % q])
 
         def base():
-            for k in range(2):
-                mm(T.ch[0:4, 256:512], T.wn[lo64:hi64, lo64:hi64:16], T.dead[lo64:hi64, 256 * k:256 * k + 256], k == 0, k == 1,
-                   ["wn", "dead0", dk], ["bp"], ["ch"])
-            act(T.base[:, 256 * q:256 * q + 256], T.ch[0:4, 256:512], AF.Identity, ["bp"], ["base%d" % q], ["ch"], bias=386.0, scale=0.25)
+            halves(T.ch[0:8, 256:384], [0, 1], True, True, ["bp"], ["ch"])
+            act(T.base[:, X * q:X * q + X], T.ch[0:8, 256:384], AF.Identity, ["bp"], ["base%d" % q], ["ch"], bias=386.0, scale=0.25)
 
         return {"place": place, "conv": conv, "vg": vgather, "score": score, "tsum": tsum, "trelu": trelu, "tmove": tmove,
                 "sg": sgather, "weigh": weigh, "relu": relu, "move": move, "hits": hits, "counts": counts, "before": before,
                 "keys": keys, "spread": spread, "winners": winners, "report": report, "deaths": deaths, "base": base}
 
-    steps = {"K": {"rows": rows, "pick": pick, "columns": columns, "windows": windows, "flags": flags, "masks": masks, "rv": variants,
-                   "pfx": pfx, "pfd": pfd, "tables": tables, "thresholds": thresholds, "movers": movers},
+    steps = {"K": {"rows": rows, "pick": pick, "columns": columns, "fills": fills, "windows": windows, "flags": flags, "masks": masks,
+                   "rv": variants, "pfx": pfx, "pfd": pfd, "tables": tables, "thresholds": thresholds, "movers": movers},
              "A": stream(0, 0), "B": stream(0, 1), "C": stream(1, 0), "D": stream(1, 1)}
     steps["A"].update(lattices(0, None))
     steps["C"].update(lattices(1, 0))
@@ -685,5 +709,28 @@ def rank_program(g, core, T, topo):
 
 
 ORDER = """
-Kcolumns.4 Kpick.z Kpick.t Kpick.a Krows.8 Krows.16 Kpick.c Kcolumns.1 Ktables.rep Kpick.A Kcolumns.2 Kcolumns.0 Ascan Krows.64 Kpick.b Acount.2 Kpick.B Ktables.gr Acount.1 Acount.0 Kwindows.0 Kwindows.1 Acount.3 Ktables.idm Alists.1 Kmasks.0 Alists.0 Kflags.0 Aseeds Kmasks.2 Kpick.p Krv.v.6.7 Ktables.thq Aterms Kmasks.1 Kmasks.3 Kcolumns.3 Krv.v.0.3 Ktables.zz Krv.s.5.6 Krv.s.7.8 Ktables.yy Kcolumns.5 Kflags.1 Ktables.gd Arepeat.0.w0 Krv.v.4.5 Krv.s.3.4 Ktables.id2 Ktables.gd11 Kpfx.s.0.4 Aexpand.0.w0 Aplace.0.s.w1 Kthresholds.0 Kmovers.0 Krows.32 Aconv.0.s Kpfx.v.4.10 Aplace.0.v.w0 Bplace.0.s.w1 Kthresholds.1 Ktables.gd10 Aconv.0.v Bplace.0.v.w0 Kpfx.v.10.16 Kthresholds.2 Ktables.gd01 Ktables.gd00 Avg.0.0.32 Bconv.0.s Bconv.0.v Kmovers.3 Kpfd.v.4.8 Ktables.o193 Arepeat.1.w1 Arepeat.2.w0 Aexpand.1.w1 Aexpand.2.w0 Aplace.1.s.w1 Avg.0.32.64 Aconv.1.s Aplace.2.s.w0 Aconv.2.s Bvg.0.32.64 Aplace.1.v.w1 Kcolumns.6 Aconv.1.v Aplace.2.v.w0 Kmovers.2 Asg.0.0.64 Kthresholds.3 Kpfd.s.0.4 Kthresholds.4 Bsg.0.0.64 Kmovers.1 Kthresholds.5 Asg.1.0.32 Ktables.thm0 Asg.1.32.48 Aconv.2.v Aweigh.0.0.64 Avg.1.0.32 Ktables.thm1 Bplace.2.s.w0 Bplace.1.s.w1 Aweigh.1.0.32 Avg.1.32.64 Kthresholds.6 Bconv.1.s Bconv.2.s Avg.2.0.32 Bvg.0.0.32 Aweigh.1.32.48 Asg.1.48.64 Arelu.0 Aweigh.1.48.64 Bplace.2.v.w0 Atsum Amove.0 Bplace.1.v.w1 Avg.2.32.64 Bsg.1.32.48 Bsg.1.48.64 Kthresholds.7 Atrelu Arelu.1 Atmove Ascore.2 Amove.1 Amove.2 Bconv.1.v Bsg.1.16.32 Bconv.2.v Ahits.2 Ahits.0 Ahits.1 Bweigh.0.0.64 Bvg.1.0.32 Bvg.1.32.64 Bvg.2.0.32 Bsg.1.0.16 Btsum Abefore Btrelu Brelu.0 Acounts Bweigh.1.0.32 Bweigh.1.32.64 Bvg.2.32.64 Bmove.0 Kmovers.4 Bscore.2 Brelu.1 Akeys Aspread Btmove Bmove.1 Bhits.0 Awinners Adeaths Cscan Bhits.1 Bmove.2 Ccount.2 Ccount.3 Clists.0 Bhits.2 Bcounts Ccount.0 Ccount.1 Clists.1 Cseeds Cterms Bbefore Crepeat.0.w1 Cexpand.0.w1 Areport Cbase Cplace.0.s.w0 Cplace.0.v.w1 Bkeys Bspread Cconv.0.s Cconv.0.v Crepeat.2.w1 Bwinners Cexpand.2.w1 Csg.0.0.32 Breport Crepeat.1.w0 Bdeaths Cexpand.1.w0 Csg.0.32.64 Cplace.2.s.w1 Dscan Dcount.2 Cplace.1.s.w0 Dcount.0 Cconv.2.s Dcount.1 Dcount.3 Cconv.1.s Dlists.0 Dlists.1 Csg.1.32.48 Csg.1.16.32 Dseeds Dterms Cplace.1.v.w0 Cconv.1.v Csg.1.0.16 Csg.1.48.64 Cvg.1.0.32 Cplace.2.v.w1 Drepeat.0.w0 Dexpand.0.w0 Cconv.2.v Cvg.1.32.64 Cweigh.0.0.64 Dplace.0.v.w0 Crelu.0 Dconv.0.v Cvg.0.0.32 Dplace.0.s.w1 Dconv.0.s Dvg.0.0.32 Cweigh.1.0.32 Cweigh.1.32.64 Drepeat.2.w0 Dexpand.2.w0 Drepeat.1.w1 Dexpand.1.w1 Crelu.1 Cmove.1 Cvg.0.32.64 Cmove.0 Dplace.2.s.w0 Dplace.1.s.w1 Dsg.0.0.32 Dconv.2.s Dconv.1.s Dplace.2.v.w0 Dplace.1.v.w1 Ctsum Dsg.0.32.64 Cvg.2.0.32 Cvg.2.32.64 Dconv.1.v Dvg.0.32.64 Dconv.2.v Dvg.1.32.64 Dsg.1.32.48 Dsg.1.0.32 Cmove.2 Cscore.2 Ctrelu Dweigh.0.0.64 Dweigh.1.0.32 Dsg.1.48.64 Dweigh.1.32.48 Dweigh.1.48.64 Dvg.1.0.32 Chits.2 Drelu.0 Ctmove Drelu.1 Chits.1 Chits.0 Dtsum Dmove.0 Dtrelu Dmove.1 Dmove.2 Dtmove Dhits.1 Dhits.0 Dbase Ccounts Dvg.2.0.32 Dvg.2.32.64 Dscore.2 Dhits.2 Dcounts Dbefore Cbefore Ckeys Creport Cspread Cwinners Dkeys Dspread Dwinners Cdeaths Ddeaths Dreport
+Kpick.t Ktables.rep Kfills.0 Kfills.1 Ktables.end Kpick.z Krows.16 Kcolumns.2 Kcolumns.0 Kfills.5 Kfills.2 Kpick.b Kfills.3 Kpick.c Krows.8 Kfills.4
+Ascan Kflags.0 Kpick.p Kpick.B Kcolumns.1 Acount.2 Acount.0 Kwindows.1 Acount.1 Kpick.a Kpick.A Acount.3 Ktables.jr Ktables.gr Krows.64 Alists
+Kwindows.0 Krv.v.0.3 Krv.s.3.4 Aseeds.1 Aseeds.0 Kmasks.0 Krv.v.4.5 Ktables.idm Aterms Arepeat.0.w0 Kmovers.0 Kmasks.2 Krv.s.7.8 Krv.s.5.6 Kmasks.3
+Ktables.thq Ktables.gd0 Ktables.thm0 Ktables.gd1 Ktables.thm1 Ktables.id2
+Kflags.1 Krv.v.6.7 Kmasks.1 Kcolumns.3 Aexpand.0.w0 Aplace.0.v.w0 Kpfx.s.0.4 Kpfd.s.0.4 Aplace.0.s.w1 Kpfx.v.10.16 Kpfx.v.4.10 Aconv.0.v
+Kthresholds.0 Aconv.0.s Bplace.0.v.w0 Bplace.0.s.w1 Kmovers.4 Avg.0.32.64 Kthresholds.1 Asg.0.0.32 Bconv.0.s Kthresholds.2 Asg.0.32.64
+Arepeat.1.w1 Bsg.0.0.32 Kthresholds.3 Kmovers.2 Bsg.0.32.64 Bconv.0.v Arepeat.2.w0 Kthresholds.4 Kmovers.1 Kpfd.v.4.8
+Aexpand.1.w1 Aexpand.2.w0 Aplace.1.s.w1 Avg.0.0.32 Aplace.2.s.w0 Kthresholds.5 Aconv.1.s Aconv.2.s Bvg.0.32.64 Aplace.1.v.w1 Asg.1.40.64 Aconv.1.v
+Kthresholds.6 Aplace.2.v.w0 Aconv.2.v Aweigh.0.0.64 Avg.1.0.32 Avg.1.32.64 Bplace.1.s.w1 Asg.1.24.40 Asg.1.0.24 Bplace.2.s.w0 Avg.2.32.64
+Kmovers.5 Arelu.0 Bconv.1.s Aweigh.1.40.64 Aweigh.1.24.40 Bconv.2.s Atsum Avg.2.0.32 Aweigh.1.0.24 Kthresholds.7 Amove.0 Atrelu Arelu.1 Atmove
+Bplace.1.v.w1 Ahits.0 Amove.1 Amove.2 Bsg.1.24.48 Ascore.2 Bconv.1.v Acounts.0.1 Ahits.1 Bvg.0.0.32 Bplace.2.v.w0 Bvg.1.28.56 Bvg.1.0.28
+Ahits.2 Kcolumns.4 Bweigh.0.0.64 Bconv.2.v Acounts.1.2 Bsg.1.48.72 Abefore Btsum Acounts.2.3 Bweigh.1.48.72 Brelu.0 Btrelu
+Bweigh.1.24.48 Btmove Bmove.0 Bvg.2.28.56 Bvg.2.0.28 Kmovers.3 Bscore.2 Akeys Bsg.1.0.24 Aspread Bweigh.1.0.24 Awinners Bhits.0 Brelu.1
+Bmove.1 Bhits.1 Adeaths Bmove.2 Cscan Ccount.0 Ccount.2 Ccount.3 Ccount.1 Clists Cseeds.0 Bcounts.0.1 Bhits.2 Bbefore Bcounts.1.2 Bcounts.2.3
+Cseeds.1 Cterms Crepeat.0.w1 Areport Cexpand.0.w1 Cbase Cplace.0.v.w1 Bkeys Cplace.0.s.w0 Cconv.0.v Bspread Cvg.0.0.32 Cconv.0.s Crepeat.1.w0
+Bwinners Cexpand.1.w0 Csg.0.32.64 Crepeat.2.w1 Bdeaths Cexpand.2.w1 Dscan Csg.0.0.32 Cplace.1.s.w0 Dcount.0 Dcount.2 Cconv.1.s Cplace.2.s.w1
+Cplace.1.v.w0 Dcount.3 Cconv.2.s Cplace.2.v.w1 Dcount.1 Dlists Dseeds.0 Cconv.1.v Breport Dseeds.1 Dterms Cvg.1.0.28 Csg.1.48.72 Drepeat.0.w0
+Dexpand.0.w0 Cconv.2.v Cvg.1.28.56 Cvg.0.32.64 Cweigh.0.0.64 Csg.1.24.48 Cweigh.1.48.72 Dplace.0.v.w0 Dconv.0.v Dplace.0.s.w1 Cweigh.1.24.48 Crelu.0
+Csg.1.0.24 Cvg.2.28.56 Dconv.0.s Ctsum Ctrelu Cmove.0 Drepeat.1.w1 Cweigh.1.0.24 Dvg.0.32.64 Dexpand.1.w1 Drepeat.2.w0 Ctmove Dplace.1.s.w1
+Dexpand.2.w0 Dvg.0.0.32 Dsg.0.32.64 Dplace.2.s.w0 Crelu.1 Chits.0 Cmove.1 Dconv.1.s Dconv.2.s Dplace.1.v.w1 Cvg.2.0.28 Dsg.0.0.32 Ccounts.0.1
+Dsg.1.0.24 Dplace.2.v.w0 Dsg.1.40.64 Dconv.1.v Dvg.1.32.64 Dconv.2.v Dsg.1.24.40 Dweigh.0.0.64 Cmove.2 Cscore.2 Dvg.1.0.32 Dweigh.1.40.64 Dtsum
+Drelu.0 Chits.1 Ccounts.1.2 Dtrelu Dweigh.1.24.40 Dvg.2.0.32 Dweigh.1.0.24 Dvg.2.32.64 Dmove.0 Drelu.1 Dtmove Dscore.2 Chits.2 Ccounts.2.3 Dmove.1
+Dhits.0 Dhits.1 Dbase Dmove.2 Cbefore Ckeys Dhits.2 Dbefore Dcounts.0.1 Dcounts.1.2 Cspread Dcounts.2.3 Cwinners Creport Dkeys Dspread Cdeaths
+Dwinners Dreport Ddeaths
 """

from concourse.bass import DstId, RemoteDMATransfer
from concourse.mybir import AluOpType as ALU, AxisListType as AX, ActivationFunctionType as AF

N = 8
S = 256
X = 128
SHARE = ((64, 64), (64, 72), (64, 72), (64, 64))
HM = max(max(s) for s in SHARE)
H = X - min(min(s) for s in SHARE)

SCRATCH = {
    "lv8": ("sbuf", [8, 256], "int32"),
    "d8": ("sbuf", [8, 256], "bfloat16"),
    "cum8": ("sbuf", [8, 256], "bfloat16"),
    "ps": ("sbuf", [33, 272], "bfloat16"),
    "pfs": ("sbuf", [128, 256 + HM], "bfloat16"),
    "pfx": ("sbuf", [128, 2 * H * 16], "bfloat16"),
    "pfd": ("sbuf", [128, 2 * HM * 8], "bfloat16"),
    "th16": ("sbuf", [16, 16], "int32"),
    "thu": ("sbuf", [16, 32], "float32"),
    "thh": ("sbuf", [16, 16], "bfloat16"),
    "thq": ("sbuf", [32, 128], "bfloat16"),
    "thx": ("sbuf", [16, 256], "bfloat16"),
    "thm": ("sbuf", [16, 256], "bfloat16"),
    "gd": ("sbuf", [32, 256], "bfloat16"),
    "rf0": ("sbuf", [128, 4112], "bfloat16"),
    "rf1": ("sbuf", [128, 4112], "bfloat16"),
    "one": ("sbuf", [128, 256], "bfloat16"),
    "o193": ("sbuf", [128, 256], "bfloat16"),
    "dc": ("sbuf", [1, 4 * 128], "bfloat16"),
    "pp": ("sbuf", [128, 3], "float32"),
    "jr": ("sbuf", [128, 16], "bfloat16"),
    "gr": ("sbuf", [128, 128], "bfloat16"),
    "t16": ("sbuf", [33, 32], "float32"),
    "rep": ("sbuf", [8, 128], "bfloat16"),
    "pa": ("sbuf", [33, 128], "bfloat16"),
    "pb": ("sbuf", [33, 128], "bfloat16"),
    "pc": ("sbuf", [33, 256], "bfloat16"),
    "fl": ("sbuf", [128, 4], "bfloat16"),
    "cols": ("sbuf", [128, 16], "float32"),
    "b8": ("sbuf", [128, 16], "float32"),
    "idm": ("sbuf", [128, 128], "bfloat16"),
    "wn": ("sbuf", [128, 128], "bfloat16"),
    "mask": ("sbuf", [128, 384], "bfloat16"),
    "sel": ("sbuf", [128, 192], "bfloat16"),
    "blk": ("sbuf", [128, 128], "float32"),
    "id2": ("sbuf", [128, 128], "float32"),
    "offb": ("sbuf", [128, 128], "bfloat16"),
    "zz": ("sbuf", [128, 144], "bfloat16"),
    "yy": ("sbuf", [128, 496], "bfloat16"),
    "wa": ("sbuf", [128, 272], "bfloat16"),
    "wb": ("sbuf", [128, 272], "bfloat16"),
    "posr": ("sbuf", [128, X], "bfloat16"),
    "rv": ("sbuf", [128, 8 * X], "bfloat16"),
    "dead": ("sbuf", [128, 512], "bfloat16"),
    "cum": ("sbuf", [128, 256], "bfloat16"),
    "junk": ("sbuf", [128, 770], "bfloat16"),
    "si": ("sbuf", [128, 4], "float32"),
    "ofi": ("sbuf", [128, 4], "uint16"),
    "ga": ("sbuf", [128, 96], "bfloat16"),
    "pw": ("sbuf", [128, 9 * 48], "float16"),
    "px": ("sbuf", [128, 3 * 384], "float16"),
    "ofv": ("sbuf", [128, 2 * 3 * X], "uint16"),
    "ofs": ("sbuf", [128, 2 * 2 * HM], "uint16"),
    "gv": ("sbuf", [128, 2 * 3 * H * 16], "bfloat16"),
    "gs0": ("sbuf", [128, 2 * HM * 16], "bfloat16"),
    "gs1": ("sbuf", [128, 2 * HM * 32], "bfloat16"),
    "dq": ("sbuf", [128, 4 * HM * 8], "bfloat16"),
    "dt": ("sbuf", [128, 2 * 128], "bfloat16"),
    "hit": ("sbuf", [128, 2 * 3 * X], "bfloat16"),
    "cn": ("sbuf", [128, 16], "float32"),
    "lc": ("sbuf", [128, 4 * 96], "float32"),
    "key": ("sbuf", [128, 16], "float32"),
    "kd": ("sbuf", [128, 48], "float32"),
    "mn": ("sbuf", [128, 4], "float32"),
    "seld": ("sbuf", [128, 384], "bfloat16"),
    "selw": ("sbuf", [128, 12], "bfloat16"),
    "base": ("sbuf", [8, 256], "float32"),
    "yas": ("sbuf", [8, 256], "float32"),
    "ycs": ("sbuf", [64, 8], "float32"),
    "w0": ("psum", [128, 512], "float32"),
    "w1": ("psum", [128, 512], "float32"),
    "qq": ("psum", [128, 1024], "float32"),
    "tb": ("psum", [128, 512], "float32"),
    "sc0": ("psum", [128, 512], "float32"),
    "sc1": ("psum", [128, 512], "float32"),
    "ch": ("psum", [128, 512], "float32"),
}
SEMAPHORES = ["cv", "cs", "cp", "cg", "llv", "lps", "lpf", "lth", "lrf0", "lrf1", "oya00", "oya01", "oya10", "oya11", "oyc0", "oyc1", "sent",
              "pw1", "pw2", "pw4", "pw5", "pw7", "pw8", "ct00", "ct01", "ct10", "ct11"]


def deal_engines(topo, src, dsts):
    off = [i for i, d in enumerate(dsts) if topo.chip(d) != topo.chip(src)]
    on = [i for i in range(len(dsts)) if i not in off]
    far = [e for e in topo.engines(src, dsts[off[0]]) if all(e in topo.engines(src, dsts[i]) for i in off)]
    near = [e for e in topo.engines(src, dsts[on[0]]) if e not in far] if on else []
    share = 1
    while share * 2 * len(off) <= len(far):
        share *= 2
    out = [None] * len(dsts)
    for k, i in enumerate(off):
        out[i] = far[k * share:(k + 1) * share]
    for k, i in enumerate(on):
        out[i] = near[k * share:(k + 1) * share]
    return out


def rank_program(g, core, T, topo):
    rank = T.rank_of(core)
    if rank is None:
        return
    cores = T.cores
    E = {"v": g.vector, "s": g.scalar, "p": g.tensor, "g": g, "y": g.sync}
    SEM = {"v": "cv", "s": "cs", "p": "cp", "g": "cg"}
    cnt = {"cv": 0, "cs": 0, "cp": 0, "cg": 0}
    final = {}
    waited = {q: {} for q in E}
    W, R, XB = {}, {}, {}
    pend = {q: ([], [], []) for q in E}

    def need(q, deps):
        best = {}
        for s_, v_ in deps:
            best[s_] = max(best.get(s_, 0), v_)
        for s_, v_ in best.items():
            if waited[q].get(s_, 0) < v_:
                E[q].wait_ge(T.sem[s_], v_)
                waited[q][s_] = v_

    def deps_of(q, r, w, x):
        own = SEM.get(q)
        deps = []
        for k in r:
            deps.append(W[k])
        for k in w:
            if k in W:
                deps.append(W[k])
            deps.extend(R.get(k, {}).items())
        if q == "p":
            deps = [d for d in deps if d[0] != own]
        for k in x:
            deps.extend([d for d in XB.get(k, {}).items() if d[0] != own])
        return deps

    def note(tok, r, w, x):
        for k in r:
            R.setdefault(k, {})[tok[0]] = tok[1]
        for k in w:
            W[k] = tok
            R[k] = {}
        for k in x:
            XB.setdefault(k, {})[tok[0]] = tok[1]

    def op(q, fn, r=(), w=(), x=(), inc=True):
        need(q, deps_of(q, r, w, x))
        ins = fn()
        p_ = pend[q]
        p_[0].extend(r); p_[1].extend(w); p_[2].extend(x)
        if inc:
            s_ = SEM[q]
            cnt[s_] += 1
            ins.then_inc(T.sem[s_], 1)
            note((s_, cnt[s_]), p_[0], p_[1], p_[2])
            pend[q] = ([], [], [])

    def dmas(q, sem, pairs, r=(), w=()):
        need(q, deps_of(q, r, w, ()))
        for out, in_ in pairs:
            E[q].dma_start(out, in_).then_inc(T.sem[sem], 16)
        note((sem, 16 * len(pairs)), r, w, ())
        final[sem] = 16 * len(pairs)

    V, A, P = g.vector, g.scalar, g.tensor

    def ts(out, in0, s1, s2, o0, o1, r, w, x=()):
        if o1 is None:
            op("v", lambda: V.tensor_scalar(out, in0, s1, None, o0), r, w, x)
        else:
            op("v", lambda: V.tensor_scalar(out, in0, s1, s2, o0, o1), r, w, x)

    def tt(out, in0, in1, o, r, w, x=()):
        op("v", lambda: V.tensor_tensor(out, in0, in1, o), r, w, x)

    def ms(ap, c, w):
        op("v", lambda: V.memset(ap, c), (), w)

    def cp(out, in_, r, w):
        op("v", lambda: V.tensor_copy(out, in_), r, w)

    def mm(out, lhsT, rhs, start, stop, r, w, x, inc=None):
        op("p", lambda: P.matmul(out, lhsT, rhs, start, stop), r, w, x, stop if inc is None else inc)

    def act(out, in_, func, r, w, x=(), inc=True, **kw):
        op("s", lambda: A.activation(out, in_, func, **kw), r, w, x, inc)

    def lin(q, out, in_, scale, bias, r, w, x=()):
        if q == "v":
            ts(out, in_, scale, bias, ALU.mult, ALU.add, r, w, x)
        else:
            act(out, in_, AF.Identity, r, w, x, scale=scale, bias=bias)

    def col(i, lo=0, hi=128):
        return T.cols[lo:hi, i:i + 1]
    R16, R8, R32, TIH, B0, B1, TH2, YB, CA, CB, C1, C2, CI, CM = range(14)

    sent = [0]

    def send(pieces, r):
        eng = deal_engines(topo, core, [cores[p_[0]] for p_ in pieces])
        trs = []
        for (d, src, dst, sem), mine in zip(pieces, eng):
            rid, pid, _ = topo.addr(cores[d])
            trs.append(RemoteDMATransfer(dst_ids=[DstId(rid=rid, pnc=pid)], dma_engine_mask=sum(1 << e for e in mine),
                                         remote_sem=T.sem[sem], src=src, dst=dst))
            sent[0] += len(mine)
        need("g", deps_of("g", r, (), ()))
        g.remote_dma_fused(trs, local_sem=T.sem.sent)

    def lands(b, dsts):
        return sum(len(e) for d, e in zip(dsts, deal_engines(topo, cores[b], [cores[d] for d in dsts])) if d == rank)

    def judges(t, b, o):
        return [((b - o + a) % N, a) for a in (0, 2 * t + 1, 2 * t + 2) if a != o]

    def offsets(t, b):
        near = lambda o: any(topo.chip(cores[d]) == topo.chip(cores[b]) for d, _ in judges(t, b, o))
        return [0] + sorted((2 * t + 1, 2 * t + 2), key=near)

    RF = [T.rf0, T.rf1]
    dmas("y", "llv", [(T.lv8[:], T.lv[:])], w=["lv8"])
    ms(T.ps[0:32, :], 0.0, ["ps"])
    dmas("s", "lps", [(T.ps[0:24, 0:S], T.pos[:])], w=["ps"])
    dmas("y", "lpf", [(T.pfs[64 * h:64 * h + 64, c:c + n], T.pf[64 * q:64 * q + 64, X * h:X * h + n])
                      for q, c, n in ((0, 0, X), (1, X, X), (0, 2 * X, HM)) for h in range(2)], w=["pfs"])
    dmas("y", "lth", [(T.th16[8 * k:8 * k + 8, :], T.th[:]) for k in range(2)], w=["th16"])
    for q in range(2):
        dmas("y", "lrf%d" % q, [(RF[q][64 * h:64 * h + 64, 0:4096], T.rf[64 * q:64 * q + 64, :]) for h in range(2)], w=["rf%d" % q])

    flag = {"allow_small_or_imprecise_dtypes": True}

    def select(out, in_, pattern, cmp_, fill, base, r, w):
        op("g", lambda: g.affine_select(out, in_, pattern, cmp_, fill, base, 1), r, w)

    def iota(out, pattern, base, cm, w):
        op("g", lambda: g.iota(out, pattern, base, cm, **flag), w=w)

    def floor_p(i, d):
        ts(T.fl[:, i:i + 1], T.pp[:, 0:1], 1.0 / d, 191.5 + 0.5 / d, ALU.mult, ALU.add, ["pp"], ["fl%d" % d])

    ms(T.one[:], 1.0, ["one"])
    iota(T.pp[:], [[1536, 3]], 0, 1, ["pp"])
    EQ, NE = ALU.is_equal, ALU.not_equal
    pck = ["pc%d" % i for i in range(6)]
    pfxk = ["pfx%d" % m for m in range(16)]
    pfdk = ["pfd%d" % m for m in range(8)]
    VAR = [(C1, ALU.add, 1.0), (C1, ALU.subtract, -1.0), (C2, ALU.add, -2.0 ** -4), (None, None, 2.0 ** -4),
           (C2, ALU.add, -2.0 ** -8), (None, None, 2.0 ** -8), (C2, ALU.add, -2.0 ** -12), (None, None, 2.0 ** -12)]
    STEPS = [(0, 0), (1, 0), (2, 0), (0, 1), (1, 1), (2, 1), (0, 2), (None, 0), (0, 3), (1, 4), (None, 1), (1, 5), (2, 6),
             (None, 2), (2, 7)]

    def rows(d):
        i = (16, 8, 64).index(d)
        floor_p(i, d)
        if d == 64:
            ts(col(CI), T.fl[:, 2:3], -4.0, T.fl[:, 0:1], ALU.mult, ALU.add, ["fl64", "fl16"], ["ci"])
            ts(col(CM), col(R16), 7.5, 4.0, ALU.is_gt, ALU.mult, ["r16"], ["cm"])
            ts(col(CM), col(CM), col(CI), None, ALU.add, None, ["cm", "ci"], ["cm"])
        else:
            ts(col(R16 + i), T.fl[:, i:i + 1], -float(d), T.pp[:, 2 - i:3 - i], ALU.mult, ALU.add, ["fl%d" % d, "pp"], ["r%d" % d])

    def pick(k):
        if k == "t":
            iota(T.t16[:, 0:16], [[0, 2], [-3, 8]], 0, 1, ["t16c"])
            iota(T.t16[:, 16:32], [[-3, 8], [0, 2]], 0, 1, ["t16a"])
        elif k in "ab":
            select(T["p" + k][:], T.one[0:33, 0:128], [[-3, 8], [0, 4], [-1, 4]], EQ, 0.0, 0, ["one"], ["p" + k])
            select(T["p" + k][:, 3::4], T.one[0:33, 0:32], [[0, 32]], EQ, 0.0, -32, ["one", "p" + k], ["p" + k + "3"])
        elif k in "AB":
            n = "p" + k.lower()
            for j in range(3):
                ts(T[n][:, (4 if k == "A" else 0) + j::8], T.t16[:, 16:32], float((j + 1) % 3), None, EQ, None, ["t16a", n], [n + str(j)])
            i = "AB".index(k)
            bank = "q%d" % i
            mm(T.qq[:, 512 * i:512 * i + 272], T[n][:], T.ps[:], True, True, [n + str(j) for j in range(4)] + ["ps", "ps1"], [bank], [bank])
        elif k == "z":
            ms(T.pc[:], 0.0, ["pc0"])
            ms(T.pc[32:33, 7::16], 0.5, ["pc0"])
        elif k == "c":
            for i in range(6):
                s_, j = divmod(i, 3)
                ts(T.pc[:, 4 * s_ + j::16], T.t16[:, 0:16], float((j + 2) % 3), 1.0 - 2 * s_, EQ, ALU.mult, ["t16c", "pc0"], [pck[i]])
            mm(T.tb[:, 0:X], T.pc[:, 0:128], T.ps[:, 0:X], True, False, ["ps", "ps1"] + pck, ["tb"], ["tb"])
            mm(T.tb[:, 0:X], T.pc[:, 120:248], T.ps[:, X:S], False, True, ["ps"] + pck, ["tb"], ["tb"])
        else:
            act(T.posr[:], T.tb[:, 0:X], AF.Copy, ["tb"], ["posr"], ["tb"])

    def columns(k):
        if k == 0:
            lin("s", col(B0), col(R16), -1.0, -0.5, ["r16"], ["b0"])
            lin("s", col(B1), col(R16), -1.0, -16.5, ["r16"], ["b1"])
            lin("s", col(TH2), col(R16), 1.0, 32.5, ["r16"], ["th2"])
        elif k == 1:
            ts(col(C1), col(R8), 3.0, 1024.0, EQ, ALU.mult, ["r8"], ["c1"])
            ts(col(C2), col(R8), 3.0, -30720.0, EQ, ALU.mult, ["r8"], ["c2"])
        elif k == 2:
            ms(T.ps[32:33, :], 1.0, ["ps1"])
        elif k == 3:
            for i, v in enumerate((-45.0 * 2 ** 30, -45.0 * 2 ** 26, -1.5 * 2 ** 27)):
                ms(T.dc[:, 128 * i:128 * i + 128], v, ["dc%d" % i])
        else:
            lin("s", col(YB), col(R16), 1.0 / 32, 384.0, ["r16"], ["yb"])
            lin("s", col(TIH), col(R16), 1.0 / 32, 0.0, ["r16"], ["tih"])
            lin("s", T.wn[:], T.idm[:], -4.0, 0.0, ["idm"], ["wn"])
            lin("s", T.dc[:, 384:392], T.one[0:1, 0:8], 768.0, 0.0, ["one"], ["dc3"])
            lin("s", T.selw[:], T.sel[:, 0::16], -2.0 ** -26, 0.0, ["sel0", "sel1"], ["selw"])

    def fills(k):
        out, value, key = ((T.yy[:, 0:248], 0.0, "yya"), (T.yy[:, 248:496], 0.0, "yyb"), (T.zz[:], 0.0, "zz0"),
                           (T.rf0[:, 4096:4112], -2.0 ** 20, "rfz0"), (T.rf1[:, 4096:4112], -2.0 ** 20, "rfz1"), (T.o193[:], 193.0, "o193"))[k]
        lin("s", out, T.one[:, 0:out.shape[1]], value, 0.0, ["one"], [key])

    def windows(k):
        w_, key, bank = (T.wa, "wa", "q0") if k == 0 else (T.wb, "wb", "q1")
        act(w_[:], T.qq[:, 512 * k:512 * k + 272], AF.Copy, [bank], [key], [bank])

    def flags(k):
        if k == 0:
            ts(T.d8[:], T.lv8[:], -1.0, 193.0, ALU.mult, ALU.add, ["lv8"], ["d8"])
            mm(T.ch[:, 0:256], T.rep[:], T.d8[:], True, True, ["rep", "d8"], ["ch"], ["ch"])
        else:
            act(T.dead[:, 0:256], T.ch[:, 0:256], AF.Copy, ["ch"], ["dead0"], ["ch"])

    def masks(k):
        if k < 3:
            ts(T.mask[:, k::3], T.gr[:], 768.0, col(CM), ALU.subtract, EQ, ["gr", "cm"], ["mask%d" % k])
        else:
            lin("s", T.sel[:, 64:128], T.one[:, 0:64], 0.0, 0.0, ["one"], ["selz"])
            for h in range(2):
                lin("s", T.sel[:, 128 * h:128 * h + 64], T.mask[:, 192 * h:192 * h + 192:3], 2.0 ** 25, 0.0, ["mask0", "selz"], ["sel%d" % h])

    def variants(q, lo, hi):
        for k in range(lo, hi):
            c_, o_, sc_ = VAR[k]
            out = T.rv[:, X * k:X * k + X]
            if c_ is None:
                lin(q, out, T.posr[:], sc_, 0.0, ["posr"], ["rv%d" % k])
            else:
                ts(out, T.posr[:], col(c_), sc_, o_, ALU.mult, ["posr", "c1", "c2"], ["rv%d" % k])

    def pfx(q, lo, hi):
        for m in range(lo, hi):
            lin(q, T.pfx[:, m::16], T.pfs[:, X - H:X + H], 1.0, 1.0 / 512, ["pfs"], [pfxk[m]])

    def pfd(q, lo, hi):
        for k in range(lo, hi):
            lin(q, T.pfd[:, k::8], T.pfs[:, S - HM:S + HM], T.b8[:, k:k + 1], T.b8[:, 8 + k:9 + k], ["pfs", "b8", "b8e"], [pfdk[k]])

    def tables(k):
        if k == "rep":
            select(T.rep[:], T.one[0:8, 0:128], [[-1, 8], [0, 16]], EQ, 0.0, 0, ["one"], ["rep"])
        elif k == "gr":
            iota(T.gr[:], [[1, 8], [0, 16]], 192, 0, ["gr"])
        elif k == "idm":
            select(T.idm[:], T.one[:, 0:128], [[-1, 128]], EQ, 0.0, 0, ["one"], ["idm"])
        elif k == "thq":
            select(T.thq[:], T.one[0:32, 0:128], [[-1, 8], [0, 16]], NE, 0.0, -16, ["one"], ["thq"])
            select(T.thq[:], T.thq[:], [[-1, 4], [0, 32]], NE, 0.0, -24, ["thq"], ["thq"])
        elif k[0:2] == "gd":
            q = int(k[2])
            a = T.gd[:, 128 * q:128 * q + 128]
            select(a, T.one[0:32, 0:128], [[0, 32], [-1, 4]], EQ, 0.0, -4 * q, ["one"], [k])
            select(a, a, [[0, 32], [-1, 4]], NE, 1.0, -8 - 4 * q, [k], [k])
            for s in range(2):
                a = T.gd[:, 128 * q + 64 * s:128 * q + 64 * s + 64]
                select(a, a, [[0, 2], [-1, 4], [0, 8]] if s else [[-1, 8], [0, 8]], NE, -32768.0, -16 - 8 * s, [k], [k + str(s)])
        elif k[0:3] == "thm":
            q = int(k[3])
            a = T.thm[:, 128 * q:128 * q + 128]
            select(a, T.one[0:16, 0:128], [[0, 2], [-1, 4], [0, 16]], EQ, 0.0, -4 * q, ["one"], [k])
            select(a, a, [[0, 2], [-1, 4], [0, 16]], NE, 1.0, -8 - 4 * q, [k], [k])
        elif k == "jr":
            iota(T.jr[:], [[1, 16]], 0, 0, ["jr"])
        elif k == "end":
            iota(T.junk[:, 768:770], [[0, 2]], 256, 0, ["end"])
        else:
            select(T.id2[:], T.idm[:], [[-1, 128]], NE, 1.0, -64, ["idm"], ["id2"])
            select(T.id2[:], T.id2[:], [[-1, 128]], NE, 1.0, 64, ["id2"], ["id2"])

    def thresholds(k):
        if k == 0:
            ts(col(CA, 0, 16), T.pp[0:16, 0:1], 8.0, -1.0, ALU.is_ge, ALU.mult, ["pp"], ["ca"])
            ts(T.thh[:], T.th16[:], -0.5, -1.0, ALU.add, ALU.mult, ["th16"], ["thh"])
            ts(col(CB, 0, 16), col(CA, 0, 16), 2.0, 1.0, ALU.mult, ALU.add, ["ca"], ["cb"])
            ts(T.thu[:, 0:16], T.th16[:], -0.5, col(CA, 0, 16), ALU.add, ALU.mult, ["th16", "ca"], ["thu0"])
        elif k == 1:
            lin("s", T.thu[:, 16:32], T.thh[:], col(CB, 0, 16), 0.0, ["thh", "cb"], ["thu1"])
        elif k == 2:
            tt(T.thq[0:16, 0:16], T.thu[:, 0:16], T.thu[:, 16:32], ALU.add, ["thu0", "thu1", "thq"], ["thq"])
        elif k < 6:
            n_ = 16 << (k - 3)
            lin("s", T.thq[0:16, n_:2 * n_], T.thq[0:16, 0:n_], 1.0, 0.0, ["thq"], ["thq"])
        else:
            c = 128 * (k - 6)
            tt(T.thx[:, c:c + 128], T.thq[0:16, :], T.thm[:, c:c + 128], ALU.mult, ["thq", "thm%d" % (k - 6)], ["thx%d" % (k - 6)])

    def movers(k):
        if k == 0:
            ts(T.b8[:, 0:8], T.gr[:, 0::16], T.fl[:, 0:1], None, EQ, None, ["gr", "fl16"], ["b8"])
            ts(T.b8[:, 8:16], T.gr[:, 0::16], T.fl[:, 0:1], 1.0 / 512, EQ, ALU.mult, ["gr", "fl16"], ["b8e"])
        elif k == 1:
            lin("s", T.zz[:, 15:143:16], T.b8[:, 0:8], 1.0, 0.0, ["b8", "zz0"], ["zz"])
        elif k == 2:
            ts(T.yy[:, 112:128], T.jr[:], col(R16), None, EQ, None, ["jr", "r16", "yya"], ["yy0"])
        elif k == 4:
            floor_p(3, 32)
            ts(col(R32), T.fl[:, 3:4], -2.0, T.fl[:, 0:1], ALU.mult, ALU.add, ["fl32", "fl16"], ["r32"])
        elif k == 5:
            for s in (1, 2):
                ts(T.yy[:, 112 + 128 * s:128 + 128 * s], T.yy[:, 112:128], col(R32), s - 193.0, ALU.mult, EQ,
                   ["yy0", "r32", "yya", "yyb"], ["yy%d" % s])
        else:
            ts(T.offb[:], T.gr[:], T.fl[:, 0:1], 4096.0, NE, ALU.mult, ["gr", "fl16"], ["offb"])
            for h in range(2):
                ts(T.blk[:, 64 * h:64 * h + 64], T.gr[:, 0:64], 768.0, col(CI), ALU.subtract, EQ, ["gr", "ci"], ["blk%d" % h])

    def lattices(t, q):
        lo, hi = (0, 128) if q is None else (64 * q, 64 * q + 64)
        i = 0 if t == 0 else 3 + 3 * q
        far = (2 * t + 1, 2 * t + 2)
        cum = [T.w0[:, 0:256], T.w1[:, 0:256]] if t == 0 else [T.cum[lo:hi, :]] * 2
        ck, cx = (["w0", "w1"], [["w0"], ["w1"]]) if t == 0 else (["cum", "cum"], [[], []])

        def scan():
            if t == 0:
                op("v", lambda: V.tensor_tensor_scan(T.cum8[:], T.one[0:8, :], T.lv8[:], 0.0, ALU.mult, ALU.add), ["one", "lv8"], ["cum8"])
                for k in range(2):
                    mm(cum[k], T.rep[:], T.cum8[:], True, True, ["rep", "cum8"], [ck[k]], cx[k])
            else:
                op("v", lambda: V.tensor_tensor_scan(cum[0], T.o193[lo:hi, :], T.dead[lo:hi, 256:512], 0.0, ALU.add, ALU.subtract),
                   ["o193", "dead1%d" % q], ["cum"])

        def count(k):
            if k < 2:
                act(T.junk[lo:hi, 256 * k:256 * k + 256], cum[0], AF.Sign, [ck[0], "b%d" % k], ["si%d" % k, "j%d" % k], cx[0],
                    bias=col(B0 + k, lo, hi), accum_out=T.si[lo:hi, k:k + 1])
            elif k == 2:
                ts(T.junk[lo:hi, 512:768], cum[1], col(TH2, lo, hi), -2.0, ALU.is_le, ALU.mult, [ck[1], "th2"], ["le"], cx[1])
            else:
                op("v", lambda: V.tensor_reduce(T.si[lo:hi, 2:3], T.junk[lo:hi, 512:769], AX.X, ALU.add), ["le", "end"], ["si2"])

        def lists():
            ts(T.ofi[lo:hi, 0:3], T.si[lo:hi, 0:3], -0.5, 128.0, ALU.mult, ALU.add, ["si0", "si1", "si2"], ["ofi"])

        def seeds(k):
            n = ("wa", "wb")[k]
            a = (T.ga[:, 48 * k:48 * k + 48], T[n][:, 0:272].indirect(T.ofi[:, 0:3]))
            if k == 0:
                cp(*a, [n, "ofi"], ["g" + n])
            else:
                act(*a, AF.Copy, [n, "ofi"], ["g" + n])

        def terms():
            keys = ["pw%d" % i + "abc"[j] for j in range(3)]
            for j in range(3):
                tt(T.pw[:, 48 * i + j:48 * i + 48:3], T.ga[:, (j + 1) % 3:48:3], T.ga[:, 48 + (j + 2) % 3:96:3], ALU.mult,
                   ["gwa", "gwb"], [keys[j]] + (["pw%d" % i] if j == 2 else []))
            there = [((rank + o) % N, i + offsets(t, (rank + o) % N).index(o)) for o in far]
            send([(d, T.pw[:, 48 * i:48 * i + 48], T.pw[:, 48 * k:48 * k + 48], "pw%d" % k) for d, k in there], keys)
            for s in (1, 2):
                b = (rank - offsets(t, rank)[s]) % N
                W["pw%d" % (i + s)] = ("pw%d" % (i + s), lands(b, [(b + o) % N for o in far]))

        def repeat(s, bank):
            c = 48 * (i + s)
            for k in range(8):
                mm(T[bank][lo:hi, 48 * k:48 * k + 48], T.idm[lo:hi, lo:hi], T.pw[lo:hi, c:c + 48], True, True,
                   ["idm", "pw%d" % (i + s)], [bank], [bank], inc=(k == 7))

        def expand(s, bank):
            tt(T.px[lo:hi, 384 * s:384 * s + 384], T[bank][lo:hi, 0:384], T.mask[lo:hi, :], ALU.mult, [bank, "mask0", "mask1", "mask2"],
               ["px%d%d" % (s, k) for k in range(2) if q in (None, k)], [bank])

        return {"scan": scan, "count": count, "lists": lists, "seeds": seeds, "terms": terms, "repeat": repeat, "expand": expand}

    def stream(t, q):
        offs = offsets(t, rank)
        first = t == 0
        lo64, hi64 = 64 * q, 64 * q + 64
        dk = "dead0" if first else "dead1%d" % q
        HS = SHARE[2 * t + q] + SHARE[2 * t + q][1:]
        HV = [X - n for n in HS]
        s0 = [0 if q == 0 else X - n for n in HS]
        v0 = [n if q == 0 else 0 for n in HS]
        gv0 = [16 * (3 * H * q + sum(HV[:s])) for s in range(3)]
        sc, scb = (T.sc0, T.sc1)[q], "sc%d" % q
        win = RF[q][:, 0:4112]
        rfk = ["rf%d" % q, "rfz%d" % q]
        spans, units = {}, {}

        def made(name, lo, hi):
            spans.setdefault(name, []).append((lo, hi))
            return ["%s%d_%d" % (name, q, lo)]

        def from_(name, lo, hi):
            return ["%s%d_%d" % (name, q, a) for a, b in spans[name] if a < hi and lo < b]

        def place(s, who, bank):
            units[(s, who)] = bank
            lo, n = (s0[s], HS[s]) if who == "s" else (v0[s], HV[s])
            out = T[bank][:, 0:n]
            for h in range(2):
                c = 256 * t + X * h + lo
                mm(out, T.sel[lo64:hi64, 64 * h:64 * h + 128], T.dead[lo64:hi64, c:c + n], h == 0, False, ["sel0", "sel1", dk], [bank], [bank])
            for i, (j, k) in enumerate(STEPS):
                if j is None:
                    mm(out, T.dc[:, 128 * k:128 * k + 128], T.one[0:1, 0:n], False, False, ["dc%d" % k, "one"], [bank], [bank])
                else:
                    mm(out, T.px[lo64:hi64, 384 * s + j:384 * s + 384:3], T.rv[lo64:hi64, X * k + lo:X * k + lo + n],
                       False, i == len(STEPS) - 1, ["px%d%d" % (s, q), "rv%d" % k], [bank], [bank])

        def conv(s, who):
            bank = units[(s, who)]
            lo, n = (s0[s], HS[s]) if who == "s" else (v0[s], HV[s])
            if who == "s" and s > 0:
                out = T.ofs[:, 2 * HM * q + s - 1:2 * HM * q + 2 * n:2]
            else:
                b = 3 * X * q + X * s + lo
                out = T.ofv[:, b:b + n]
            ts(out, T[bank][:, 0:n], 0.2, 4096.0, ALU.add, ALU.min, [bank], ["of%s%d%d" % (who, q, s)], [bank])

        def vgather(s, lo, hi):
            c = 3 * X * q + X * s + v0[s]
            f = 16 * (X * q + v0[s] - X + H)
            tt(T.gv[:, gv0[s] + 16 * lo:gv0[s] + 16 * hi], win.indirect(T.ofv[:, c + lo:c + hi]), T.pfx[:, f + 16 * lo:f + 16 * hi],
               ALU.mult, rfk + ["ofv%d%d" % (q, s)] + pfxk, made("gv%d" % s, lo, hi))

        def score(s):
            out = sc[:, X * s + v0[s]:X * s + v0[s] + HV[s]]
            key = made("sc%d" % s, v0[s], v0[s] + HV[s])
            mm(out, T.thx[:, 128 * q:128 * q + 128], T.one[0:16, 0:HV[s]], True, False, ["thx%d" % q, "one"], key, [scb])
            for m in range(16):
                mm(out, T.zz[:, 15 - m:143 - m], T.gv[:, gv0[s] + m:gv0[s] + 16 * HV[s]:16], False, m == 15,
                   ["zz"] + from_("gv%d" % s, 0, X), key, [scb])

        nt = HV[0] + HV[1]

        def tsum():
            mm(T.tb[0:nt, 0:128], T.one[0:16, 0:nt], T.thx[:, 128 * q:128 * q + 128], True, False, ["thx%d" % q, "one"], ["tb"], ["tb"])
            for m in range(16):
                mm(T.tb[0:nt, m:128:16], T.gv[:, gv0[0] + m:gv0[2]:16], T.zz[:, 15:143:16], False, m == 15,
                   ["zz"] + from_("gv0", 0, X) + from_("gv1", 0, X), ["tb"], ["tb"])

        def trelu():
            act(T.dt[0:nt, 128 * q:128 * q + 128], T.tb[0:nt, 0:128], AF.Relu, ["tb"], ["dt%d" % q], ["tb"])

        def tmove():
            for s in range(2):
                mm(sc[:, X * s + v0[s]:X * s + v0[s] + HV[s]], T.dt[0:nt, 128 * q:128 * q + 128], T.idm[0:nt, HV[0] * s:HV[0] * s + HV[s]],
                   True, True, ["dt%d" % q, "idm"], made("sc%d" % s, v0[s], v0[s] + HV[s]), [scb], inc=(s == 1))

        def sgather(s, lo, hi):
            if s == 0:
                b, c = 16 * HM * q, 3 * X * q + s0[0]
                act(T.gs0[:, b + 16 * lo:b + 16 * hi], win.indirect(T.ofv[:, c + lo:c + hi]), AF.Copy,
                    rfk + ["ofs%d0" % q], made("gs0", lo, hi))
            else:
                b, c = 32 * HM * q, 2 * HM * q
                act(T.gs1[:, b + 32 * lo:b + 32 * hi], win.indirect(T.ofs[:, c + 2 * lo:c + 2 * hi]), AF.Copy,
                    rfk + ["ofs%d1" % q, "ofs%d2" % q], made("gs1", lo, hi))

        q0 = [0, 1024 - 8 * HS[1]]

        def qbanks(s, lo, hi):
            return ["q%d" % k for k in range((q0[s] + 8 * lo) // 512, (q0[s] + 8 * hi - 1) // 512 + 1)]

        def weigh(s, lo, hi):
            banks = qbanks(s, lo, hi)
            r = from_("gs%d" % s, lo, hi) + pfdk
            d = 8 * (HM if q == 0 else HM - HS[s])
            gd = T.gd[:, 128 * q + 64 * s:128 * q + 64 * s + 64]
            for x in range(lo, hi, 8):
                c = q0[s] + 8 * x
                mm(T.qq[:, c:c + 64], T.thq[:], gd, True, False, ["thq", "gd%d%d" % (q, s)], banks, banks)
                if s == 0:
                    b = 16 * (HM * q + x)
                    mm(T.qq[:, c:c + 64], T.gs0[:, b:b + 128], T.pfd[:, d + 8 * x:d + 8 * x + 64], False, True,
                       r, banks, banks, inc=(x + 8 == hi))
                else:
                    for y in (0, 4):
                        b = 32 * (HM * q + x + y)
                        mm(T.qq[:, c + 8 * y:c + 8 * y + 32], T.gs1[:, b:b + 128], T.pfd[:, d + 8 * (x + y):d + 8 * (x + y) + 32],
                           False, y > 0, r, banks, banks, inc=(x + y + 4 == hi))

        dq0 = [16 * HM * q, 16 * HM * q + 8 * HM]

        def relu(s):
            banks = qbanks(s, 0, HS[s])
            act(T.dq[:, dq0[s]:dq0[s] + 8 * HS[s]], T.qq[:, q0[s]:q0[s] + 8 * HS[s]], AF.Relu, banks, ["dq%d%d" % (q, s)], banks)

        def move(s):
            b = dq0[min(s, 1)]
            key = made("sc%d" % s, s0[s], s0[s] + HS[s])
            for k in range(8):
                c = 128 * s + 112 - 16 * k
                mm(sc[:, X * s + s0[s]:X * s + s0[s] + HS[s]], T.yy[:, c:c + 128], T.dq[:, b + k:b + 8 * HS[s]:8], k == 0, k == 7,
                   ["dq%d%d" % (q, min(s, 1)), "yy%d" % s], key, [scb])

        cn0 = 8 * t + 4 * q
        cnk = ["cn%d%d%d" % (t, q, s) for s in range(3)]

        def hits(s):
            b = X * (3 * q + s)
            act(T.hit[:, b:b + X], sc[:, X * s:X * s + X], AF.Sign, from_("sc%d" % s, 0, X),
                ["hit%d%d" % (q, s), cnk[s]], [scb], bias=1.0 / 64, scale=-1.0, accum_out=T.cn[:, cn0 + s:cn0 + s + 1])

        def counts(lo, hi):
            to = lambda b: sorted(set(d for s in range(lo, hi) for d, _ in judges(t, b, offsets(t, b)[s])))
            call.update({s: lo for s in range(lo, hi)})
            send([(d, T.cn[:, cn0 + lo:cn0 + hi], T.lc[:, slot(rank, d, lo):slot(rank, d, lo) + hi - lo], ct) for d in to(rank)], cnk[lo:hi])
            got[0] += sum(lands(b, to(b)) for b in range(N) if b != rank)
            W[ct] = (ct, got[0])

        ct, got, call = "ct%d%d" % (t, q), [0], {}

        def slot(b, d, s):
            return 96 * (2 * t + q) + 32 * call[s] + 4 * ((d - b) % N) + s - call[s]

        die = sc[lo64:hi64, 0:256] if first else sc[0:8, 0:X]
        k0 = 8 * q

        def halves(out, ks, start, stop, key, bank):
            for k in ks:
                for h in range(2):
                    c = 256 * k + X * h
                    mm(out, T.selw[lo64:hi64, 4 * h:4 * h + 8], T.dead[lo64:hi64, c:c + X], start and (k, h) == (ks[0], 0),
                       stop and (k, h) == (ks[-1], 1), ["selw", "dead0", dk] + cnk * (not stop), key, bank)

        def before():
            lin("s", T.key[:, k0:k0 + 3], T.cn[:, cn0:cn0 + 3], 1.0, col(TIH), cnk + ["tih"], ["k0%d" % q])
            if first:
                mm(die, T.wn[lo64:hi64, lo64:hi64], T.dead[lo64:hi64, 0:256], True, False, ["wn", dk] + cnk, ["die%d" % q], [scb])
            else:
                halves(die, [1], True, False, ["die%d" % q], [scb])
                mm(die, T.dc[:, 384:392], T.one[0:1, 0:X], False, False, ["dc3", "one"], ["die%d" % q], [scb])

        def keys():
            for s in range(3):
                c0, c1 = [slot(b, rank, offsets(t, b).index(o)) for b, o in judges(t, rank, offs[s])]
                ts(T.key[:, k0 + 4 + s:k0 + 5 + s], T.key[:, k0 + s:k0 + s + 1], T.lc[:, c0:c0 + 1], T.lc[:, c1:c1 + 1], ALU.add, ALU.add,
                   [ct, "k0%d" % q], ["k1%d%d" % (q, s)])
            mm(T.ch[:, 64:67], T.id2[:], T.key[:, k0 + 4:k0 + 7], True, True, ["id2"] + ["k1%d%d" % (q, s) for s in range(3)], ["kt"], ["ch"])

        def spread():
            for s in range(3):
                lin("v", T.kd[:, 16 * s:16 * s + 16], T.yy[:, 112:128], T.key[:, k0 + 4 + s:k0 + 5 + s], 0.0, ["yy0", "k1%d%d" % (q, s)], ["kd%d" % s])
            mm(T.ch[:, 0:48], T.blk[:], T.kd[:], True, True, ["blk0", "blk1", "kd0", "kd1", "kd2"], ["kp"], ["ch"])

        def winners():
            for s in range(3):
                op("v", lambda: V.tensor_reduce(T.mn[:, s:s + 1], T.ch[:, 16 * s:16 * s + 16], AX.X, ALU.min), ["kp"], ["mn%d" % s], ["ch"])
            for s in range(3):
                c, b = 128 * s, X * (3 * q + s)
                ts(T.seld[:, c:c + (128 if first else 8)], T.offb[:] if first else T.offb[:, 0::16], T.ch[:, 64 + s:65 + s], T.mn[:, s:s + 1],
                   ALU.add, ALU.is_le, ["offb", "kt", "mn%d" % s], ["seld%d" % s], ["ch"])
                r = ["seld%d" % s, "hit%d%d" % (q, s)]
                if first:
                    for h in range(2):
                        mm(sc[lo64:hi64, X * h:X * h + X], T.seld[:, c + 64 * h:c + 64 * h + 64], T.hit[:, b:b + X],
                           False, (s, h) == (2, 1), r, ["die%d" % q], [scb])
                else:
                    mm(die, T.seld[:, c:c + 8], T.hit[:, b:b + X], False, s == 2, r, ["die%d" % q], [scb])

        def report():
            lin("s", T.ycs[:, 4 * q + t:4 * q + t + 1], T.ch[0:64, 64:65], -0.5, col(YB, 0, 64), ["kt", "yb"], ["yc%d%d" % (q, t)], ["ch"])
            if not first:
                dmas("s", "oyc%d" % q, [(T.yc[lo64:hi64, :], T.ycs[:, 4 * q:4 * q + 2])], r=["yc%d0" % q, "yc%d1" % q])

        def deaths():
            if first:
                ts(T.dead[lo64:hi64, 256:512], die, 2.5 - 768, 192.0, ALU.is_lt, ALU.add, ["die%d" % q], ["dead1%d" % q], [scb])
            else:
                tt(T.yas[:, X * q:X * q + X], die, T.base[:, X * q:X * q + X], ALU.max, ["die%d" % q, "base%d" % q], ["yas%d" % q], [scb])
                for h in range(2):
                    dmas("ys"[h], "oya%d%d" % (q, h), [(T.ya[4 * q:4 * q + 4, X * h:X * h + X], T.yas[4 * h:4 * h + 4, X * q:X * q + X])],
                         r=["yas%d" % q])

        def base():
            halves(T.ch[0:8, 256:384], [0, 1], True, True, ["bp"], ["ch"])
            act(T.base[:, X * q:X * q + X], T.ch[0:8, 256:384], AF.Identity, ["bp"], ["base%d" % q], ["ch"], bias=386.0, scale=0.25)

        return {"place": place, "conv": conv, "vg": vgather, "score": score, "tsum": tsum, "trelu": trelu, "tmove": tmove,
                "sg": sgather, "weigh": weigh, "relu": relu, "move": move, "hits": hits, "counts": counts, "before": before,
                "keys": keys, "spread": spread, "winners": winners, "report": report, "deaths": deaths, "base": base}

    steps = {"K": {"rows": rows, "pick": pick, "columns": columns, "fills": fills, "windows": windows, "flags": flags, "masks": masks,
                   "rv": variants, "pfx": pfx, "pfd": pfd, "tables": tables, "thresholds": thresholds, "movers": movers},
             "A": stream(0, 0), "B": stream(0, 1), "C": stream(1, 0), "D": stream(1, 1)}
    steps["A"].update(lattices(0, None))
    steps["C"].update(lattices(1, 0))
    steps["D"].update(lattices(1, 1))
    for word in ORDER.split():
        name, *args = word[1:].split(".")
        steps[word[0]][name](*[int(a) if a.isdigit() else a for a in args])

    final.update(cnt)
    final["sent"] = sent[0]
    need("g", list(final.items()))


ORDER = """
Kpick.t Ktables.rep Kfills.0 Kfills.1 Ktables.end Kpick.z Krows.16 Kcolumns.2 Kcolumns.0 Kfills.5 Kfills.2 Kpick.b Kfills.3 Kpick.c Krows.8 Kfills.4
Ascan Kflags.0 Kpick.p Kpick.B Kcolumns.1 Acount.2 Acount.0 Kwindows.1 Acount.1 Kpick.a Kpick.A Acount.3 Ktables.jr Ktables.gr Krows.64 Alists
Kwindows.0 Krv.v.0.3 Krv.s.3.4 Aseeds.1 Aseeds.0 Kmasks.0 Krv.v.4.5 Ktables.idm Aterms Arepeat.0.w0 Kmovers.0 Kmasks.2 Krv.s.7.8 Krv.s.5.6 Kmasks.3
Ktables.thq Ktables.gd0 Ktables.thm0 Ktables.gd1 Ktables.thm1 Ktables.id2
Kflags.1 Krv.v.6.7 Kmasks.1 Kcolumns.3 Aexpand.0.w0 Aplace.0.v.w0 Kpfx.s.0.4 Kpfd.s.0.4 Aplace.0.s.w1 Kpfx.v.10.16 Kpfx.v.4.10 Aconv.0.v
Kthresholds.0 Aconv.0.s Bplace.0.v.w0 Bplace.0.s.w1 Kmovers.4 Avg.0.32.64 Kthresholds.1 Asg.0.0.32 Bconv.0.s Kthresholds.2 Asg.0.32.64
Arepeat.1.w1 Bsg.0.0.32 Kthresholds.3 Kmovers.2 Bsg.0.32.64 Bconv.0.v Arepeat.2.w0 Kthresholds.4 Kmovers.1 Kpfd.v.4.8
Aexpand.1.w1 Aexpand.2.w0 Aplace.1.s.w1 Avg.0.0.32 Aplace.2.s.w0 Kthresholds.5 Aconv.1.s Aconv.2.s Bvg.0.32.64 Aplace.1.v.w1 Asg.1.40.64 Aconv.1.v
Kthresholds.6 Aplace.2.v.w0 Aconv.2.v Aweigh.0.0.64 Avg.1.0.32 Avg.1.32.64 Bplace.1.s.w1 Asg.1.24.40 Asg.1.0.24 Bplace.2.s.w0 Avg.2.32.64
Kmovers.5 Arelu.0 Bconv.1.s Aweigh.1.40.64 Aweigh.1.24.40 Bconv.2.s Atsum Avg.2.0.32 Aweigh.1.0.24 Kthresholds.7 Amove.0 Atrelu Arelu.1 Atmove
Bplace.1.v.w1 Ahits.0 Amove.1 Amove.2 Bsg.1.24.48 Ascore.2 Bconv.1.v Acounts.0.1 Ahits.1 Bvg.0.0.32 Bplace.2.v.w0 Bvg.1.28.56 Bvg.1.0.28
Ahits.2 Kcolumns.4 Bweigh.0.0.64 Bconv.2.v Acounts.1.2 Bsg.1.48.72 Abefore Btsum Acounts.2.3 Bweigh.1.48.72 Brelu.0 Btrelu
Bweigh.1.24.48 Btmove Bmove.0 Bvg.2.28.56 Bvg.2.0.28 Kmovers.3 Bscore.2 Akeys Bsg.1.0.24 Aspread Bweigh.1.0.24 Awinners Bhits.0 Brelu.1
Bmove.1 Bhits.1 Adeaths Bmove.2 Cscan Ccount.0 Ccount.2 Ccount.3 Ccount.1 Clists Cseeds.0 Bcounts.0.1 Bhits.2 Bbefore Bcounts.1.2 Bcounts.2.3
Cseeds.1 Cterms Crepeat.0.w1 Areport Cexpand.0.w1 Cbase Cplace.0.v.w1 Bkeys Cplace.0.s.w0 Cconv.0.v Bspread Cvg.0.0.32 Cconv.0.s Crepeat.1.w0
Bwinners Cexpand.1.w0 Csg.0.32.64 Crepeat.2.w1 Bdeaths Cexpand.2.w1 Dscan Csg.0.0.32 Cplace.1.s.w0 Dcount.0 Dcount.2 Cconv.1.s Cplace.2.s.w1
Cplace.1.v.w0 Dcount.3 Cconv.2.s Cplace.2.v.w1 Dcount.1 Dlists Dseeds.0 Cconv.1.v Breport Dseeds.1 Dterms Cvg.1.0.28 Csg.1.48.72 Drepeat.0.w0
Dexpand.0.w0 Cconv.2.v Cvg.1.28.56 Cvg.0.32.64 Cweigh.0.0.64 Csg.1.24.48 Cweigh.1.48.72 Dplace.0.v.w0 Dconv.0.v Dplace.0.s.w1 Cweigh.1.24.48 Crelu.0
Csg.1.0.24 Cvg.2.28.56 Dconv.0.s Ctsum Ctrelu Cmove.0 Drepeat.1.w1 Cweigh.1.0.24 Dvg.0.32.64 Dexpand.1.w1 Drepeat.2.w0 Ctmove Dplace.1.s.w1
Dexpand.2.w0 Dvg.0.0.32 Dsg.0.32.64 Dplace.2.s.w0 Crelu.1 Chits.0 Cmove.1 Dconv.1.s Dconv.2.s Dplace.1.v.w1 Cvg.2.0.28 Dsg.0.0.32 Ccounts.0.1
Dsg.1.0.24 Dplace.2.v.w0 Dsg.1.40.64 Dconv.1.v Dvg.1.32.64 Dconv.2.v Dsg.1.24.40 Dweigh.0.0.64 Cmove.2 Cscore.2 Dvg.1.0.32 Dweigh.1.40.64 Dtsum
Drelu.0 Chits.1 Ccounts.1.2 Dtrelu Dweigh.1.24.40 Dvg.2.0.32 Dweigh.1.0.24 Dvg.2.32.64 Dmove.0 Drelu.1 Dtmove Dscore.2 Chits.2 Ccounts.2.3 Dmove.1
Dhits.0 Dhits.1 Dbase Dmove.2 Cbefore Ckeys Dhits.2 Dbefore Dcounts.0.1 Dcounts.1.2 Cspread Dcounts.2.3 Cwinners Creport Dkeys Dspread Cdeaths
Dwinners Dreport Ddeaths
"""
